import numpy as np, ml_dtypes
CORES = [2,3,42,43,82,83,122,123]
N = 8
BF = ml_dtypes.bfloat16
V, NF, NS, J, AM, RO = 512, 4096, 2048, 9, 255, 3
NV = N * V
def parts(rng):
    x = rng.integers(0, 256, (N, 8, 16, V)); y = rng.integers(0, 256, (N, 8, 16, NF)); f = rng.integers(0, NF, (N, 8, 16, NS))
    c = rng.integers(0, NV, (N, 8, 16, V)); e = rng.integers(0, NS, (N, 8, V))
    th = rng.integers(1180, 1440, (N, 8, 1)) + rng.integers(-60, 61, (N, 8, 16))
    return x, y, f, c, e, th
def halves(rng, n, edge, w):
    x = rng.integers(0, w, (N, 8, 16, V)); h = NF // 2; s = rng.integers(0, 2, (N, 8, h)); m = np.zeros((N, 8, NF), np.int64)
    m[..., 0::2] = s; m[..., 1::2] = 1 - s
    y = rng.integers(0, w, (N, 8, 16, NF)) + (256 - w) * m[:, :, None, :]
    r = (np.argsort(rng.random((N, 8, 16, NS)), axis=2) < n[:, :, None, :]).astype(np.int64)
    u = rng.integers(0, h, r.shape); u = np.where(rng.random(r.shape) < edge, (h - 1) * rng.integers(0, 2, r.shape), u)
    f = 2 * u + (np.take_along_axis(s, u.reshape(N, 8, -1), 2).reshape(u.shape) ^ r)
    return x, y, f
def pack(x, y, f, c, e, th):
    return {"x0": np.ascontiguousarray(x.reshape(N, 128, V)).astype(np.float32).astype(BF), "frm": np.ascontiguousarray(y.reshape(N, 128, NF)).astype(np.float32).astype(BF),
            "rol": np.ascontiguousarray(f.reshape(N, 128, NS)).astype(np.int32), "cas": np.ascontiguousarray(c.reshape(N, 128, V)).astype(np.int32),
            "sc0": np.ascontiguousarray(e).astype(np.int32), "th": np.ascontiguousarray(th.reshape(N, 128, 1)).astype(np.int32)}
def setup_inputs(rng):
    return pack(*parts(rng))
def setup_inputs_spread(rng):
    x, y, f, c, e, th = parts(rng); w = rng.choice(np.array([1.0, 2.0, 4.0]), (N, 8, 1, 1))
    x = (rng.random(x.shape) * np.exp2(rng.integers(0, 9, (N, 8, 1, V)))).astype(np.int64)
    y = (rng.random(y.shape) * np.exp2(rng.integers(0, 9, (N, 8, 1, NF)))).astype(np.int64)
    f = np.minimum((NF * rng.random(f.shape) ** w).astype(np.int64), NF - 1); c = NV - 1 - np.minimum((NV * rng.random(c.shape) ** w).astype(np.int64), NV - 1)
    e = np.minimum((NS * rng.random(e.shape) ** w[..., 0]).astype(np.int64), NS - 1)
    th = np.minimum((4080 * rng.random((N, 8, 1)) ** 2 * rng.random((N, 8, 16))).astype(np.int64), 4079)
    return pack(x, y, f, c, e, th)
def setup_inputs_ends(rng):
    x, y, f, c, e, th = parts(rng); k = np.arange(16)
    def flat(n):
        return 255 * np.where(rng.random((N, 8, 1, n)) < 0.5, rng.integers(0, 2, (N, 8, 1, n)), rng.integers(0, 2, (N, 8, 16, n)))
    x, y = flat(V), flat(NF)
    y[..., 0] = 255 * rng.integers(0, 2, (N, 8, 1)); y[..., NF - 1] = 255 - y[..., 0]
    x[0, :, :, 0] = 255 * rng.integers(0, 2, (8, 1)); x[N - 1, :, :, V - 1] = 255 * rng.integers(0, 2, (8, 1))
    f = np.where(rng.random(f.shape) < 0.85, (NF - 1) * rng.integers(0, 2, f.shape), f)
    c = np.where(rng.random(c.shape) < 0.85, (NV - 1) * rng.integers(0, 2, c.shape), c)
    e = np.where(rng.random(e.shape) < 0.85, (NS - 1) * rng.integers(0, 2, e.shape), e)
    th = 4079 * (rng.random((N, 8, 16)) < rng.choice(np.array([0.0, 0.25, 0.5, 1.0]), (N, 8, 1))).astype(np.int64)
    th[:, 7] = 4079 * ((k & 3) == 3)
    y[:, 7, :, 0] = 0; y[:, 7, :, NF - 1] = 255; x[0, 7, :, 0] = 0; x[N - 1, 7, :, V - 1] = 255; f[:, 7, :, NS - 1] = (NF - 1) * (k & 1)
    y[:, 6, :, 0] = 255; y[:, 6, :, NF - 1] = 255; x[0, 6, :, 0] = 0; x[N - 1, 6, :, V - 1] = 0; f[:, 6, :, NS - 1] = (NF - 1) * (1 - (k & 1))
    for g in (6, 7):
        c[:, g, :, V - 2:] = ((NV - 1) * ((k >> 1) & 1))[:, None]; e[:, g, V - 2:] = NS - 1
    return pack(x, y, f, c, e, th)
def setup_inputs_corners(rng):
    x, y, f, c, e, th = parts(rng); n = rng.choice(np.array([0, 1, J - 1, J, J + 1, 15, 16]), (N, 8, NS))
    n[..., 0] = J - 1; n[..., NS - 1] = J; n[..., NS - 2] = J - 1; n[::2, ::2, 0] = J; n[::2, 1::2, NS - 1] = J - 1
    x, y, f = halves(rng, n, 0.2, 8)
    e = np.where(rng.random(e.shape) < 0.5, rng.choice(np.array([0, 1, NS - 2, NS - 1]), e.shape), e)
    me = (np.arange(N)[:, None] * V + np.arange(V))[:, None, None, :]; kind = ((np.arange(N)[:, None] + np.arange(8)) & 3)[:, :, None, None]
    own = np.where(rng.random(c.shape) < 0.5, me, c); nxt = (me + 1 + np.arange(16)[:, None]) % NV; few = rng.choice(np.array([0, V - 1, NV - V, NV - 1]), c.shape)
    c = np.where(kind == 0, own, np.where(kind == 1, nxt, np.where(kind == 2, few, c)))
    return pack(x, y, f, c, e, rng.integers(300, 1600, (N, 8, 16)))
def setup_inputs_crowd(rng):
    x, y, f, c, e, th = parts(rng); a, g = np.arange(N)[:, None], np.arange(8)[None, :]
    part = ((a >= 2) & ((a & 1) == 0))[:, :, None]
    sp = rng.integers(0, NS, (N, 8, 1)); n = rng.integers(15, 17, (N, 8, NS))
    n = np.where(((a >= 2) & ((g & 1) == 1))[:, :, None], rng.integers(0, 17, n.shape), n); np.put_along_axis(n, sp, J - 1, 2)
    bit = rng.integers(0, 2, (N, 8, NS // 2)); strong = np.zeros((N, 8, NS), np.int64); strong[..., 0::2] = bit; strong[..., 1::2] = 1 - bit
    n = np.where(part, np.where(strong == 1, rng.integers(15, 17, n.shape), rng.integers(0, J, n.shape)), n)
    x, y, f = halves(rng, n, 0.1, 4)
    e = np.where((g & 1)[:, :, None] == 0, (sp + 1) & (NS - 1), (sp + 1 + rng.integers(0, NS - 1, (N, 8, V))) & (NS - 1))
    hit = rng.integers(0, 2, (N, 8, V))
    for q in range(2, N, 2):
        m = (AM + 1) * (1 + 2 * int(rng.integers(0, 2 * V // (AM + 1))))
        o = np.argsort((rng.random((8, V // 2)) + rng.random((8, 1))).reshape(-1)); z = np.zeros(4 * V, np.int64); z[o[:m]] = 1
        hit[q, :, 0::2] = z.reshape(8, V // 2)
    u = rng.integers(0, NS // 2, (N, 8, V)); e = np.where(part, 2 * u + (np.take_along_axis(bit, u, 2) ^ hit), e)
    less = rng.random((N, 8)) < 0.5; less[0] = False; less[1] = False; less[2::2] = False; less[1, rng.integers(0, 8)] = True; less[3, 7] = True
    at = 2 * rng.integers(0, V // 2, (N, 8)); at[:, 7] = V - 2
    for q in range(N):
        for j in range(8):
            if less[q, j]: e[q, j, at[q, j]:at[q, j] + 2] = sp[q, j, 0]
    three = np.take_along_axis(rng.integers(0, NV, (N, 8, 3)), rng.integers(0, 3, (N, 8, 16 * V)), 2).reshape(c.shape)
    kind = (g & 3)[:, :, None, None]; one = rng.integers(0, NV, (1, 8, 1, 1))
    c = np.where(kind == 0, one, np.where(kind == 1, three, c)); c[1::2, 0::4, 15, V - 1] = rng.integers(0, NV, c[1::2, 0::4, 15, V - 1].shape)
    loose = np.argsort(rng.random((N, 8, 16)), axis=2) < min(4, 15 - J)
    th = np.where(loose, rng.integers(4024, 4041, (N, 8, 16)), rng.integers(4080 - AM, 3984, (N, 8, 16)))
    low = (((g & 3) == 1) & (a != 1))[:, :, None]
    return pack(x, y, f, c, e, np.where(low, rng.integers(300, 1600, (N, 8, 16)), th))
def setup_inputs_ties(rng):
    x, y, f, c, e, th = parts(rng); pt = rng.integers(0, 16, (8, 16, 1))
    x = 20 * rng.integers(0, 13, (N, 8, 1, V)) + pt; y = 20 * rng.integers(0, 13, (N, 8, 1, NF)) + pt
    th = 320 * rng.integers(2, 6, (N, 8, 1)) + rng.integers(-1, 2, (N, 8, 16))
    return pack(x, y, f, c, e, th)
def check_inputs(d):
    bad = []
    for k, lo, hi in (("x0", 0, 255), ("frm", 0, 255), ("rol", 0, NF - 1), ("cas", 0, NV - 1), ("sc0", 0, NS - 1), ("th", 0, 4079)):
        v = np.asarray(d[k]).astype(np.float64)
        if not (np.min(v) >= lo and np.max(v) <= hi): bad.append("range of " + k)
        elif np.any(v != np.floor(v)): bad.append("whole numbers in " + k)
    return bad
def reference(x0, frm, rol, cas, sc0, th):
    x = x0.astype(np.float32).astype(np.int64).reshape(N, 8, 16, V); y = frm.astype(np.float32).astype(np.int64).reshape(N, 8, 16, NF)
    f = rol.astype(np.int64).reshape(N, 8, 16, NS); c = cas.astype(np.int64).reshape(N, 8, 16, V); e = sc0.astype(np.int64).reshape(N, 8, V)
    lim = th.astype(np.int64).reshape(N, 8, 16, 1); jumps = np.zeros(N, np.int64)
    for t in range(RO):
        own = np.arange(t & 1, V, 2)
        xa = np.array(x.transpose(1, 2, 0, 3)).reshape(8, 16, NV); ca = np.array(c.transpose(1, 2, 0, 3)).reshape(8, 16, NV)
        for a in range(N):
            ev = e[a][:, own]; ck = c[a][:, :, own]; fk = np.take_along_axis(f[a], ev[:, None, :], 2)
            yk = np.take_along_axis(y[a], fk.reshape(8, 1, -1), 2).reshape(8, 16, 16, -1); xk = np.take_along_axis(xa, ck.reshape(8, 1, -1), 2).reshape(8, 16, 16, -1)
            dist = np.add.reduce(np.abs(yk - xk), axis=1)
            b = np.argmin(dist, axis=1)[:, None, :]
            rej = dist > lim[a] + (jumps[a] & AM)
            jump = np.add.reduce(rej.astype(np.int64), axis=1)[:, None, :] >= J
            fb = np.take_along_axis(fk, b, 1); cb = np.take_along_axis(ck, b, 1)
            yb = np.take_along_axis(y[a], fb, 2); cc = np.take_along_axis(ca, cb, 2); xo = xa[:, :, a * V + own]
            x[a][:, :, own] = np.where(jump, (xo + yb) >> 1, np.abs(xo - yb))
            c[a][:, :, own] = np.where(rej & ~jump, cc, ck)
            e[a][:, own] = np.where(jump, fb & (NS - 1), (ev[:, None, :] + 1) & (NS - 1))[:, 0]
            jumps[a] = np.add.reduce(jump.reshape(-1).astype(np.int64))
    return {"yx": x.reshape(N, 128, V).astype(np.float32).astype(BF), "yc": c.reshape(N, 128, V).astype(np.float32), "ye": e.astype(np.float32)}

@@ -1,0 +1,427 @@
+from concourse.bass import DstId, RemoteDMATransfer
+from concourse.mybir import AluOpType as A, AxisListType, ActivationFunctionType as F
+
+N = 8
+C1 = 12582912.0
+XOFF = (0, 4096, 6144); XW = (512, 256, 256)
+COFF = (0, 2048, 3072); CW = (256, 128, 128)
+XWIN = ((0, 4096), (0, 6144), (4096, 8192))
+CWIN = ((0, 2048), (0, 3072), (2048, 4096))
+XCH = (4, 4, 4, 2, 1, 1)
+
+SCRATCH = {
+    "XT": ("sbuf", [128, 8192], "bfloat16"), "CT": ("sbuf", [128, 4096], "int32"),
+    "frs": ("sbuf", [128, 4096], "bfloat16"), "rls": ("sbuf", [128, 2048], "int32"),
+    "LHa": ("sbuf", [128, 1024], "int32"), "LHb": ("sbuf", [128, 768], "int32"),
+    "scs": ("sbuf", [128, 32], "int32"), "ths": ("sbuf", [128, 8], "int32"),
+    "M": ("sbuf", [128, 256], "float32"), "Mb": ("sbuf", [128, 256], "bfloat16"),
+    "Bb": ("sbuf", [128, 144], "bfloat16"), "Bf": ("sbuf", [128, 144], "float32"),
+    "oneb": ("sbuf", [128, 128], "bfloat16"), "onef": ("sbuf", [128, 128], "float32"),
+    "rst": ("sbuf", [128, 256], "float32"),
+    "ci": ("sbuf", [128, 16], "int32"), "cf": ("sbuf", [128, 16], "float32"),
+    "kf": ("sbuf", [128, 128], "float32"), "ku": ("sbuf", [128, 64], "uint16"),
+    "tin": ("sbuf", [128, 128], "float32"), "tout": ("sbuf", [128, 128], "float32"),
+    "yxs": ("sbuf", [128, 512], "bfloat16"), "ycs": ("sbuf", [128, 512], "float32"), "yes": ("sbuf", [128, 32], "float32"),
+    "wa": ("sbuf", [128, 256], "int32"), "wb": ("sbuf", [128, 256], "int32"), "wc": ("sbuf", [128, 256], "int32"),
+    "pk": ("sbuf", [128, 256], "int32"),
+    "KEY0": ("psum", [128, 512], "float32"), "KEY1": ("psum", [128, 512], "float32"),
+    "DN0": ("psum", [128, 512], "float32"), "DN1": ("psum", [128, 512], "float32"),
+    "CNT": ("psum", [128, 512], "float32"), "FCP": ("psum", [128, 512], "float32"), "AAP": ("psum", [128, 512], "float32"),
+}
+for _t in range(3):
+    for _n, _w, _d in (("yk", 4096, "bfloat16"), ("dd", 4096, "bfloat16"), ("ab", 4096, "bfloat16"),
+                       ("xo", 256, "uint16"), ("fo", 256, "uint16"), ("f4", 256, "float32"), ("fc", 256, "float32"),
+                       ("xm", 256, "float32"), ("xn", 256, "float32"), ("sm", 256, "float32"), ("W", 512, "float32"),
+                       ("sn", 256, "float32"), ("sg", 256, "bfloat16"), ("r1", 272, "bfloat16"), ("oh", 256, "float32"),
+                       ("df", 256, "float32"), ("dm", 256, "float32"),
+                       ("ti", 256, "int32"), ("tf", 256, "float32"), ("tu", 128, "uint16")):
+        SCRATCH["%s%d" % (_n, _t)] = ("sbuf", [128, _w], _d)
+
+SEMAPHORES = ["cv", "cs", "ct", "cg", "loc", "lx", "lsc", "lth", "lca", "lro", "lfr", "ox", "oc", "oe"]
+for _e in range(3):
+    SEMAPHORES += ["xa%d_%d" % (_e, _a) for _a in range(4)] + ["ha%d_%d" % (_e, _a) for _a in range(4)] + ["xp%d" % _e, "ca%d" % _e]
+
+
+def bits(engines):
+    m = 0
+    for e in engines:
+        m |= 1 << e
+    return m
+
+
+def rank_program(g, core, T, topo):
+    cores = list(T.cores)
+    chips = []
+    for c in cores:
+        if topo.chip(c) not in chips:
+            chips.append(topo.chip(c))
+    place = [[c for c in cores if topo.chip(c) == ch] for ch in chips]
+    aid = [[h for h in topo.cores_of(p[0]) if h not in cores and topo.die(h) == topo.die(p[0])][:2] for p in place]
+
+    def order(a):
+        return [a ^ s for s in sorted((1, 2, 3), key=lambda s: topo.same_plane(chips[a], chips[a ^ s]))]
+
+    def dst(c):
+        rid, pid, _ = topo.addr(c)
+        return DstId(rid=rid, pnc=pid)
+
+    def xs(e, q):
+        return T.XT[:, XOFF[e] + q * XW[e]:XOFF[e] + (q + 1) * XW[e]]
+
+    def cs(e, q):
+        return T.CT[:, COFF[e] + q * CW[e]:COFF[e] + (q + 1) * CW[e]]
+
+    rank = T.rank_of(core)
+    if rank is None:
+        for a in range(4):
+            if core in aid[a]:
+                j = aid[a].index(core); sent = 0
+                eng = topo.engines(core, place[a][0])
+                for e in range(3):
+                    for b in order(a):
+                        src = place[b][j]; ap = cs(e, T.rank_of(src))
+                        g.wait_ge(T.sem["ha%d_%d" % (e, b)], len(topo.engines(src, core)))
+                        g.remote_dma_fused([RemoteDMATransfer(dst_ids=[dst(c) for c in place[a]], dma_engine_mask=bits(eng),
+                                                              remote_sem=T.sem["ca%d" % e], srcs=[ap], dsts=[ap, ap])], local_sem=T.sem.loc)
+                        sent += len(eng)
+                g.wait_ge(T.sem.loc, sent)
+        return
+
+    a = chips.index(topo.chip(core)); j = place[a].index(core); mate = place[a][1 - j]
+    far = order(a)
+    off = topo.engines(core, place[far[0]][j]); on = topo.engines(core, mate); high = [e for e in on if e not in off]
+
+    Q = {"v": g.vector, "s": g.scalar, "t": g.tensor, "y": g.sync, "g": g}
+    CS = {"v": "cv", "s": "cs", "t": "ct", "g": "cg"}
+    cnt = {"cv": 0, "cs": 0, "ct": 0, "cg": 0}
+    seen = {q: {} for q in Q}
+    wr = {}; rd = {}; loc = [0]
+
+    def wait(q, toks):
+        need = {}
+        for s, v in toks:
+            need[s] = max(need.get(s, 0), v)
+        for s, v in need.items():
+            if seen[q].get(s, 0) < v:
+                Q[q].wait_ge(T.sem[s], v); seen[q][s] = v
+
+    def deps(q, R, W):
+        toks = []
+        for n in R:
+            toks += wr[n]
+        for n in W:
+            toks += wr.get(n, []) + rd.get(n, [])
+        wait(q, toks)
+
+    def done(tok, R, W):
+        for n in R:
+            rd.setdefault(n, []).append(tok)
+        for n in W:
+            wr[n] = [tok]; rd[n] = []
+
+    def op(q, R, W, fn):
+        deps(q, R, W)
+        s = CS[q]; cnt[s] += 1
+        fn().then_inc(T.sem[s], 1)
+        done((s, cnt[s]), R, W)
+
+    def dma(q, sem, R, W, out, in_):
+        deps(q, R, W)
+        Q[q].dma_start(out, in_).then_inc(T.sem[sem], 16)
+        done((sem, 16), R, W)
+
+    V = g.vector
+
+    def ts(R, W, out, in0, s1, op0, s2=None, op1=None):
+        if op1 is None:
+            op("v", R, [W], lambda: V.tensor_scalar(out, in0, s1, None, op0))
+        else:
+            op("v", R, [W], lambda: V.tensor_scalar(out, in0, s1, s2, op0, op1))
+
+    def tt(R, W, out, in0, in1, o):
+        op("v", R, [W], lambda: V.tensor_tensor(out, in0, in1, o))
+
+    def cp(R, W, out, in_):
+        op("v", R, [W], lambda: V.tensor_copy(out, in_))
+
+    def act(R, W, out, in_, f, bias=0.0):
+        op("s", R, [W], lambda: g.scalar.activation(out, in_, f, bias=bias))
+
+    def mms(R, W, ms):
+        deps("t", R, W)
+        for m in ms[:-1]:
+            g.tensor.matmul(*m)
+        cnt["ct"] += 1
+        g.tensor.matmul(*ms[-1]).then_inc(T.sem.ct, 1)
+        done(("ct", cnt["ct"]), R, W)
+
+    def col(b, i, n=16):
+        return b[:, i * 16:i * 16 + n]
+
+    def tr(cores_, eng, sem, ap):
+        loc[0] += len(eng)
+        return RemoteDMATransfer(dst_ids=[dst(c) for c in cores_], dma_engine_mask=bits(eng), remote_sem=T.sem[sem], srcs=[ap], dsts=[ap] * len(cores_))
+
+    def send_x(e):
+        deps("g", ["x%d" % e], [])
+        ap = xs(e, rank)
+        t1 = tr([place[b][j] for b in far], off, "xa%d_%d" % (e, a), ap); t2 = tr([mate], high, "xp%d" % e, ap)
+        if e == 0:
+            g.remote_dma_fused([t1], local_sem=T.sem.loc); g.remote_dma_fused([t2], local_sem=T.sem.loc)
+        else:
+            g.remote_dma_fused([t1, t2], local_sem=T.sem.loc)
+        toks = []
+        for i, b in enumerate(far):
+            tok = ("xa%d_%d" % (e, b), len(off)); toks.append(tok)
+            wait("g", [tok])
+            g.remote_dma_fused([tr([mate], on if i == 2 else high, "xp%d" % e, xs(e, T.rank_of(place[b][j])))], local_sem=T.sem.loc)
+        wr["X%d" % e] = toks + [("xp%d" % e, 3 * len(high) + len(on))] + wr["x%d" % e]
+
+    def send_c(e):
+        deps("g", ["c%d" % e], [])
+        ap = cs(e, rank)
+        g.remote_dma_fused([tr([aid[b][j] for b in far], off, "ha%d_%d" % (e, a), ap), tr([mate], high, "ca%d" % e, ap)], local_sem=T.sem.loc)
+        wr["C%d" % e] = [("ca%d" % e, len(high) + 6 * len(topo.engines(aid[a][0], core)))] + wr["c%d" % e]
+
+    cas = T.LHa[:, 512:1024]
+    dma("y", "lx", [], ["x0"], xs(0, rank), T.x0[:])
+    dma("s", "lsc", [], ["sc"], T.scs[:], T.sc0[:])
+    dma("s", "lca", [], ["cas"], cas, T.cas[:])
+    dma("y", "lro", [], ["rol"], T.rls[:], T.rol[:])
+    dma("s", "lth", [], ["th"], T.ths[:, 0:1], T.th[:])
+    dma("y", "lfr", ["rol"], ["frm"], T.frs[:], T.frm[:])
+
+    op("g", [], ["P"], lambda: g.iota(T.ci[:, 0:1], [[0, 1]], 0, 1))
+    op("g", [], ["M"], lambda: g.iota(T.M[:], [[1, 256]], 0, 0, allow_small_or_imprecise_dtypes=True))
+    send_x(0)
+    op("v", [], ["oneb"], lambda: V.memset(T.oneb[:], 1.0))
+    op("v", [], ["onef"], lambda: V.memset(T.onef[:], 1.0))
+    op("v", [], ["rst"], lambda: V.memset(T.rst[:], 0.0))
+    op("v", [], ["rst"], lambda: V.memset(T.rst[:, 0::16], 33554432.0))
+    ci = lambda i: T.ci[:, i:i + 1]
+    cf = lambda i: T.cf[:, i:i + 1]
+    ts(["P"], "ci1", ci(1), ci(0), 15, A.bitwise_and)
+    ts(["P"], "ci2", ci(2), ci(0), 112, A.bitwise_and)
+    ts(["P"], "ci3", ci(3), ci(0), 4, A.arith_shift_right, 1, A.bitwise_and)
+    cp(["ci1"], "rf", cf(0), ci(1))
+    ts(["ci1"], "r16", cf(1), ci(1), 16.0, A.mult)
+    ts(["ci1"], "r256", cf(2), ci(1), 256.0, A.mult)
+    ts(["ci2"], "tgt", cf(3), ci(2), 15.0, A.add)
+    cp(["ci3"], "m1", cf(5), ci(3))
+    ts(["ci3"], "m0", cf(4), ci(3), -1.0, A.mult, 1.0, A.add)
+    M16 = T.M[:, 0:16]
+    permf, jc, eye = col(T.kf, 0), col(T.kf, 1), col(T.kf, 2)
+    perm = col(T.ku, 0); perm2 = [col(T.ku, 1), col(T.ku, 2)]
+    ts(["M", "r16"], "permf", permf, M16, cf(1), A.add)
+    ts(["M", "rf"], "jc", jc, M16, 16.0, A.mult, cf(0), A.add)
+    ts(["M", "rf"], "eye", eye, M16, cf(0), A.is_equal)
+    ts(["permf"], "perm20", perm2[0], permf, 2.0, A.mult)
+    ts(["permf"], "perm21", perm2[1], permf, 2.0, A.mult, 1.0, A.add)
+    cp(["permf"], "perm", perm, permf)
+    ts(["M", "tgt"], "Bb", T.Bb[:], T.M[:, 0:144], cf(3), A.is_equal, 256.0, A.mult)
+    ts(["M", "tgt"], "Bf", T.Bf[:], T.M[:, 0:144], cf(3), A.is_equal)
+    cp(["M"], "Mb", T.Mb[:], T.M[:])
+    for t in range(3):
+        op("v", [], ["rz%d" % t], lambda: V.memset(T["r1%d" % t][:, 256:272], 0.0))
+    selb = lambda x: T.Bb[:, 15 - x:143 - x]
+    self_ = lambda x: T.Bf[:, 15 - x:143 - x]
+
+    def turn(R, W, blk, src, out):
+        i0 = T.tin[:, 32 * blk:32 * blk + 32]; o0 = T.tout[:, 32 * blk:32 * blk + 32]
+        ts(R + ["m0"], "ta%d" % blk, T.tin[:, 32 * blk:32 * blk + 16], src, cf(4), A.mult)
+        ts(R + ["m1"], "tb%d" % blk, T.tin[:, 32 * blk + 16:32 * blk + 32], src, cf(5), A.mult)
+        op("v", ["ta%d" % blk, "tb%d" % blk], ["to%d" % blk], lambda: V.transpose(o0, i0))
+        tt(["to%d" % blk], W, out, T.tout[:, 32 * blk:32 * blk + 16], T.tout[:, 32 * blk + 16:32 * blk + 32], A.add)
+
+    ti = lambda t, i: col(T["ti%d" % t], i)
+    tf = lambda t, i: col(T["tf%d" % t], i)
+    tu = lambda t, i: col(T["tu%d" % t], i)
+    ck = [T.LHa[:, 512:1024:2], T.LHa[:, 513:1024:2], T.LHb[:, 512:768]]
+    ckn = ["cas", "cas", "cn0"]
+    LH = [T.LHa, T.LHa, T.LHb]
+    nb = [cf(6), cf(7), cf(8)]
+    rol = T.rls[:, 0:2048]
+
+    def scene_next(t):
+        cp(["ew%d" % t], "eu%d" % t, tu(t, 1), ti(t, 0))
+        ts(["ew%d" % t], "ea%d" % t, ti(t, 1), ti(t, 0), 1.0, A.add)
+        ts(["ea%d" % t], "eb%d" % t, ti(t, 2), ti(t, 1), 2047, A.bitwise_and)
+
+    def x_offsets(t, R, src, sub):
+        ts(R, "wa", T.wa[:], src, 4097.0, A.mult, sub, A.add)
+        ts(["wa"], "wb", T.wb[:], T.wa[:], 1, A.arith_shift_right, 4095, A.bitwise_and)
+        if t == 1:
+            ts(["wb"], "wc", T.wc[:], T.wb[:], 1.0, A.add, 2048.0, A.min)
+            tt(["wb", "wc"], "wa", T.wa[:], T.wb[:], T.wc[:], A.add)
+            cp(["wa"], "xo1", T.xo1[:], T.wa[:])
+        else:
+            cp(["wb"], "xo2", T.xo2[:], T.wb[:])
+
+    def pack(e, R, lo, hi):
+        w = CW[e]
+        ts(R, "pk", T.pk[:, 0:w], hi, 4096.0, A.mult)
+        tt(R + ["pk"], "c%d" % e, cs(e, rank), T.pk[:, 0:w], lo, A.add)
+
+    def own(t):
+        src = [T.XT[:, rank * 512:rank * 512 + 512:2], T.XT[:, rank * 512 + 1:rank * 512 + 512:2], xs(1, rank)][t]
+        R = ["x1" if t == 2 else "x0"]
+        act(R, "xn%d" % t, T["xn%d" % t][:], src, F.Identity, -C1)
+        act(R, "xm%d" % t, T["xm%d" % t][:], src, F.Identity, -0.5)
+
+    def frames(t, q, r0, r1):
+        o = T["yk%d" % t][:, r0 * 256:r1 * 256]; i = T.frs[:, 0:4096].indirect(T["fo%d" % t][:, r0 * 16:r1 * 16])
+        W = ["yk%d_%d" % (t, r) for r in range(r0, r1)]
+        op(q, ["frm", "fo%d" % t], W, (lambda: V.tensor_copy(o, i)) if q == "v" else (lambda: g.scalar.activation(o, i, F.Copy)))
+
+    for t in (0, 1):
+        cp(["sc"], "er%d" % t, tu(t, 0), T.scs[:, t::2])
+    cp(["cas", "perm20"], "xo0", T.xo0[:], cas.indirect(perm2[0]))
+    pack(0, ["cas"], ck[0], ck[1])
+    send_c(0)
+    ts(["th"], "nb0", nb[0], T.ths[:, 0:1], -256.0, A.mult, -128.0, A.add)
+    for t in (0, 1):
+        turn(["sc"], "ew%d" % t, t, T.scs[:, t::2], ti(t, 0))
+        scene_next(t)
+    x_offsets(1, ["cas", "perm21"], cas.indirect(perm2[1]), -4096.0)
+    own(0)
+    for t in (0, 1):
+        cp(["rol", "er%d" % t], "fo%d" % t, T["fo%d" % t][:], rol.indirect(tu(t, 0)))
+    for t in (0, 1):
+        ts(["rol", "eu%d" % t], "f4%d" % t, T["f4%d" % t][:], rol.indirect(tu(t, 1)), 4096.0, A.mult)
+        tt(["f4%d" % t, "cas"], "fc%d" % t, T["fc%d" % t][:], T["f4%d" % t][:], ck[t], A.add)
+    frames(0, "s", 0, 4); frames(0, "v", 8, 16); frames(0, "s", 4, 8)
+
+    for t in range(3):
+        B = lambda n: T["%s%d" % (n, t)]
+        n_ = lambda n: "%s%d" % (n, t)
+        KEY = T["KEY%d" % (t & 1)]; DN = T["DN%d" % (t & 1)]; key = "KEY%d" % (t & 1); dn = "DN%d" % (t & 1)
+        win = T.XT[:, XWIN[t][0]:XWIN[t][1]]
+        XR = [["X0"], ["X0", "X1"], ["X1", "X2"]][t]; CR = [["C0"], ["C0", "C1"], ["C1", "C2"]][t]
+        yk = ["yk%d_%d" % (t, r) for r in range(16)]
+        mms(["oneb", "Mb"], [key, dn], [(KEY[:, 0:256], T.oneb[0:1, :], T.Mb[0:1, :], True, False)])
+        r0 = 0
+        for n in XCH:
+            r1 = r0 + n; c0, c1 = r0 * 256, r1 * 256
+            tt(XR + [n_("xo")] + yk[r0:r1], "dd%d_%d" % (t, r0), B("dd")[:, c0:c1], win.indirect(B("xo")[:, r0 * 16:r1 * 16]), B("yk")[:, c0:c1], A.subtract)
+            act(["dd%d_%d" % (t, r0)], "ab%d_%d" % (t, r0), B("ab")[:, c0:c1], B("dd")[:, c0:c1], F.Abs)
+            mms(["Bb", "ab%d_%d" % (t, r0)], ["k%d_%d" % (t, r0)],
+                [(KEY[:, 0:256], selb(r), B("ab")[:, r * 256:r * 256 + 256], False, r == 15) for r in range(r0, r1)])
+            if r1 == 16:
+                wr[key] = wr["k%d_%d" % (t, r0)]
+            if r1 % 4 == 0:
+                b0 = r1 - 4
+                mms(["Bb"], ["n%d_%d" % (t, b0)],
+                    [(DN[:, b0 * 16:r1 * 16], selb(k), B("ab")[:, b0 * 256 + k:r1 * 256:16], k == 0, k == 15) for k in range(16)])
+            r0 = r1
+        wr[dn] = wr["n%d_12" % t]
+        act([dn, n_("nb")], n_("sg"), B("sg")[:], DN[:, 0:256], F.Sign, nb[t])
+        mms([n_("sg"), "Bb"], ["CNT"], [(T.CNT[:, 0:16], selb(r), col(B("sg"), r), r == 0, r == 15) for r in range(16)])
+        op("v", [key, "rst"], [n_("sn")], lambda: V.tensor_tensor_scan(B("sn")[:], T.rst[:], KEY[:, 0:256], 0.0, A.add, A.min))
+        cp([n_("sn")], n_("ki"), ti(t, 3), B("sn")[:, 15::16])
+
+        def best_pair():
+            ts([n_("ki")], n_("kb"), ti(t, 5), ti(t, 3), 15, A.bitwise_and)
+            cp([n_("kb")], n_("ub"), tu(t, 3), ti(t, 5))
+            tt([n_("ub"), "eye", n_("fc")], n_("oh"), B("oh")[:], eye.indirect(tu(t, 3)), B("fc")[:], A.mult)
+            mms([n_("oh"), "Bf"], ["FCP"], [(T.FCP[:, 0:16], self_(r), B("oh")[:, r::16], r == 0, r == 15) for r in range(16)])
+
+        if t == 2:
+            best_pair()
+        ts([n_("ki")], n_("kk"), ti(t, 4), ti(t, 3), 255, A.bitwise_and)
+        ts([n_("kk"), "r256"], n_("uo"), tu(t, 2), ti(t, 4), cf(2), A.add)
+        yb = B("yk")[:, 0:4096].indirect(tu(t, 2))
+        tt(yk + [n_("uo"), n_("xm")], n_("sm"), B("sm")[:], yb, B("xm")[:], A.add)
+        tt(yk + [n_("uo"), n_("xn")], n_("Wd"), B("W")[:, 0:256], yb, B("xn")[:], A.subtract)
+        ts([n_("sm")], n_("Wa"), B("W")[:, 256:512], B("sm")[:], 2 * C1, A.add, 0.5, A.mult)
+        ts(["CNT"], n_("J"), tf(t, 0), T.CNT[:, 0:16], 256.0, A.is_ge, 256.0, A.mult)
+        tt([n_("J"), "jc"], n_("sf"), tf(t, 1), tf(t, 0), jc, A.add)
+        cp([n_("sf")], n_("us"), tu(t, 4), tf(t, 1))
+        if t == 2:
+            act([n_("sg")], n_("r1"), B("r1")[:, 0:256], B("sg")[:], F.Relu)
+        xout = T.yxs[:, 0::2] if t == 2 else xs(t + 1, rank)
+        act([n_("Wd"), n_("Wa"), n_("us")], "x%d" % (t + 1), xout, B("W")[:, 0:512].indirect(tu(t, 4)), F.Abs, -C1)
+        if t == 2:
+            dma("y", "ox", ["x3", "yxo"], [], T.yx[:], T.yxs[:])
+        else:
+            send_x(t + 1)
+            act([n_("sg")], n_("r1"), B("r1")[:, 0:256], B("sg")[:], F.Relu)
+            best_pair()
+            op("v", [n_("J")], [n_("jr")], lambda: V.tensor_reduce(cf(9 + t), tf(t, 0), AxisListType.X, A.add))
+            mms([n_("jr"), "onef"], ["AAP"], [(T.AAP[:, 0:1], T.onef[:], cf(9 + t), True, True)])
+            own(t + 1)
+        ts([n_("J")], n_("J1"), tf(t, 2), tf(t, 0), 1.0 / 256, A.mult)
+        tt([n_("J"), "permf"], n_("jb"), tf(t, 3), tf(t, 0), permf, A.max)
+        cp(["FCP"], n_("fi"), ti(t, 6), T.FCP[:, 0:16])
+        cp([n_("jb")], n_("up"), tu(t, 7), tf(t, 3))
+        fi = ti(t, 6); FI = [n_("fi")]
+
+        def scene(out, W):
+            ts(FI, n_("fb"), ti(t, 7), fi, 12, A.arith_shift_right, 2047, A.bitwise_and)
+            tt([n_("fb"), n_("eb")], n_("e1"), tf(t, 4), ti(t, 7), ti(t, 2), A.subtract)
+            tt([n_("e1"), n_("J1")], n_("e2"), tf(t, 5), tf(t, 4), tf(t, 2), A.mult)
+            tt([n_("e2"), n_("eb")], W, out, tf(t, 5), ti(t, 2), A.add)
+
+        if t == 0:
+            scene(ti(2, 0), "ew2")
+            scene_next(2)
+        if t < 2:
+            cp(["AAP"], n_("a1"), ci(4 + t), T.AAP[:, 0:1])
+            ts([n_("a1")], n_("a2"), ci(6 + t), ci(4 + t), 65535, A.bitwise_and)
+            ts([n_("a2"), "nb0"], "nb%d" % (t + 1), nb[t + 1], ci(6 + t), -1.0, A.mult, nb[0], A.add)
+            for r in range(0, 16, 4):
+                frames(t + 1, "s", r, r + 4)
+        if t == 0:
+            ts(FI, "h0", ti(t, 8), fi, 1, A.arith_shift_right, 2047, A.bitwise_and)
+            ts(FI, "s0", ti(t, 9), fi, 1, A.bitwise_and)
+            cp(["h0"], "uc0", tu(t, 5), ti(t, 8))
+        else:
+            ts(FI, n_("p"), ti(t, 10), fi, 1, A.bitwise_and)
+            ts(FI, n_("h2"), ti(t, 11), fi, 2, A.arith_shift_right, 1023, A.bitwise_and)
+            if t == 1:
+                ts(FI, "h1", ti(t, 8), fi, 1, A.arith_shift_right, 2047, A.bitwise_and)
+                ts(FI, "z1", ti(t, 12), fi, 1, A.arith_shift_right, 1, A.bitwise_and)
+                ts(["p1"], "pa1", ti(t, 13), ti(t, 10), -4096.0, A.mult, 2048.0, A.add)
+                tt(["p1", "z1"], "s1", ti(t, 9), ti(t, 10), ti(t, 12), A.max)
+                tt(["pa1", "h21"], "pb1", ti(t, 14), ti(t, 13), ti(t, 11), A.add)
+                tt(["pb1", "h1"], "pc1", ti(t, 15), ti(t, 14), ti(t, 8), A.max)
+            else:
+                ts(["p2"], "pa2", ti(t, 13), ti(t, 10), 1024.0, A.mult)
+                ts(FI, "s2", ti(t, 9), fi, 1, A.arith_shift_right, 1, A.bitwise_and)
+                tt(["pa2", "h22"], "pc2", ti(t, 15), ti(t, 13), ti(t, 11), A.add)
+            cp([n_("pc")], n_("uc"), tu(t, 5), ti(t, 15))
+        ts([n_("s")], n_("q1"), tf(t, 6), ti(t, 9), 256.0, A.mult)
+        if t == 0:
+            ts(["rol", "eu2"], "f42", T.f42[:], rol.indirect(tu(2, 1)), 4096.0, A.mult)
+        cw = T.CT[:, CWIN[t][0]:CWIN[t][1]].indirect(tu(t, 5))
+        lh = "LH%d" % (t >> 1)
+        if t > 0:
+            ts(CR + [n_("uc")], lh + "lo", LH[t][:, 0:256], cw, 4095, A.bitwise_and)
+        tt([n_("q1"), "jc"], n_("q2"), tf(t, 7), tf(t, 6), jc, A.add)
+        if t == 0:
+            ts(["f42", "perm"], "fo2", T.fo2[:], T.f42[:, 0:256].indirect(perm), 1.0 / 4096, A.mult)
+            ts(CR + [n_("uc")], lh + "lo", LH[t][:, 0:256], cw, 4095, A.bitwise_and)
+        ts(CR + [n_("uc")], lh + "hi", LH[t][:, 256:512], cw, 12, A.arith_shift_right)
+        cp([n_("q2")], n_("uq"), tu(t, 6), tf(t, 7))
+        tt([lh + "lo", lh + "hi", ckn[t], n_("uq")], n_("df"), B("df")[:], LH[t][:, 0:512].indirect(tu(t, 6)), ck[t], A.subtract)
+        tt([n_("r1"), n_("rz"), n_("up"), n_("df")], n_("dm"), B("dm")[:], B("r1")[:, 0:272].indirect(tu(t, 7)), B("df")[:], A.mult)
+        cout = [ck[2], T.ycs[:, 1::2], T.ycs[:, 0::2]][t]
+        tt([n_("dm"), ckn[t]], n_("cn"), cout, B("dm")[:], ck[t], A.add)
+        if t == 0:
+            pack(1, ["cn0"], T.LHb[:, 512:768:2], T.LHb[:, 513:768:2])
+            send_c(1)
+            x_offsets(2, ["cn0", "perm"], ck[2].indirect(perm), 0.0)
+            tt(["f42", "cn0"], "fc2", T.fc2[:], T.f42[:], ck[2], A.add)
+        elif t == 1:
+            pack(2, ["cn1"], T.ycs[:, 1::4], T.ycs[:, 3::4])
+            send_c(2)
+            scene(tf(t, 9), "en1")
+            turn(["en1"], "ye1", 2, tf(t, 9), T.yes[:, 1::2])
+            cp(["x2"], "yxo", T.yxs[:, 1::2], xs(2, rank))
+        else:
+            dma("y", "oc", ["cn1", "cn2"], [], T.yc[:], T.ycs[:])
+            scene(tf(t, 9), "en2")
+            turn(["en2"], "ye2", 3, tf(t, 9), T.yes[:, 0::2])
+            dma("s", "oe", ["ye1", "ye2"], [], T.ye[:], T.yes[:])
+
+    wait("g", [("loc", loc[0])])
+    wait("y", [("ox", 16), ("oc", 16), ("oe", 16)] + list(cnt.items()))

@@ -2,6 +2,7 @@ from concourse.bass import DstId, RemoteDMATransfer
 from concourse.mybir import AluOpType as A, AxisListType, ActivationFunctionType as F
 
 N = 8
+SIM = 128
 C1 = 12582912.0
 XOFF = (0, 4096, 6144); XW = (512, 256, 256)
 COFF = (0, 2048, 3072); CW = (256, 128, 128)
@@ -39,7 +40,7 @@ for _t in range(3):
 
 SEMAPHORES = ["cv", "cs", "ct", "cg", "loc", "lx", "lsc", "lth", "lca", "lro", "lfr", "ox", "oc", "oe"]
 for _e in range(3):
-    SEMAPHORES += ["xa%d_%d" % (_e, _a) for _a in range(4)] + ["ha%d_%d" % (_e, _a) for _a in range(4)] + ["xp%d" % _e, "ca%d" % _e]
+    SEMAPHORES += ["xa%d_%d" % (_e, _a) for _a in range(4)] + ["ha%d_%d" % (_e, _a) for _a in range(4)] + ["xp%d" % _e, "xr%d" % _e, "ca%d" % _e]
 
 
 def bits(engines):
@@ -61,6 +62,16 @@ def rank_program(g, core, T, topo):
     def order(a):
         return [a ^ s for s in sorted((1, 2, 3), key=lambda s: topo.same_plane(chips[a], chips[a ^ s]))]
 
+    def beside(a, j):
+        p = place[a][0]
+        return [h for h in range(SIM) if topo.mates(topo.chip(h), chips[a]) and topo.may_write(h, p) and (topo.die(h) == topo.die(p)) == (j == 0)]
+
+    def via_x(b, a, j):
+        return beside(a, j)[0] if b == order(a)[0] else place[a][j]
+
+    def via_c(b, a, j):
+        return aid[a][j] if topo.same_plane(chips[a], chips[b]) else beside(a, j)[1]
+
     def dst(c):
         rid, pid, _ = topo.addr(c)
         return DstId(rid=rid, pnc=pid)
@@ -73,18 +84,21 @@ def rank_program(g, core, T, topo):
 
     rank = T.rank_of(core)
     if rank is None:
-        for a in range(4):
-            if core in aid[a]:
-                j = aid[a].index(core); sent = 0
-                eng = topo.engines(core, place[a][0])
-                for e in range(3):
+        sent = 0
+        for e in range(3):
+            for a in range(4):
+                for j in range(2):
                     for b in order(a):
-                        src = place[b][j]; ap = cs(e, T.rank_of(src))
-                        g.wait_ge(T.sem["ha%d_%d" % (e, b)], len(topo.engines(src, core)))
-                        g.remote_dma_fused([RemoteDMATransfer(dst_ids=[dst(c) for c in place[a]], dma_engine_mask=bits(eng),
-                                                              remote_sem=T.sem["ca%d" % e], srcs=[ap], dsts=[ap, ap])], local_sem=T.sem.loc)
-                        sent += len(eng)
-                g.wait_ge(T.sem.loc, sent)
+                        src = place[b][j]; q = T.rank_of(src)
+                        for via, got, ap, sem in ((via_x(b, a, j), "xa", xs(e, q), "xr"), (via_c(b, a, j), "ha", cs(e, q), "ca")):
+                            if via == core:
+                                eng = topo.engines(core, place[a][0])
+                                g.wait_ge(T.sem["%s%d_%d" % (got, e, b)], len(topo.engines(src, core)))
+                                g.remote_dma_fused([RemoteDMATransfer(dst_ids=[dst(c) for c in place[a]], dma_engine_mask=bits(eng),
+                                                                      remote_sem=T.sem["%s%d" % (sem, e)], srcs=[ap], dsts=[ap, ap])], local_sem=T.sem.loc)
+                                sent += len(eng)
+        if sent:
+            g.wait_ge(T.sem.loc, sent)
         return
 
     a = chips.index(topo.chip(core)); j = place[a].index(core); mate = place[a][1 - j]
@@ -165,23 +179,26 @@ def rank_program(g, core, T, topo):
     def send_x(e):
         deps("g", ["x%d" % e], [])
         ap = xs(e, rank)
-        t1 = tr([place[b][j] for b in far], off, "xa%d_%d" % (e, a), ap); t2 = tr([mate], high, "xp%d" % e, ap)
+        t1 = tr([via_x(a, b, j) for b in far], off, "xa%d_%d" % (e, a), ap); t2 = tr([mate], high, "xp%d" % e, ap)
         if e == 0:
             g.remote_dma_fused([t1], local_sem=T.sem.loc); g.remote_dma_fused([t2], local_sem=T.sem.loc)
         else:
             g.remote_dma_fused([t1, t2], local_sem=T.sem.loc)
         toks = []
         for i, b in enumerate(far):
+            if i == 0:
+                continue
             tok = ("xa%d_%d" % (e, b), len(off)); toks.append(tok)
             wait("g", [tok])
             g.remote_dma_fused([tr([mate], on if i == 2 else high, "xp%d" % e, xs(e, T.rank_of(place[b][j])))], local_sem=T.sem.loc)
-        wr["X%d" % e] = toks + [("xp%d" % e, 3 * len(high) + len(on))] + wr["x%d" % e]
+        wr["X%d" % e] = toks + [("xp%d" % e, 2 * len(high) + len(on)), ("xr%d" % e, 2 * len(off))] + wr["x%d" % e]
 
     def send_c(e):
         deps("g", ["c%d" % e], [])
         ap = cs(e, rank)
-        g.remote_dma_fused([tr([aid[b][j] for b in far], off, "ha%d_%d" % (e, a), ap), tr([mate], high, "ca%d" % e, ap)], local_sem=T.sem.loc)
-        wr["C%d" % e] = [("ca%d" % e, len(high) + 6 * len(topo.engines(aid[a][0], core)))] + wr["c%d" % e]
+        g.remote_dma_fused([tr([via_c(a, b, j) for b in far], off, "ha%d_%d" % (e, a), ap), tr([mate], high, "ca%d" % e, ap)], local_sem=T.sem.loc)
+        n = sum(len(topo.engines(via_c(b, a, i), core)) for b in far for i in range(2))
+        wr["C%d" % e] = [("ca%d" % e, len(high) + n)] + wr["c%d" % e]
 
     cas = T.LHa[:, 512:1024]
     dma("y", "lx", [], ["x0"], xs(0, rank), T.x0[:])
@@ -219,19 +236,30 @@ def rank_program(g, core, T, topo):
     ts(["permf"], "perm21", perm2[1], permf, 2.0, A.mult, 1.0, A.add)
     cp(["permf"], "perm", perm, permf)
     ts(["M", "tgt"], "Bb", T.Bb[:], T.M[:, 0:144], cf(3), A.is_equal, 256.0, A.mult)
-    ts(["M", "tgt"], "Bf", T.Bf[:], T.M[:, 0:144], cf(3), A.is_equal)
+    ts(["M", "tgt"], "wa", T.wa[:, 0:144], T.M[:, 0:144], cf(3), A.subtract, 12.0, A.add)
+    ts(["ci1"], "ci8", ci(8), ci(1), 2, A.arith_shift_right)
+    cp(["M"], "wc", T.wc[:, 0:64], T.M[:, 0:64])
+    ts(["wa"], "wb", T.wb[:, 0:144], T.wa[:, 0:144], 4083, A.bitwise_and)
+    cp(["ci8"], "rh", cf(11), ci(8))
+    ts(["wc"], "pk", T.pk[:, 0:64], T.wc[:, 0:64], 3, A.bitwise_and)
+    ts(["wb"], "Bf", T.Bf[:], T.wb[:, 0:144], 0.0, A.is_equal)
+    ts(["pk", "rh"], "mk", T.kf[:, 64:128], T.pk[:, 0:64], cf(11), A.is_equal)
     cp(["M"], "Mb", T.Mb[:], T.M[:])
     for t in range(3):
         op("v", [], ["rz%d" % t], lambda: V.memset(T["r1%d" % t][:, 256:272], 0.0))
     selb = lambda x: T.Bb[:, 15 - x:143 - x]
-    self_ = lambda x: T.Bf[:, 15 - x:143 - x]
+    self_ = lambda x: T.Bf[:, 3 - x:131 - x]
+
+    def turn_steps(R, W, blk, src, out):
+        i0 = T.tin[:, 32 * blk:32 * blk + 32]; o0 = T.tout[:, 32 * blk:32 * blk + 32]
+        return [lambda: ts(R + ["m0"], "ta%d" % blk, T.tin[:, 32 * blk:32 * blk + 16], src, cf(4), A.mult),
+                lambda: ts(R + ["m1"], "tb%d" % blk, T.tin[:, 32 * blk + 16:32 * blk + 32], src, cf(5), A.mult),
+                lambda: op("v", ["ta%d" % blk, "tb%d" % blk], ["to%d" % blk], lambda: V.transpose(o0, i0)),
+                lambda: tt(["to%d" % blk], W, out, T.tout[:, 32 * blk:32 * blk + 16], T.tout[:, 32 * blk + 16:32 * blk + 32], A.add)]
 
     def turn(R, W, blk, src, out):
-        i0 = T.tin[:, 32 * blk:32 * blk + 32]; o0 = T.tout[:, 32 * blk:32 * blk + 32]
-        ts(R + ["m0"], "ta%d" % blk, T.tin[:, 32 * blk:32 * blk + 16], src, cf(4), A.mult)
-        ts(R + ["m1"], "tb%d" % blk, T.tin[:, 32 * blk + 16:32 * blk + 32], src, cf(5), A.mult)
-        op("v", ["ta%d" % blk, "tb%d" % blk], ["to%d" % blk], lambda: V.transpose(o0, i0))
-        tt(["to%d" % blk], W, out, T.tout[:, 32 * blk:32 * blk + 16], T.tout[:, 32 * blk + 16:32 * blk + 32], A.add)
+        for f in turn_steps(R, W, blk, src, out):
+            f()
 
     ti = lambda t, i: col(T["ti%d" % t], i)
     tf = lambda t, i: col(T["tf%d" % t], i)
@@ -312,23 +340,32 @@ def rank_program(g, core, T, topo):
                 b0 = r1 - 4
                 mms(["Bb"], ["n%d_%d" % (t, b0)],
                     [(DN[:, b0 * 16:r1 * 16], selb(k), B("ab")[:, b0 * 256 + k:r1 * 256:16], k == 0, k == 15) for k in range(16)])
+            if r0 == 0 and t > 0:
+                own(t)
             r0 = r1
         wr[dn] = wr["n%d_12" % t]
+        if t == 1:
+            ts(["rol", "eu2"], "f42", T.f42[:], rol.indirect(tu(2, 1)), 4096.0, A.mult)
+            ts(["f42", "perm"], "fo2", T.fo2[:], T.f42[:, 0:256].indirect(perm), 1.0 / 4096, A.mult)
+        if t == 2:
+            tt(["f42", "cn0"], "fc2", T.fc2[:], T.f42[:], ck[2], A.add)
+            turn(["en1"], "ye1", 2, tf(1, 9), T.yes[:, 1::2])
+            cp(["x2"], "yxo", T.yxs[:, 1::2], xs(2, rank))
         act([dn, n_("nb")], n_("sg"), B("sg")[:], DN[:, 0:256], F.Sign, nb[t])
         mms([n_("sg"), "Bb"], ["CNT"], [(T.CNT[:, 0:16], selb(r), col(B("sg"), r), r == 0, r == 15) for r in range(16)])
         op("v", [key, "rst"], [n_("sn")], lambda: V.tensor_tensor_scan(B("sn")[:], T.rst[:], KEY[:, 0:256], 0.0, A.add, A.min))
         cp([n_("sn")], n_("ki"), ti(t, 3), B("sn")[:, 15::16])
 
         def best_pair():
-            ts([n_("ki")], n_("kb"), ti(t, 5), ti(t, 3), 15, A.bitwise_and)
-            cp([n_("kb")], n_("ub"), tu(t, 3), ti(t, 5))
             tt([n_("ub"), "eye", n_("fc")], n_("oh"), B("oh")[:], eye.indirect(tu(t, 3)), B("fc")[:], A.mult)
-            mms([n_("oh"), "Bf"], ["FCP"], [(T.FCP[:, 0:16], self_(r), B("oh")[:, r::16], r == 0, r == 15) for r in range(16)])
+            mms([n_("oh"), "Bf"], ["FCP"], [(T.FCP[:, 0:64], self_(x), B("oh")[:, x::4], x == 0, x == 3) for x in range(4)])
 
+        ts([n_("ki")], n_("kk"), ti(t, 4), ti(t, 3), 255, A.bitwise_and)
+        ts([n_("ki")], n_("kb"), ti(t, 5), ti(t, 3), 15, A.bitwise_and)
+        ts([n_("kk"), "r256"], n_("uo"), tu(t, 2), ti(t, 4), cf(2), A.add)
+        cp([n_("kb")], n_("ub"), tu(t, 3), ti(t, 5))
         if t == 2:
             best_pair()
-        ts([n_("ki")], n_("kk"), ti(t, 4), ti(t, 3), 255, A.bitwise_and)
-        ts([n_("kk"), "r256"], n_("uo"), tu(t, 2), ti(t, 4), cf(2), A.add)
         yb = B("yk")[:, 0:4096].indirect(tu(t, 2))
         tt(yk + [n_("uo"), n_("xm")], n_("sm"), B("sm")[:], yb, B("xm")[:], A.add)
         tt(yk + [n_("uo"), n_("xn")], n_("Wd"), B("W")[:, 0:256], yb, B("xn")[:], A.subtract)
@@ -348,28 +385,35 @@ def rank_program(g, core, T, topo):
             best_pair()
             op("v", [n_("J")], [n_("jr")], lambda: V.tensor_reduce(cf(9 + t), tf(t, 0), AxisListType.X, A.add))
             mms([n_("jr"), "onef"], ["AAP"], [(T.AAP[:, 0:1], T.onef[:], cf(9 + t), True, True)])
-            own(t + 1)
-        ts([n_("J")], n_("J1"), tf(t, 2), tf(t, 0), 1.0 / 256, A.mult)
-        tt([n_("J"), "permf"], n_("jb"), tf(t, 3), tf(t, 0), permf, A.max)
-        cp(["FCP"], n_("fi"), ti(t, 6), T.FCP[:, 0:16])
-        cp([n_("jb")], n_("up"), tu(t, 7), tf(t, 3))
-        fi = ti(t, 6); FI = [n_("fi")]
-
-        def scene(out, W):
-            ts(FI, n_("fb"), ti(t, 7), fi, 12, A.arith_shift_right, 2047, A.bitwise_and)
-            tt([n_("fb"), n_("eb")], n_("e1"), tf(t, 4), ti(t, 7), ti(t, 2), A.subtract)
-            tt([n_("e1"), n_("J1")], n_("e2"), tf(t, 5), tf(t, 4), tf(t, 2), A.mult)
-            tt([n_("e2"), n_("eb")], W, out, tf(t, 5), ti(t, 2), A.add)
-
-        if t == 0:
-            scene(ti(2, 0), "ew2")
-            scene_next(2)
-        if t < 2:
-            cp(["AAP"], n_("a1"), ci(4 + t), T.AAP[:, 0:1])
-            ts([n_("a1")], n_("a2"), ci(6 + t), ci(4 + t), 65535, A.bitwise_and)
-            ts([n_("a2"), "nb0"], "nb%d" % (t + 1), nb[t + 1], ci(6 + t), -1.0, A.mult, nb[0], A.add)
             for r in range(0, 16, 4):
                 frames(t + 1, "s", r, r + 4)
+        if t == 1:
+            x_offsets(2, ["cn0", "perm"], ck[2].indirect(perm), 0.0)
+        tt([n_("J"), "permf"], n_("jb"), tf(t, 3), tf(t, 0), permf, A.max)
+        fm = B("tf")[:, 160:224]; fh = B("tf")[:, 224:256]
+        tt(["FCP", "mk"], n_("fm"), fm, T.FCP[:, 0:64], T.kf[:, 64:128], A.mult)
+        ts([n_("J")], n_("J1"), tf(t, 2), tf(t, 0), 1.0 / 256, A.mult)
+        tt([n_("fm")], n_("fh"), fh, B("tf")[:, 160:224:2], B("tf")[:, 161:224:2], A.add)
+        cp([n_("jb")], n_("up"), tu(t, 7), tf(t, 3))
+        tt([n_("fh")], n_("fi"), ti(t, 6), B("tf")[:, 224:256:2], B("tf")[:, 225:256:2], A.add)
+        fi = ti(t, 6); FI = [n_("fi")]
+
+        eo, en = (ti(2, 0), "ew2") if t == 0 else (tf(t, 9), n_("en"))
+        fill = [lambda: ts(FI, n_("fb"), ti(t, 7), fi, 12, A.arith_shift_right, 2047, A.bitwise_and),
+                lambda: tt([n_("fb"), n_("eb")], n_("e1"), tf(t, 4), ti(t, 7), ti(t, 2), A.subtract),
+                lambda: tt([n_("e1"), n_("J1")], n_("e2"), tf(t, 5), tf(t, 4), tf(t, 2), A.mult),
+                lambda: tt([n_("e2"), n_("eb")], en, eo, tf(t, 5), ti(t, 2), A.add)]
+        if t < 2:
+            fill += [lambda: cp(["AAP"], n_("a1"), ci(4 + t), T.AAP[:, 0:1]),
+                     lambda: ts([n_("a1")], n_("a2"), ci(6 + t), ci(4 + t), 65535, A.bitwise_and),
+                     lambda: ts([n_("a2"), "nb0"], "nb%d" % (t + 1), nb[t + 1], ci(6 + t), -1.0, A.mult, nb[0], A.add)]
+        else:
+            fill += turn_steps(["en2"], "ye2", 3, tf(t, 9), T.yes[:, 0::2])
+            fill.append(lambda: dma("s", "oe", ["ye1", "ye2"], [], T.ye[:], T.yes[:]))
+
+        def more(n=1):
+            for _ in range(min(n, len(fill))):
+                fill.pop(0)()
         if t == 0:
             ts(FI, "h0", ti(t, 8), fi, 1, A.arith_shift_right, 2047, A.bitwise_and)
             ts(FI, "s0", ti(t, 9), fi, 1, A.bitwise_and)
@@ -390,38 +434,33 @@ def rank_program(g, core, T, topo):
                 tt(["pa2", "h22"], "pc2", ti(t, 15), ti(t, 13), ti(t, 11), A.add)
             cp([n_("pc")], n_("uc"), tu(t, 5), ti(t, 15))
         ts([n_("s")], n_("q1"), tf(t, 6), ti(t, 9), 256.0, A.mult)
-        if t == 0:
-            ts(["rol", "eu2"], "f42", T.f42[:], rol.indirect(tu(2, 1)), 4096.0, A.mult)
+        more()
         cw = T.CT[:, CWIN[t][0]:CWIN[t][1]].indirect(tu(t, 5))
         lh = "LH%d" % (t >> 1)
-        if t > 0:
-            ts(CR + [n_("uc")], lh + "lo", LH[t][:, 0:256], cw, 4095, A.bitwise_and)
         tt([n_("q1"), "jc"], n_("q2"), tf(t, 7), tf(t, 6), jc, A.add)
-        if t == 0:
-            ts(["f42", "perm"], "fo2", T.fo2[:], T.f42[:, 0:256].indirect(perm), 1.0 / 4096, A.mult)
-            ts(CR + [n_("uc")], lh + "lo", LH[t][:, 0:256], cw, 4095, A.bitwise_and)
-        ts(CR + [n_("uc")], lh + "hi", LH[t][:, 256:512], cw, 12, A.arith_shift_right)
+        more()
+        if t < 2:
+            more(9)
+        ts(CR + [n_("uc")], lh + "lo", LH[t][:, 0:256], cw, 4095, A.bitwise_and)
         cp([n_("q2")], n_("uq"), tu(t, 6), tf(t, 7))
+        ts(CR + [n_("uc")], lh + "hi", LH[t][:, 256:512], cw, 12, A.arith_shift_right)
+        more()
         tt([lh + "lo", lh + "hi", ckn[t], n_("uq")], n_("df"), B("df")[:], LH[t][:, 0:512].indirect(tu(t, 6)), ck[t], A.subtract)
+        more(2)
         tt([n_("r1"), n_("rz"), n_("up"), n_("df")], n_("dm"), B("dm")[:], B("r1")[:, 0:272].indirect(tu(t, 7)), B("df")[:], A.mult)
+        more(2)
         cout = [ck[2], T.ycs[:, 1::2], T.ycs[:, 0::2]][t]
         tt([n_("dm"), ckn[t]], n_("cn"), cout, B("dm")[:], ck[t], A.add)
         if t == 0:
             pack(1, ["cn0"], T.LHb[:, 512:768:2], T.LHb[:, 513:768:2])
             send_c(1)
-            x_offsets(2, ["cn0", "perm"], ck[2].indirect(perm), 0.0)
-            tt(["f42", "cn0"], "fc2", T.fc2[:], T.f42[:], ck[2], A.add)
+            scene_next(2)
         elif t == 1:
             pack(2, ["cn1"], T.ycs[:, 1::4], T.ycs[:, 3::4])
             send_c(2)
-            scene(tf(t, 9), "en1")
-            turn(["en1"], "ye1", 2, tf(t, 9), T.yes[:, 1::2])
-            cp(["x2"], "yxo", T.yxs[:, 1::2], xs(2, rank))
         else:
             dma("y", "oc", ["cn1", "cn2"], [], T.yc[:], T.ycs[:])
-            scene(tf(t, 9), "en2")
-            turn(["en2"], "ye2", 3, tf(t, 9), T.yes[:, 0::2])
-            dma("s", "oe", ["ye1", "ye2"], [], T.ye[:], T.yes[:])
+            more(9)
 
     wait("g", [("loc", loc[0])])
     wait("y", [("ox", 16), ("oc", 16), ("oe", 16)] + list(cnt.items()))

@@ -8,7 +8,9 @@ XOFF = (0, 4096, 6144); XW = (512, 256, 256)
 COFF = (0, 2048, 3072); CW = (256, 128, 128)
 XWIN = ((0, 4096), (0, 6144), (4096, 8192))
 CWIN = ((0, 2048), (0, 3072), (2048, 4096))
-XCH = (4, 4, 4, 2, 1, 1)
+BPC = ((0, 2), (2, 4), (4, 6), (6, 7), (7, 8))
+APC = ((8, 10), (10, 12), (12, 14), (14, 15), (15, 16))
+NB = sum(b - a for a, b in BPC)
 
 SCRATCH = {
     "XT": ("sbuf", [128, 8192], "bfloat16"), "CT": ("sbuf", [128, 4096], "int32"),
@@ -25,15 +27,18 @@ SCRATCH = {
     "yxs": ("sbuf", [128, 512], "bfloat16"), "ycs": ("sbuf", [128, 512], "float32"), "yes": ("sbuf", [128, 32], "float32"),
     "wa": ("sbuf", [128, 256], "int32"), "wb": ("sbuf", [128, 256], "int32"), "wc": ("sbuf", [128, 256], "int32"),
     "pk": ("sbuf", [128, 256], "int32"),
-    "KEY0": ("psum", [128, 512], "float32"), "KEY1": ("psum", [128, 512], "float32"),
-    "DN0": ("psum", [128, 512], "float32"), "DN1": ("psum", [128, 512], "float32"),
-    "CNT": ("psum", [128, 512], "float32"), "FCP": ("psum", [128, 512], "float32"), "AAP": ("psum", [128, 512], "float32"),
+    "keep": ("sbuf", [128, 256], "bfloat16"), "Bo": ("sbuf", [128, 128], "float32"), "E": ("sbuf", [128, 256], "float32"),
+    "Bn": ("sbuf", [128, 144], "bfloat16"), "B2": ("sbuf", [128, 144], "bfloat16"), "Id": ("sbuf", [128, 128], "bfloat16"),
+    "KEY": ("psum", [128, 512], "float32"), "FCP": ("psum", [128, 512], "float32"), "AAP": ("psum", [128, 512], "float32"),
 }
+for _i in range((NB + 1) // 2):
+    SCRATCH["YP%d" % _i] = ("psum", [128, 512], "float32")
 for _t in range(3):
     for _n, _w, _d in (("yk", 4096, "bfloat16"), ("dd", 4096, "bfloat16"), ("ab", 4096, "bfloat16"),
                        ("xo", 256, "uint16"), ("fo", 256, "uint16"), ("f4", 256, "float32"), ("fc", 256, "float32"),
                        ("xm", 256, "float32"), ("xn", 256, "float32"), ("sm", 256, "float32"), ("W", 512, "float32"),
-                       ("sn", 256, "float32"), ("sg", 256, "bfloat16"), ("r1", 272, "bfloat16"), ("oh", 256, "float32"),
+                       ("sn", 256, "float32"), ("rj", 288, "bfloat16"), ("r1", 560, "bfloat16"), ("oh", 256, "float32"),
+                       ("TH", 256, "float32"), ("nr", 256, "bfloat16"),
                        ("df", 256, "float32"), ("dm", 256, "float32"),
                        ("ti", 256, "int32"), ("tf", 256, "float32"), ("tu", 128, "uint16")):
         SCRATCH["%s%d" % (_n, _t)] = ("sbuf", [128, _w], _d)
@@ -158,8 +163,8 @@ def rank_program(g, core, T, topo):
     def cp(R, W, out, in_):
         op("v", R, [W], lambda: V.tensor_copy(out, in_))
 
-    def act(R, W, out, in_, f, bias=0.0):
-        op("s", R, [W], lambda: g.scalar.activation(out, in_, f, bias=bias))
+    def act(R, W, out, in_, f, bias=0.0, scale=1.0):
+        op("s", R, [W], lambda: g.scalar.activation(out, in_, f, bias=bias, scale=scale))
 
     def mms(R, W, ms):
         deps("t", R, W)
@@ -203,9 +208,9 @@ def rank_program(g, core, T, topo):
     cas = T.LHa[:, 512:1024]
     dma("y", "lx", [], ["x0"], xs(0, rank), T.x0[:])
     dma("s", "lsc", [], ["sc"], T.scs[:], T.sc0[:])
-    dma("s", "lca", [], ["cas"], cas, T.cas[:])
-    dma("y", "lro", [], ["rol"], T.rls[:], T.rol[:])
     dma("s", "lth", [], ["th"], T.ths[:, 0:1], T.th[:])
+    dma("y", "lca", [], ["cas"], cas, T.cas[:])
+    dma("y", "lro", [], ["rol"], T.rls[:], T.rol[:])
     dma("y", "lfr", ["rol"], ["frm"], T.frs[:], T.frm[:])
 
     op("g", [], ["P"], lambda: g.iota(T.ci[:, 0:1], [[0, 1]], 0, 1))
@@ -246,8 +251,26 @@ def rank_program(g, core, T, topo):
     ts(["pk", "rh"], "mk", T.kf[:, 64:128], T.pk[:, 0:64], cf(11), A.is_equal)
     cp(["M"], "Mb", T.Mb[:], T.M[:])
     for t in range(3):
-        op("v", [], ["rz%d" % t], lambda: V.memset(T["r1%d" % t][:, 256:272], 0.0))
+        op("v", [], ["rz%d" % t], lambda: V.memset(T["r1%d" % t][:, 544:560], 0.0))
+        op("v", [], ["rp%d" % t], lambda: V.memset(T["rj%d" % t][:], 0.0))
+    op("v", [], ["keep"], lambda: V.memset(T.keep[:], 1.0))
+    op("v", [], ["keep"], lambda: V.memset(T.keep[:, 0::16], 0.0))
+    roff = col(T.kf, 3)
+    cp(["M"], "wa", T.wa[:], T.M[:])
+    ts(["wa"], "wb", T.wb[:], T.wa[:], 15, A.bitwise_and)
+    ts(["wa"], "wc", T.wc[:, 0:128], T.wa[:, 0:128], 112, A.bitwise_and)
+    ts(["wa"], "pk", T.pk[:, 0:16], T.wa[:, 0:16], 1, A.bitwise_and)
+    ts(["wc", "tgt"], "Bo", T.Bo[:], T.wc[:, 0:128], 15.0, A.add, cf(3), A.is_equal)
+    ts(["pk", "m1"], "ro0", T.tin[:, 96:112], T.pk[:, 0:16], cf(5), A.not_equal, 272.0, A.mult)
+    tt(["ro0", "jc"], "roff", roff, T.tin[:, 96:112], jc, A.add)
+    if NB:
+        ts(["M", "tgt"], "Bn", T.Bn[:], T.M[:, 0:144], cf(3), A.is_equal, -256.0, A.mult)
+        ts(["M", "tgt"], "B2", T.B2[:], T.M[:, 0:144], cf(3), A.is_equal, 512.0, A.mult)
+        cp(["P"], "pf", cf(12), ci(0))
+        ts(["M", "pf"], "Id", T.Id[:], T.M[:, 0:128], cf(12), A.is_equal)
     selb = lambda x: T.Bb[:, 15 - x:143 - x]
+    seln = lambda x: T.Bn[:, 15 - x:143 - x]
+    sel2 = lambda x: T.B2[:, 15 - x:143 - x]
     self_ = lambda x: T.Bf[:, 3 - x:131 - x]
 
     def turn_steps(R, W, blk, src, out):
@@ -275,15 +298,16 @@ def rank_program(g, core, T, topo):
         ts(["ew%d" % t], "ea%d" % t, ti(t, 1), ti(t, 0), 1.0, A.add)
         ts(["ea%d" % t], "eb%d" % t, ti(t, 2), ti(t, 1), 2047, A.bitwise_and)
 
-    def x_offsets(t, R, src, sub):
-        ts(R, "wa", T.wa[:], src, 4097.0, A.mult, sub, A.add)
+    def x_offsets(t):
+        ts([ckn[t]], "wa", T.wa[:], ck[t], 4097.0, A.mult, -4096.0 if t == 1 else 0.0, A.add)
         ts(["wa"], "wb", T.wb[:], T.wa[:], 1, A.arith_shift_right, 4095, A.bitwise_and)
         if t == 1:
             ts(["wb"], "wc", T.wc[:], T.wb[:], 1.0, A.add, 2048.0, A.min)
             tt(["wb", "wc"], "wa", T.wa[:], T.wb[:], T.wc[:], A.add)
-            cp(["wa"], "xo1", T.xo1[:], T.wa[:])
+            cp(["wa", "perm"], "xo1", T.xo1[:], T.wa[:, 0:256].indirect(perm))
+            ts(["wa"], "f41", T.f41[:], T.wa[:], -3072.0, A.add, 4096.0, A.mult)
         else:
-            cp(["wb"], "xo2", T.xo2[:], T.wb[:])
+            cp(["wb", "perm"], "xo2", T.xo2[:], T.wb[:, 0:256].indirect(perm))
 
     def pack(e, R, lo, hi):
         w = CW[e]
@@ -303,110 +327,150 @@ def rank_program(g, core, T, topo):
 
     for t in (0, 1):
         cp(["sc"], "er%d" % t, tu(t, 0), T.scs[:, t::2])
+    ts(["th"], "nb0", nb[0], T.ths[:, 0:1], 256.0, A.mult, 255.0, A.add)
+    ts(["wb", "rf", "nb0"], "E", T.E[:], T.wb[:], cf(0), A.is_equal, nb[0], A.mult)
+    mms(["E", "Bo"], ["AAP"], [(T.AAP[:, 0:256], T.Bo[:], T.E[:], True, True)])
+    own(0); own(1)
+    act(["AAP"], "TH0", T.TH0[:], T.AAP[:, 0:256], F.Copy)
+    turns = [turn_steps(["sc"], "ew%d" % t, t, T.scs[:, t::2], ti(t, 0)) for t in (0, 1)]
+    for f0, f1 in zip(*turns):
+        f0(); f1()
+    for t in (0, 1):
+        scene_next(t)
     cp(["cas", "perm20"], "xo0", T.xo0[:], cas.indirect(perm2[0]))
     pack(0, ["cas"], ck[0], ck[1])
     send_c(0)
-    ts(["th"], "nb0", nb[0], T.ths[:, 0:1], -256.0, A.mult, -128.0, A.add)
-    for t in (0, 1):
-        turn(["sc"], "ew%d" % t, t, T.scs[:, t::2], ti(t, 0))
-        scene_next(t)
-    x_offsets(1, ["cas", "perm21"], cas.indirect(perm2[1]), -4096.0)
-    own(0)
+    ts(["cas"], "f40", T.f40[:], ck[0], 4096.0, A.mult)
+    x_offsets(1)
     for t in (0, 1):
         cp(["rol", "er%d" % t], "fo%d" % t, T["fo%d" % t][:], rol.indirect(tu(t, 0)))
-    for t in (0, 1):
-        ts(["rol", "eu%d" % t], "f4%d" % t, T["f4%d" % t][:], rol.indirect(tu(t, 1)), 4096.0, A.mult)
-        tt(["f4%d" % t, "cas"], "fc%d" % t, T["fc%d" % t][:], T["f4%d" % t][:], ck[t], A.add)
+
+    def pair(t):
+        if t < 2:
+            tt(["rol", "eu%d" % t, "f4%d" % t], "fc%d" % t, T["fc%d" % t][:], rol.indirect(tu(t, 1)), T["f4%d" % t][:], A.add)
+        else:
+            tt(["f42", "wb"], "fc2", T.fc2[:], T.f42[:], T.wb[:], A.add)
+    pair(0)
     frames(0, "s", 0, 4); frames(0, "v", 8, 16); frames(0, "s", 4, 8)
 
     for t in range(3):
         B = lambda n: T["%s%d" % (n, t)]
         n_ = lambda n: "%s%d" % (n, t)
-        KEY = T["KEY%d" % (t & 1)]; DN = T["DN%d" % (t & 1)]; key = "KEY%d" % (t & 1); dn = "DN%d" % (t & 1)
+        KEY = T.KEY; key = "KEY"
         win = T.XT[:, XWIN[t][0]:XWIN[t][1]]
         XR = [["X0"], ["X0", "X1"], ["X1", "X2"]][t]; CR = [["C0"], ["C0", "C1"], ["C1", "C2"]][t]
         yk = ["yk%d_%d" % (t, r) for r in range(16)]
-        mms(["oneb", "Mb"], [key, dn], [(KEY[:, 0:256], T.oneb[0:1, :], T.Mb[0:1, :], True, False)])
-        r0 = 0
-        for n in XCH:
-            r1 = r0 + n; c0, c1 = r0 * 256, r1 * 256
-            tt(XR + [n_("xo")] + yk[r0:r1], "dd%d_%d" % (t, r0), B("dd")[:, c0:c1], win.indirect(B("xo")[:, r0 * 16:r1 * 16]), B("yk")[:, c0:c1], A.subtract)
-            act(["dd%d_%d" % (t, r0)], "ab%d_%d" % (t, r0), B("ab")[:, c0:c1], B("dd")[:, c0:c1], F.Abs)
-            mms(["Bb", "ab%d_%d" % (t, r0)], ["k%d_%d" % (t, r0)],
-                [(KEY[:, 0:256], selb(r), B("ab")[:, r * 256:r * 256 + 256], False, r == 15) for r in range(r0, r1)])
-            if r1 == 16:
-                wr[key] = wr["k%d_%d" % (t, r0)]
-            if r1 % 4 == 0:
-                b0 = r1 - 4
-                mms(["Bb"], ["n%d_%d" % (t, b0)],
-                    [(DN[:, b0 * 16:r1 * 16], selb(k), B("ab")[:, b0 * 256 + k:r1 * 256:16], k == 0, k == 15) for k in range(16)])
-            if r0 == 0 and t > 0:
-                own(t)
-            r0 = r1
-        wr[dn] = wr["n%d_12" % t]
+        mms(["oneb", "Mb"], [key], [(KEY[:, 0:256], T.oneb[0:1, :], T.Mb[0:1, :], True, False)])
+        blk = lambda n, r0, r1: B(n)[:, r0 * 256:r1 * 256]
+        yp = lambda r: T["YP%d" % (r // 2)][:, (r % 2) * 256:(r % 2) * 256 + 256]
+        for r in range(0, NB, 2):
+            mms(["Id", "Bn"] + yk[r:r + 2], ["YP%d" % (r // 2)],
+                [(T["YP%d" % (r // 2)][:], T.Id[:], blk("yk", r, r + 2), True, True)] +
+                [(KEY[:, 0:256], seln(x), blk("yk", x, x + 1), False, False) for x in (r, r + 1)])
+        steps = max(len(APC), len(BPC))
+
+        def sums(sel, R, n, r0, r1, last):
+            mms(R, ["k%s%d_%d" % (n, t, r0)], [(KEY[:, 0:256], sel(r), blk(n, r, r + 1), False, last and r == r1 - 1) for r in range(r0, r1)])
+            if last:
+                wr[key] = wr["k%s%d_%d" % (n, t, r0)]
+        for i in range(steps + 1):
+            if i < len(APC):
+                r0, r1 = APC[i]
+                tt(XR + [n_("xo")] + yk[r0:r1], "dd%d_%d" % (t, r0), blk("dd", r0, r1), win.indirect(B("xo")[:, r0 * 16:r1 * 16]), blk("yk", r0, r1), A.subtract)
+            if i < len(BPC):
+                r0, r1 = BPC[i]
+                act(XR + [n_("xo")], "dd%d_%d" % (t, r0), blk("dd", r0, r1), win.indirect(B("xo")[:, r0 * 16:r1 * 16]), F.Copy)
+                sums(seln, ["Bn", "dd%d_%d" % (t, r0)], "dd", r0, r1, False)
+            if 0 < i <= len(BPC):
+                r0, r1 = BPC[i - 1]
+                for x0, x1 in ((r0, r1),) if r0 // 2 == (r1 - 1) // 2 else [(r, r + 1) for r in range(r0, r1)]:
+                    tt(["dd%d_%d" % (t, r0), "YP%d" % (x0 // 2)], "ab%d_%d" % (t, x0), blk("ab", x0, x1), blk("dd", x0, x1),
+                       T["YP%d" % (x0 // 2)][:, (x0 % 2) * 256:(x0 % 2 + x1 - x0) * 256], A.max)
+                    sums(sel2, ["B2", "ab%d_%d" % (t, x0)], "ab", x0, x1, False)
+            if 0 < i <= len(APC):
+                r0, r1 = APC[i - 1]
+                act(["dd%d_%d" % (t, r0)], "ab%d_%d" % (t, r0), blk("ab", r0, r1), blk("dd", r0, r1), F.Abs)
+                sums(selb, ["Bb", "ab%d_%d" % (t, r0)], "ab", r0, r1, i == steps)
         if t == 1:
-            ts(["rol", "eu2"], "f42", T.f42[:], rol.indirect(tu(2, 1)), 4096.0, A.mult)
             ts(["f42", "perm"], "fo2", T.fo2[:], T.f42[:, 0:256].indirect(perm), 1.0 / 4096, A.mult)
-        if t == 2:
-            tt(["f42", "cn0"], "fc2", T.fc2[:], T.f42[:], ck[2], A.add)
-            turn(["en1"], "ye1", 2, tf(1, 9), T.yes[:, 1::2])
-            cp(["x2"], "yxo", T.yxs[:, 1::2], xs(2, rank))
-        act([dn, n_("nb")], n_("sg"), B("sg")[:], DN[:, 0:256], F.Sign, nb[t])
-        mms([n_("sg"), "Bb"], ["CNT"], [(T.CNT[:, 0:16], selb(r), col(B("sg"), r), r == 0, r == 15) for r in range(16)])
+        else:
+            pair(1 if t == 0 else 2)
+        if t < 2:
+            frames(t + 1, "s", 0, 3)
         op("v", [key, "rst"], [n_("sn")], lambda: V.tensor_tensor_scan(B("sn")[:], T.rst[:], KEY[:, 0:256], 0.0, A.add, A.min))
+        tt([key, n_("TH"), n_("rp")], n_("rj"), B("rj")[:, 16:272], KEY[:, 0:256], B("TH")[:], A.is_gt)
         cp([n_("sn")], n_("ki"), ti(t, 3), B("sn")[:, 15::16])
+        count = lambda: op("v", [n_("rj"), "keep"], [n_("nr")], lambda: V.tensor_tensor_scan(B("nr")[:], T.keep[:], B("rj")[:, 16:272], 0.0, A.mult, A.add))
+
+        def turn_rejected():
+            op("v", [n_("rj"), n_("rp")], [n_("r1")], lambda: V.transpose(B("r1")[:, 0:256], B("rj")[:, 16:272]))
+            op("v", [n_("rj"), n_("rp")], [n_("r2")], lambda: V.transpose(B("r1")[:, 256:544], B("rj")[:, 0:288]))
 
         def best_pair():
             tt([n_("ub"), "eye", n_("fc")], n_("oh"), B("oh")[:], eye.indirect(tu(t, 3)), B("fc")[:], A.mult)
             mms([n_("oh"), "Bf"], ["FCP"], [(T.FCP[:, 0:64], self_(x), B("oh")[:, x::4], x == 0, x == 3) for x in range(4)])
 
+        kb = lambda: ts([n_("ki")], n_("kb"), ti(t, 5), ti(t, 3), 15, A.bitwise_and)
+        ub = lambda: cp([n_("kb")], n_("ub"), tu(t, 3), ti(t, 5))
+        nrej = B("nr")[:, 15::16]
+        count()
+        if t == 2:
+            kb()
         ts([n_("ki")], n_("kk"), ti(t, 4), ti(t, 3), 255, A.bitwise_and)
-        ts([n_("ki")], n_("kb"), ti(t, 5), ti(t, 3), 15, A.bitwise_and)
-        ts([n_("kk"), "r256"], n_("uo"), tu(t, 2), ti(t, 4), cf(2), A.add)
-        cp([n_("kb")], n_("ub"), tu(t, 3), ti(t, 5))
+        if t == 2:
+            ub()
+        ts([n_("nr")], n_("J"), tf(t, 0), nrej, 9.0, A.is_ge, 256.0, A.mult)
         if t == 2:
             best_pair()
+        ts([n_("kk"), "r256"], n_("uo"), tu(t, 2), ti(t, 4), cf(2), A.add)
+        tt([n_("J"), "jc"], n_("sf"), tf(t, 1), tf(t, 0), jc, A.add)
         yb = B("yk")[:, 0:4096].indirect(tu(t, 2))
         tt(yk + [n_("uo"), n_("xm")], n_("sm"), B("sm")[:], yb, B("xm")[:], A.add)
-        tt(yk + [n_("uo"), n_("xn")], n_("Wd"), B("W")[:, 0:256], yb, B("xn")[:], A.subtract)
-        ts([n_("sm")], n_("Wa"), B("W")[:, 256:512], B("sm")[:], 2 * C1, A.add, 0.5, A.mult)
-        ts(["CNT"], n_("J"), tf(t, 0), T.CNT[:, 0:16], 256.0, A.is_ge, 256.0, A.mult)
-        tt([n_("J"), "jc"], n_("sf"), tf(t, 1), tf(t, 0), jc, A.add)
         cp([n_("sf")], n_("us"), tu(t, 4), tf(t, 1))
-        if t == 2:
-            act([n_("sg")], n_("r1"), B("r1")[:, 0:256], B("sg")[:], F.Relu)
+        tt(yk + [n_("uo"), n_("xn")], n_("Wd"), B("W")[:, 0:256], yb, B("xn")[:], A.subtract)
+        act([n_("sm")], n_("Wa"), B("W")[:, 256:512], B("sm")[:], F.Identity, C1, 0.5)
         xout = T.yxs[:, 0::2] if t == 2 else xs(t + 1, rank)
         act([n_("Wd"), n_("Wa"), n_("us")], "x%d" % (t + 1), xout, B("W")[:, 0:512].indirect(tu(t, 4)), F.Abs, -C1)
         if t == 2:
             dma("y", "ox", ["x3", "yxo"], [], T.yx[:], T.yxs[:])
         else:
             send_x(t + 1)
-            act([n_("sg")], n_("r1"), B("r1")[:, 0:256], B("sg")[:], F.Relu)
-            best_pair()
+            kb()
             op("v", [n_("J")], [n_("jr")], lambda: V.tensor_reduce(cf(9 + t), tf(t, 0), AxisListType.X, A.add))
+            ub()
             mms([n_("jr"), "onef"], ["AAP"], [(T.AAP[:, 0:1], T.onef[:], cf(9 + t), True, True)])
-            for r in range(0, 16, 4):
-                frames(t + 1, "s", r, r + 4)
+        ts([n_("nr")], n_("J2"), tf(t, 8), nrej, 9.0, A.is_ge, 544.0, A.mult)
+        if t < 2:
+            best_pair()
+            for r0, r1 in ((3, 8), (8, 12), (12, 16)):
+                frames(t + 1, "s", r0, r1)
+            if t == 0:
+                own(2)
+            else:
+                act(["x2"], "yxo", T.yxs[:, 1::2], xs(2, rank), F.Copy)
+            turn_rejected()
         if t == 1:
-            x_offsets(2, ["cn0", "perm"], ck[2].indirect(perm), 0.0)
-        tt([n_("J"), "permf"], n_("jb"), tf(t, 3), tf(t, 0), permf, A.max)
+            x_offsets(2)
         fm = B("tf")[:, 160:224]; fh = B("tf")[:, 224:256]
         tt(["FCP", "mk"], n_("fm"), fm, T.FCP[:, 0:64], T.kf[:, 64:128], A.mult)
-        ts([n_("J")], n_("J1"), tf(t, 2), tf(t, 0), 1.0 / 256, A.mult)
+        tt([n_("J2"), "roff"], n_("jb"), tf(t, 3), tf(t, 8), roff, A.max)
         tt([n_("fm")], n_("fh"), fh, B("tf")[:, 160:224:2], B("tf")[:, 161:224:2], A.add)
-        cp([n_("jb")], n_("up"), tu(t, 7), tf(t, 3))
+        ts([n_("J")], n_("J1"), tf(t, 2), tf(t, 0), 1.0 / 256, A.mult)
         tt([n_("fh")], n_("fi"), ti(t, 6), B("tf")[:, 224:256:2], B("tf")[:, 225:256:2], A.add)
+        cp([n_("jb")], n_("up"), tu(t, 7), tf(t, 3))
         fi = ti(t, 6); FI = [n_("fi")]
+        at = 12 if t < 2 else 0
 
         eo, en = (ti(2, 0), "ew2") if t == 0 else (tf(t, 9), n_("en"))
-        fill = [lambda: ts(FI, n_("fb"), ti(t, 7), fi, 12, A.arith_shift_right, 2047, A.bitwise_and),
+        fill = [lambda: ts(FI, n_("fb"), ti(t, 7), fi, 12 - at, A.arith_shift_right, 2047, A.bitwise_and),
                 lambda: tt([n_("fb"), n_("eb")], n_("e1"), tf(t, 4), ti(t, 7), ti(t, 2), A.subtract),
                 lambda: tt([n_("e1"), n_("J1")], n_("e2"), tf(t, 5), tf(t, 4), tf(t, 2), A.mult),
                 lambda: tt([n_("e2"), n_("eb")], en, eo, tf(t, 5), ti(t, 2), A.add)]
         if t < 2:
             fill += [lambda: cp(["AAP"], n_("a1"), ci(4 + t), T.AAP[:, 0:1]),
                      lambda: ts([n_("a1")], n_("a2"), ci(6 + t), ci(4 + t), 65535, A.bitwise_and),
-                     lambda: ts([n_("a2"), "nb0"], "nb%d" % (t + 1), nb[t + 1], ci(6 + t), -1.0, A.mult, nb[0], A.add)]
+                     lambda: cp([n_("a2")], "nb%d" % (t + 1), nb[t + 1], ci(6 + t)),
+                     lambda: act(["nb%d" % (t + 1), "TH0"], "TH%d" % (t + 1), T["TH%d" % (t + 1)][:], T.TH0[:], F.Identity, nb[t + 1])]
         else:
             fill += turn_steps(["en2"], "ye2", 3, tf(t, 9), T.yes[:, 0::2])
             fill.append(lambda: dma("s", "oe", ["ye1", "ye2"], [], T.ye[:], T.yes[:]))
@@ -414,50 +478,44 @@ def rank_program(g, core, T, topo):
         def more(n=1):
             for _ in range(min(n, len(fill))):
                 fill.pop(0)()
-        if t == 0:
-            ts(FI, "h0", ti(t, 8), fi, 1, A.arith_shift_right, 2047, A.bitwise_and)
-            ts(FI, "s0", ti(t, 9), fi, 1, A.bitwise_and)
-            cp(["h0"], "uc0", tu(t, 5), ti(t, 8))
+        if t < 2:
+            ts(FI, n_("h"), ti(t, 8), fi, 13, A.arith_shift_right)
         else:
-            ts(FI, n_("p"), ti(t, 10), fi, 1, A.bitwise_and)
-            ts(FI, n_("h2"), ti(t, 11), fi, 2, A.arith_shift_right, 1023, A.bitwise_and)
-            if t == 1:
-                ts(FI, "h1", ti(t, 8), fi, 1, A.arith_shift_right, 2047, A.bitwise_and)
-                ts(FI, "z1", ti(t, 12), fi, 1, A.arith_shift_right, 1, A.bitwise_and)
-                ts(["p1"], "pa1", ti(t, 13), ti(t, 10), -4096.0, A.mult, 2048.0, A.add)
-                tt(["p1", "z1"], "s1", ti(t, 9), ti(t, 10), ti(t, 12), A.max)
-                tt(["pa1", "h21"], "pb1", ti(t, 14), ti(t, 13), ti(t, 11), A.add)
-                tt(["pb1", "h1"], "pc1", ti(t, 15), ti(t, 14), ti(t, 8), A.max)
-            else:
-                ts(["p2"], "pa2", ti(t, 13), ti(t, 10), 1024.0, A.mult)
-                ts(FI, "s2", ti(t, 9), fi, 1, A.arith_shift_right, 1, A.bitwise_and)
-                tt(["pa2", "h22"], "pc2", ti(t, 15), ti(t, 13), ti(t, 11), A.add)
-            cp([n_("pc")], n_("uc"), tu(t, 5), ti(t, 15))
+            ts(FI, n_("h"), ti(t, 8), fi, 1, A.arith_shift_right, 2047, A.bitwise_and)
+        ts(FI, n_("s"), ti(t, 9), fi, at, A.arith_shift_right, 1, A.bitwise_and)
+        ts([n_("h")], n_("uc"), tu(t, 5), ti(t, 8), 1536.0 if t == 1 else 0.0, A.add)
         ts([n_("s")], n_("q1"), tf(t, 6), ti(t, 9), 256.0, A.mult)
-        more()
         cw = T.CT[:, CWIN[t][0]:CWIN[t][1]].indirect(tu(t, 5))
         lh = "LH%d" % (t >> 1)
-        tt([n_("q1"), "jc"], n_("q2"), tf(t, 7), tf(t, 6), jc, A.add)
-        more()
         if t < 2:
-            more(9)
+            more(4)
         ts(CR + [n_("uc")], lh + "lo", LH[t][:, 0:256], cw, 4095, A.bitwise_and)
-        cp([n_("q2")], n_("uq"), tu(t, 6), tf(t, 7))
+        tt([n_("q1"), "jc"], n_("q2"), tf(t, 7), tf(t, 6), jc, A.add)
         ts(CR + [n_("uc")], lh + "hi", LH[t][:, 256:512], cw, 12, A.arith_shift_right)
-        more()
+        cp([n_("q2")], n_("uq"), tu(t, 6), tf(t, 7))
+        if t == 2:
+            turn_rejected()
+        else:
+            more()
         tt([lh + "lo", lh + "hi", ckn[t], n_("uq")], n_("df"), B("df")[:], LH[t][:, 0:512].indirect(tu(t, 6)), ck[t], A.subtract)
-        more(2)
-        tt([n_("r1"), n_("rz"), n_("up"), n_("df")], n_("dm"), B("dm")[:], B("r1")[:, 0:272].indirect(tu(t, 7)), B("df")[:], A.mult)
-        more(2)
+        more()
+        tt([n_("r1"), n_("r2"), n_("rz"), n_("up"), n_("df")], n_("dm"), B("dm")[:], B("r1")[:, 0:560].indirect(tu(t, 7)), B("df")[:], A.mult)
+        more()
         cout = [ck[2], T.ycs[:, 1::2], T.ycs[:, 0::2]][t]
         tt([n_("dm"), ckn[t]], n_("cn"), cout, B("dm")[:], ck[t], A.add)
         if t == 0:
+            more(9)
+            cp(["ew2"], "eu2", tu(2, 1), ti(2, 0))
             pack(1, ["cn0"], T.LHb[:, 512:768:2], T.LHb[:, 513:768:2])
             send_c(1)
-            scene_next(2)
+            ts(["ew2"], "ea2", ti(2, 1), ti(2, 0), 1.0, A.add)
+            ts(["rol", "eu2"], "f42", T.f42[:], rol.indirect(tu(2, 1)), 4096.0, A.mult)
+            ts(["ea2"], "eb2", ti(2, 2), ti(2, 1), 2047, A.bitwise_and)
         elif t == 1:
+            more(9)
             pack(2, ["cn1"], T.ycs[:, 1::4], T.ycs[:, 3::4])
             send_c(2)
+            turn(["en1"], "ye1", 2, tf(1, 9), T.yes[:, 1::2])
         else:
             dma("y", "oc", ["cn1", "cn2"], [], T.yc[:], T.ycs[:])
             more(9)

@@ -8,18 +8,19 @@ XOFF = (0, 4096, 6144); XW = (512, 256, 256)
 COFF = (0, 2048, 3072); CW = (256, 128, 128)
 XWIN = ((0, 4096), (0, 6144), (4096, 8192))
 CWIN = ((0, 2048), (0, 3072), (2048, 4096))
-BPC = ((0, 2), (2, 4), (4, 6), (6, 7), (7, 8))
-APC = ((8, 10), (10, 12), (12, 14), (14, 15), (15, 16))
-NB = sum(b - a for a, b in BPC)
+EARLY = (3, 3)
+PIECES = ((0, 2, "B"), (2, 4, "B"), (4, 6, "B"), (6, 7, "B"), (7, 8, "B"), (8, 10, "A"), (10, 12, "A"), (12, 14, "A"), (14, 15, "A"), (15, 16, "A"))
 
 SCRATCH = {
     "XT": ("sbuf", [128, 8192], "bfloat16"), "CT": ("sbuf", [128, 4096], "int32"),
     "frs": ("sbuf", [128, 4096], "bfloat16"), "rls": ("sbuf", [128, 2048], "int32"),
-    "LHa": ("sbuf", [128, 1024], "int32"), "LHb": ("sbuf", [128, 768], "int32"),
+    "LHa": ("sbuf", [128, 1024], "int32"), "LHb": ("sbuf", [128, 512], "int32"), "cn0": ("sbuf", [128, 256], "float32"),
+    "rj": ("sbuf", [128, 288], "bfloat16"), "r1": ("sbuf", [128, 560], "bfloat16"), "TH": ("sbuf", [128, 256], "float32"),
+    "ar": ("sbuf", [128, 128], "bfloat16"),
     "scs": ("sbuf", [128, 32], "int32"), "ths": ("sbuf", [128, 8], "int32"),
     "M": ("sbuf", [128, 256], "float32"), "Mb": ("sbuf", [128, 256], "bfloat16"),
     "Bb": ("sbuf", [128, 144], "bfloat16"), "Bf": ("sbuf", [128, 144], "float32"),
-    "oneb": ("sbuf", [128, 128], "bfloat16"), "onef": ("sbuf", [128, 128], "float32"),
+    "oneb": ("sbuf", [128, 256], "bfloat16"), "onef": ("sbuf", [128, 128], "float32"),
     "rst": ("sbuf", [128, 256], "float32"),
     "ci": ("sbuf", [128, 16], "int32"), "cf": ("sbuf", [128, 16], "float32"),
     "kf": ("sbuf", [128, 128], "float32"), "ku": ("sbuf", [128, 64], "uint16"),
@@ -29,21 +30,22 @@ SCRATCH = {
     "pk": ("sbuf", [128, 256], "int32"),
     "keep": ("sbuf", [128, 256], "bfloat16"), "Bo": ("sbuf", [128, 128], "float32"), "E": ("sbuf", [128, 256], "float32"),
     "Bn": ("sbuf", [128, 144], "bfloat16"), "B2": ("sbuf", [128, 144], "bfloat16"), "Id": ("sbuf", [128, 128], "bfloat16"),
-    "KEY": ("psum", [128, 512], "float32"), "FCP": ("psum", [128, 512], "float32"), "AAP": ("psum", [128, 512], "float32"),
+    "Idn": ("sbuf", [128, 128], "bfloat16"),
+    "KEY": ("psum", [128, 512], "float32"), "FCP": ("psum", [128, 512], "float32"), "XP": ("psum", [128, 512], "float32"),
+    "rr": ("sbuf", [128, 256], "bfloat16"),
 }
-for _i in range((NB + 1) // 2):
+for _i in range(4):
     SCRATCH["YP%d" % _i] = ("psum", [128, 512], "float32")
 for _t in range(3):
     for _n, _w, _d in (("yk", 4096, "bfloat16"), ("dd", 4096, "bfloat16"), ("ab", 4096, "bfloat16"),
                        ("xo", 256, "uint16"), ("fo", 256, "uint16"), ("f4", 256, "float32"), ("fc", 256, "float32"),
-                       ("xm", 256, "float32"), ("xn", 256, "float32"), ("sm", 256, "float32"), ("W", 512, "float32"),
-                       ("sn", 256, "float32"), ("rj", 288, "bfloat16"), ("r1", 560, "bfloat16"), ("oh", 256, "float32"),
-                       ("TH", 256, "float32"), ("nr", 256, "bfloat16"),
+                       ("xn", 256, "float32"), ("sm", 256, "float32"), ("W", 512, "float32"),
+                       ("sn", 256, "float32"), ("oh", 256, "float32"), ("nr", 256, "bfloat16"),
                        ("df", 256, "float32"), ("dm", 256, "float32"),
                        ("ti", 256, "int32"), ("tf", 256, "float32"), ("tu", 128, "uint16")):
         SCRATCH["%s%d" % (_n, _t)] = ("sbuf", [128, _w], _d)
 
-SEMAPHORES = ["cv", "cs", "ct", "cg", "loc", "lx", "lsc", "lth", "lca", "lro", "lfr", "ox", "oc", "oe"]
+SEMAPHORES = ["cv", "cs", "ct", "cg", "loc", "lx", "lsc", "lth", "lca", "lro", "lfr", "ox", "oc0", "oc1", "oe"]
 for _e in range(3):
     SEMAPHORES += ["xa%d_%d" % (_e, _a) for _a in range(4)] + ["ha%d_%d" % (_e, _a) for _a in range(4)] + ["xp%d" % _e, "xr%d" % _e, "ca%d" % _e]
 
@@ -53,6 +55,15 @@ def bits(engines):
     for e in engines:
         m |= 1 << e
     return m
+
+
+def distance_order():
+    n = len(PIECES) // 2; out = []
+    for i in range(n + 1):
+        for step, p, sums in (("diff", n + i, None), ("pick", i, "less"), ("max", i - 1, "twice"), ("abs", n + i - 1, "sum")):
+            if (i < n if step in ("diff", "pick") else i > 0):
+                out += [(step, p, None)] + [(sums, p, r) for r in range(*PIECES[p][:2]) if sums]
+    return out
 
 
 def rank_program(g, core, T, topo):
@@ -71,8 +82,11 @@ def rank_program(g, core, T, topo):
         p = place[a][0]
         return [h for h in range(SIM) if topo.mates(topo.chip(h), chips[a]) and topo.may_write(h, p) and (topo.die(h) == topo.die(p)) == (j == 0)]
 
-    def via_x(b, a, j):
-        return beside(a, j)[0] if b == order(a)[0] else place[a][j]
+    def across(a, j):
+        return [h for h in topo.cores_of(place[a][0]) if topo.die(h) != topo.die(place[a][0])][j]
+
+    def high_of(c, a):
+        return [e for e in topo.engines(c, aid[a][0]) if e not in topo.engines(c, place[order(a)[2]][0])]
 
     def via_c(b, a, j):
         return aid[a][j] if topo.same_plane(chips[a], chips[b]) else beside(a, j)[1]
@@ -93,15 +107,24 @@ def rank_program(g, core, T, topo):
         for e in range(3):
             for a in range(4):
                 for j in range(2):
-                    for b in order(a):
-                        src = place[b][j]; q = T.rank_of(src)
-                        for via, got, ap, sem in ((via_x(b, a, j), "xa", xs(e, q), "xr"), (via_c(b, a, j), "ha", cs(e, q), "ca")):
-                            if via == core:
-                                eng = topo.engines(core, place[a][0])
-                                g.wait_ge(T.sem["%s%d_%d" % (got, e, b)], len(topo.engines(src, core)))
-                                g.remote_dma_fused([RemoteDMATransfer(dst_ids=[dst(c) for c in place[a]], dma_engine_mask=bits(eng),
-                                                                      remote_sem=T.sem["%s%d" % (sem, e)], srcs=[ap], dsts=[ap, ap])], local_sem=T.sem.loc)
-                                sent += len(eng)
+                    if across(a, j) == core:
+                        ap = xs(e, T.rank_of(place[a][j])); to = place[order(a)[2]]
+                        g.wait_ge(T.sem["xa%d_%d" % (e, a)], len(high_of(place[a][j], a)))
+                        two = ((to, topo.engines(core, to[0]), "xr%d" % e), ([place[a][1 - j]], high_of(core, a), "xa%d_%d" % (e, a)))
+                        g.remote_dma_fused([RemoteDMATransfer(dst_ids=[dst(c) for c in cs_], dma_engine_mask=bits(eng), remote_sem=T.sem[sem],
+                                                              srcs=[ap], dsts=[ap] * len(cs_)) for cs_, eng, sem in two], local_sem=T.sem.loc)
+                        sent += sum(len(x[1]) for x in two)
+                    b = order(a)[0]
+                    jobs = [(beside(a, j)[0], "xa%d_%d" % (e, b), len(topo.engines(place[b][j], beside(a, j)[0])), xs(e, T.rank_of(place[b][j])), "xr", place[a])]
+                    jobs += [(via_c(b, a, j), "ha%d_%d" % (e, b), len(topo.engines(place[b][j], via_c(b, a, j))), cs(e, T.rank_of(place[b][j])), "ca", place[a])
+                             for b in order(a)]
+                    for via, got, n, ap, sem, to in jobs:
+                        if via == core:
+                            eng = topo.engines(core, to[0])
+                            g.wait_ge(T.sem[got], n)
+                            g.remote_dma_fused([RemoteDMATransfer(dst_ids=[dst(c) for c in to], dma_engine_mask=bits(eng),
+                                                                  remote_sem=T.sem["%s%d" % (sem, e)], srcs=[ap], dsts=[ap] * len(to))], local_sem=T.sem.loc)
+                            sent += len(eng)
         if sent:
             g.wait_ge(T.sem.loc, sent)
         return
@@ -181,22 +204,17 @@ def rank_program(g, core, T, topo):
         loc[0] += len(eng)
         return RemoteDMATransfer(dst_ids=[dst(c) for c in cores_], dma_engine_mask=bits(eng), remote_sem=T.sem[sem], srcs=[ap], dsts=[ap] * len(cores_))
 
-    def send_x(e):
+    def send_x(e, meanwhile=None):
         deps("g", ["x%d" % e], [])
         ap = xs(e, rank)
-        t1 = tr([via_x(a, b, j) for b in far], off, "xa%d_%d" % (e, a), ap); t2 = tr([mate], high, "xp%d" % e, ap)
-        if e == 0:
-            g.remote_dma_fused([t1], local_sem=T.sem.loc); g.remote_dma_fused([t2], local_sem=T.sem.loc)
-        else:
-            g.remote_dma_fused([t1, t2], local_sem=T.sem.loc)
-        toks = []
-        for i, b in enumerate(far):
-            if i == 0:
-                continue
-            tok = ("xa%d_%d" % (e, b), len(off)); toks.append(tok)
-            wait("g", [tok])
-            g.remote_dma_fused([tr([mate], on if i == 2 else high, "xp%d" % e, xs(e, T.rank_of(place[b][j])))], local_sem=T.sem.loc)
-        wr["X%d" % e] = toks + [("xp%d" % e, 2 * len(high) + len(on)), ("xr%d" % e, 2 * len(off))] + wr["x%d" % e]
+        g.remote_dma_fused([tr([beside(far[0], j)[0], place[far[1]][j]], off, "xa%d_%d" % (e, a), ap),
+                            tr([across(a, j)], high, "xa%d_%d" % (e, a), ap)], local_sem=T.sem.loc)
+        if meanwhile:
+            meanwhile()
+        toks = [("xa%d_%d" % (e, far[1]), len(off))]
+        wait("g", toks)
+        g.remote_dma_fused([tr([mate], on, "xp%d" % e, xs(e, T.rank_of(place[far[1]][j])))], local_sem=T.sem.loc)
+        wr["X%d" % e] = toks + [("xa%d_%d" % (e, a), len(high)), ("xp%d" % e, len(on)), ("xr%d" % e, 4 * len(off))] + wr["x%d" % e]
 
     def send_c(e):
         deps("g", ["c%d" % e], [])
@@ -215,10 +233,18 @@ def rank_program(g, core, T, topo):
 
     op("g", [], ["P"], lambda: g.iota(T.ci[:, 0:1], [[0, 1]], 0, 1))
     op("g", [], ["M"], lambda: g.iota(T.M[:], [[1, 256]], 0, 0, allow_small_or_imprecise_dtypes=True))
-    send_x(0)
-    op("v", [], ["oneb"], lambda: V.memset(T.oneb[:], 1.0))
-    op("v", [], ["onef"], lambda: V.memset(T.onef[:], 1.0))
+
+    def patterns():
+        for n, out, pat, base in (("K16", T.E[:], [[0, 16], [1, 16]], 0), ("K2", T.tin[:, 96:112], [[0, 8], [1, 2]], 0),
+                                  ("K4", T.tout[:, 64:128], [[0, 16], [1, 4]], 0), ("KL", T.sn0[:, 0:128], [[16, 8], [0, 16]], 15)):
+            op("g", [], [n], lambda: g.iota(out, pat, base, 0, allow_small_or_imprecise_dtypes=True))
+    send_x(0, patterns)
+    act(["M"], "oneb", T.oneb[:], T.M[:], F.Identity, 1.0, 0.0)
+    act(["M"], "onef", T.onef[:], T.M[:, 0:128], F.Identity, 1.0, 0.0)
+    act(["M"], "Mb", T.Mb[:], T.M[:], F.Copy)
     op("v", [], ["rst"], lambda: V.memset(T.rst[:], 0.0))
+    op("v", [], ["rz"], lambda: V.memset(T.r1[:, 544:560], 0.0))
+    op("v", [], ["rj"], lambda: V.memset(T.rj[:], 0.0))
     op("v", [], ["rst"], lambda: V.memset(T.rst[:, 0::16], 33554432.0))
     ci = lambda i: T.ci[:, i:i + 1]
     cf = lambda i: T.cf[:, i:i + 1]
@@ -238,36 +264,20 @@ def rank_program(g, core, T, topo):
     ts(["M", "rf"], "jc", jc, M16, 16.0, A.mult, cf(0), A.add)
     ts(["M", "rf"], "eye", eye, M16, cf(0), A.is_equal)
     ts(["permf"], "perm20", perm2[0], permf, 2.0, A.mult)
-    ts(["permf"], "perm21", perm2[1], permf, 2.0, A.mult, 1.0, A.add)
     cp(["permf"], "perm", perm, permf)
     ts(["M", "tgt"], "Bb", T.Bb[:], T.M[:, 0:144], cf(3), A.is_equal, 256.0, A.mult)
     ts(["M", "tgt"], "wa", T.wa[:, 0:144], T.M[:, 0:144], cf(3), A.subtract, 12.0, A.add)
     ts(["ci1"], "ci8", ci(8), ci(1), 2, A.arith_shift_right)
-    cp(["M"], "wc", T.wc[:, 0:64], T.M[:, 0:64])
+    cp(["P"], "pf", cf(12), ci(0))
     ts(["wa"], "wb", T.wb[:, 0:144], T.wa[:, 0:144], 4083, A.bitwise_and)
     cp(["ci8"], "rh", cf(11), ci(8))
-    ts(["wc"], "pk", T.pk[:, 0:64], T.wc[:, 0:64], 3, A.bitwise_and)
+    ts(["M", "pf"], "Id", T.Id[:], T.M[:, 0:128], cf(12), A.is_equal)
     ts(["wb"], "Bf", T.Bf[:], T.wb[:, 0:144], 0.0, A.is_equal)
-    ts(["pk", "rh"], "mk", T.kf[:, 64:128], T.pk[:, 0:64], cf(11), A.is_equal)
-    cp(["M"], "Mb", T.Mb[:], T.M[:])
-    for t in range(3):
-        op("v", [], ["rz%d" % t], lambda: V.memset(T["r1%d" % t][:, 544:560], 0.0))
-        op("v", [], ["rp%d" % t], lambda: V.memset(T["rj%d" % t][:], 0.0))
-    op("v", [], ["keep"], lambda: V.memset(T.keep[:], 1.0))
-    op("v", [], ["keep"], lambda: V.memset(T.keep[:, 0::16], 0.0))
+    act(["rst"], "keep", T.keep[:], T.rst[:], F.Identity, 1.0, -1.0 / 33554432.0)
+    act(["Bb"], "Bn", T.Bn[:], T.Bb[:], F.Identity, 0.0, -1.0)
+    act(["Bb"], "B2", T.B2[:], T.Bb[:], F.Identity, 0.0, 2.0)
+    act(["Id"], "Idn", T.Idn[:], T.Id[:], F.Identity, 0.0, -1.0)
     roff = col(T.kf, 3)
-    cp(["M"], "wa", T.wa[:], T.M[:])
-    ts(["wa"], "wb", T.wb[:], T.wa[:], 15, A.bitwise_and)
-    ts(["wa"], "wc", T.wc[:, 0:128], T.wa[:, 0:128], 112, A.bitwise_and)
-    ts(["wa"], "pk", T.pk[:, 0:16], T.wa[:, 0:16], 1, A.bitwise_and)
-    ts(["wc", "tgt"], "Bo", T.Bo[:], T.wc[:, 0:128], 15.0, A.add, cf(3), A.is_equal)
-    ts(["pk", "m1"], "ro0", T.tin[:, 96:112], T.pk[:, 0:16], cf(5), A.not_equal, 272.0, A.mult)
-    tt(["ro0", "jc"], "roff", roff, T.tin[:, 96:112], jc, A.add)
-    if NB:
-        ts(["M", "tgt"], "Bn", T.Bn[:], T.M[:, 0:144], cf(3), A.is_equal, -256.0, A.mult)
-        ts(["M", "tgt"], "B2", T.B2[:], T.M[:, 0:144], cf(3), A.is_equal, 512.0, A.mult)
-        cp(["P"], "pf", cf(12), ci(0))
-        ts(["M", "pf"], "Id", T.Id[:], T.M[:, 0:128], cf(12), A.is_equal)
     selb = lambda x: T.Bb[:, 15 - x:143 - x]
     seln = lambda x: T.Bn[:, 15 - x:143 - x]
     sel2 = lambda x: T.B2[:, 15 - x:143 - x]
@@ -287,7 +297,7 @@ def rank_program(g, core, T, topo):
     ti = lambda t, i: col(T["ti%d" % t], i)
     tf = lambda t, i: col(T["tf%d" % t], i)
     tu = lambda t, i: col(T["tu%d" % t], i)
-    ck = [T.LHa[:, 512:1024:2], T.LHa[:, 513:1024:2], T.LHb[:, 512:768]]
+    ck = [T.LHa[:, 512:1024:2], T.LHa[:, 513:1024:2], T.cn0[:]]
     ckn = ["cas", "cas", "cn0"]
     LH = [T.LHa, T.LHa, T.LHb]
     nb = [cf(6), cf(7), cf(8)]
@@ -311,14 +321,14 @@ def rank_program(g, core, T, topo):
 
     def pack(e, R, lo, hi):
         w = CW[e]
-        ts(R, "pk", T.pk[:, 0:w], hi, 4096.0, A.mult)
-        tt(R + ["pk"], "c%d" % e, cs(e, rank), T.pk[:, 0:w], lo, A.add)
+        ts(R, "FCP", T.FCP[:, 256:256 + w], hi, 4096.0, A.mult)
+        tt(R + ["FCP"], "c%d" % e, cs(e, rank), T.FCP[:, 256:256 + w], lo, A.add)
+
+    mine = [T.XT[:, rank * 512:rank * 512 + 512:2], T.XT[:, rank * 512 + 1:rank * 512 + 512:2], xs(1, rank)]
+    minen = ["x0", "x0", "x1"]
 
     def own(t):
-        src = [T.XT[:, rank * 512:rank * 512 + 512:2], T.XT[:, rank * 512 + 1:rank * 512 + 512:2], xs(1, rank)][t]
-        R = ["x1" if t == 2 else "x0"]
-        act(R, "xn%d" % t, T["xn%d" % t][:], src, F.Identity, -C1)
-        act(R, "xm%d" % t, T["xm%d" % t][:], src, F.Identity, -0.5)
+        act([minen[t]], "xn%d" % t, T["xn%d" % t][:], mine[t], F.Identity, -C1)
 
     def frames(t, q, r0, r1):
         o = T["yk%d" % t][:, r0 * 256:r1 * 256]; i = T.frs[:, 0:4096].indirect(T["fo%d" % t][:, r0 * 16:r1 * 16])
@@ -327,11 +337,7 @@ def rank_program(g, core, T, topo):
 
     for t in (0, 1):
         cp(["sc"], "er%d" % t, tu(t, 0), T.scs[:, t::2])
-    ts(["th"], "nb0", nb[0], T.ths[:, 0:1], 256.0, A.mult, 255.0, A.add)
-    ts(["wb", "rf", "nb0"], "E", T.E[:], T.wb[:], cf(0), A.is_equal, nb[0], A.mult)
-    mms(["E", "Bo"], ["AAP"], [(T.AAP[:, 0:256], T.Bo[:], T.E[:], True, True)])
     own(0); own(1)
-    act(["AAP"], "TH0", T.TH0[:], T.AAP[:, 0:256], F.Copy)
     turns = [turn_steps(["sc"], "ew%d" % t, t, T.scs[:, t::2], ti(t, 0)) for t in (0, 1)]
     for f0, f1 in zip(*turns):
         f0(); f1()
@@ -340,6 +346,14 @@ def rank_program(g, core, T, topo):
     cp(["cas", "perm20"], "xo0", T.xo0[:], cas.indirect(perm2[0]))
     pack(0, ["cas"], ck[0], ck[1])
     send_c(0)
+    ts(["th"], "nb0", nb[0], T.ths[:, 0:1], 256.0, A.mult, 255.0, A.add)
+    ts(["KL", "tgt"], "Bo", T.Bo[:], T.sn0[:, 0:128], cf(3), A.is_equal)
+    ts(["K16", "rf", "nb0"], "K16", T.E[:], T.E[:], cf(0), A.is_equal, nb[0], A.mult)
+    mms(["K16", "Bo"], ["KEY"], [(T.KEY[:, 0:256], T.Bo[:], T.E[:], True, True)])
+    act(["KEY"], "TH", T.TH[:], T.KEY[:, 0:256], F.Copy)
+    ts(["K2", "m1"], "K2", T.tin[:, 96:112], T.tin[:, 96:112], cf(5), A.not_equal, 272.0, A.mult)
+    ts(["K4", "rh"], "mk", T.kf[:, 64:128], T.tout[:, 64:128], cf(11), A.is_equal)
+    tt(["K2", "jc"], "roff", roff, T.tin[:, 96:112], jc, A.add)
     ts(["cas"], "f40", T.f40[:], ck[0], 4096.0, A.mult)
     x_offsets(1)
     for t in (0, 1):
@@ -351,6 +365,7 @@ def rank_program(g, core, T, topo):
         else:
             tt(["f42", "wb"], "fc2", T.fc2[:], T.f42[:], T.wb[:], A.add)
     pair(0)
+    cp(["cas"], "FCP", T.FCP[:, 256:512], ck[0])
     frames(0, "s", 0, 4); frames(0, "v", 8, 16); frames(0, "s", 4, 8)
 
     for t in range(3):
@@ -360,51 +375,59 @@ def rank_program(g, core, T, topo):
         win = T.XT[:, XWIN[t][0]:XWIN[t][1]]
         XR = [["X0"], ["X0", "X1"], ["X1", "X2"]][t]; CR = [["C0"], ["C0", "C1"], ["C1", "C2"]][t]
         yk = ["yk%d_%d" % (t, r) for r in range(16)]
-        mms(["oneb", "Mb"], [key], [(KEY[:, 0:256], T.oneb[0:1, :], T.Mb[0:1, :], True, False)])
+        mms(["oneb", "Mb"], [key], [(KEY[:, 0:256], T.oneb[0:1, 0:128], T.Mb[0:1, :], True, False)])
+        if t > 0:
+            mms(["oneb", n_("ar")], [n_("ka")], [(KEY[:, 0:256], T.ar[0:1, :], T.oneb[0:1, :], False, False)])
         blk = lambda n, r0, r1: B(n)[:, r0 * 256:r1 * 256]
-        yp = lambda r: T["YP%d" % (r // 2)][:, (r % 2) * 256:(r % 2) * 256 + 256]
-        for r in range(0, NB, 2):
-            mms(["Id", "Bn"] + yk[r:r + 2], ["YP%d" % (r // 2)],
-                [(T["YP%d" % (r // 2)][:], T.Id[:], blk("yk", r, r + 2), True, True)] +
-                [(KEY[:, 0:256], seln(x), blk("yk", x, x + 1), False, False) for x in (r, r + 1)])
-        steps = max(len(APC), len(BPC))
-
-        def sums(sel, R, n, r0, r1, last):
-            mms(R, ["k%s%d_%d" % (n, t, r0)], [(KEY[:, 0:256], sel(r), blk(n, r, r + 1), False, last and r == r1 - 1) for r in range(r0, r1)])
-            if last:
-                wr[key] = wr["k%s%d_%d" % (n, t, r0)]
-        for i in range(steps + 1):
-            if i < len(APC):
-                r0, r1 = APC[i]
-                tt(XR + [n_("xo")] + yk[r0:r1], "dd%d_%d" % (t, r0), blk("dd", r0, r1), win.indirect(B("xo")[:, r0 * 16:r1 * 16]), blk("yk", r0, r1), A.subtract)
-            if i < len(BPC):
-                r0, r1 = BPC[i]
-                act(XR + [n_("xo")], "dd%d_%d" % (t, r0), blk("dd", r0, r1), win.indirect(B("xo")[:, r0 * 16:r1 * 16]), F.Copy)
-                sums(seln, ["Bn", "dd%d_%d" % (t, r0)], "dd", r0, r1, False)
-            if 0 < i <= len(BPC):
-                r0, r1 = BPC[i - 1]
-                for x0, x1 in ((r0, r1),) if r0 // 2 == (r1 - 1) // 2 else [(r, r + 1) for r in range(r0, r1)]:
-                    tt(["dd%d_%d" % (t, r0), "YP%d" % (x0 // 2)], "ab%d_%d" % (t, x0), blk("ab", x0, x1), blk("dd", x0, x1),
-                       T["YP%d" % (x0 // 2)][:, (x0 % 2) * 256:(x0 % 2 + x1 - x0) * 256], A.max)
-                    sums(sel2, ["B2", "ab%d_%d" % (t, x0)], "ab", x0, x1, False)
-            if 0 < i <= len(APC):
-                r0, r1 = APC[i - 1]
-                act(["dd%d_%d" % (t, r0)], "ab%d_%d" % (t, r0), blk("ab", r0, r1), blk("dd", r0, r1), F.Abs)
-                sums(selb, ["Bb", "ab%d_%d" % (t, r0)], "ab", r0, r1, i == steps)
-        if t == 1:
+        yp = lambda r0, r1: T["YP%d" % (r0 // 2)][:, 256 * (r0 % 2):256 * (r0 % 2 + r1 - r0)]
+        for r0, r1, w in PIECES:
+            if w in "CD":
+                mms(["Idn"] + yk[r0:r1], ["YP%d" % (r0 // 2)], [(yp(r0, r1), T.Idn[:], blk("yk", r0, r1), True, False)])
+            elif w == "B":
+                mms(["Id", "Bn"] + yk[r0:r1], ["YP%d" % (r0 // 2)], [(yp(r0, r1), T.Id[:], blk("yk", r0, r1), True, True)] +
+                    [(KEY[:, 0:256], seln(r), blk("yk", r, r + 1), False, False) for r in range(r0, r1)])
+        calls = distance_order()
+        for step, i, r in calls:
+            r0, r1, w = PIECES[i]
+            dd, ab, y = "dd%d_%d" % (t, r0), "ab%d_%d" % (t, r0), "YP%d" % (r0 // 2)
+            xk = win.indirect(B("xo")[:, r0 * 16:r1 * 16])
+            if step == "diff":
+                tt(XR + [n_("xo")] + yk[r0:r1], dd, blk("dd", r0, r1), xk, blk("yk", r0, r1), A.subtract)
+            elif step == "take":
+                cp(XR + [n_("xo")], dd, blk("dd", r0, r1), xk)
+            elif step == "pick":
+                act(XR + [n_("xo")], dd, blk("dd", r0, r1), xk, F.Copy)
+            elif step == "max":
+                tt([dd, y], ab, blk("ab", r0, r1), blk("dd", r0, r1), yp(r0, r1), A.max)
+            elif step == "add":
+                mms(["Id", dd], [y], [(yp(r0, r1), T.Id[:], blk("dd", r0, r1), False, True)])
+            elif step == "abs":
+                act([dd if w == "A" else y], ab, blk("ab", r0, r1), blk("dd", r0, r1) if w == "A" else yp(r0, r1), F.Abs)
+            else:
+                sel, wt, n, src = {"less": (seln, "Bn", "dd", dd), "twice": (sel2, "B2", "ab", ab), "sum": (selb, "Bb", "ab", ab)}[step]
+                last = (step, i, r) == calls[-1]
+                mms([wt, src], [key] if last else [], [(KEY[:, 0:256], sel(r), blk(n, r, r + 1), False, last)])
+        if t == 0:
+            pair(1)
+        elif t == 1:
             ts(["f42", "perm"], "fo2", T.fo2[:], T.f42[:, 0:256].indirect(perm), 1.0 / 4096, A.mult)
         else:
-            pair(1 if t == 0 else 2)
+            pair(2)
+        if t == 1:
+            own(2)
         if t < 2:
-            frames(t + 1, "s", 0, 3)
+            frames(t + 1, "s", 0, EARLY[t])
+        else:
+            act(["cn0"], "XP", T.XP[:, 0:256], ck[2], F.Copy)
+            act(["x2"], "yxo", T.yxs[:, 1::2], xs(2, rank), F.Copy)
         op("v", [key, "rst"], [n_("sn")], lambda: V.tensor_tensor_scan(B("sn")[:], T.rst[:], KEY[:, 0:256], 0.0, A.add, A.min))
-        tt([key, n_("TH"), n_("rp")], n_("rj"), B("rj")[:, 16:272], KEY[:, 0:256], B("TH")[:], A.is_gt)
+        tt([key, "TH"], "rj", T.rj[:, 16:272], KEY[:, 0:256], T.TH[:], A.is_gt)
         cp([n_("sn")], n_("ki"), ti(t, 3), B("sn")[:, 15::16])
-        count = lambda: op("v", [n_("rj"), "keep"], [n_("nr")], lambda: V.tensor_tensor_scan(B("nr")[:], T.keep[:], B("rj")[:, 16:272], 0.0, A.mult, A.add))
+        count = lambda: op("v", ["rj", "keep"], [n_("nr")], lambda: V.tensor_tensor_scan(B("nr")[:], T.keep[:], T.rj[:, 16:272], 0.0, A.mult, A.add))
 
         def turn_rejected():
-            op("v", [n_("rj"), n_("rp")], [n_("r1")], lambda: V.transpose(B("r1")[:, 0:256], B("rj")[:, 16:272]))
-            op("v", [n_("rj"), n_("rp")], [n_("r2")], lambda: V.transpose(B("r1")[:, 256:544], B("rj")[:, 0:288]))
+            op("v", ["rj"], ["r1"], lambda: V.transpose(T.r1[:, 0:256], T.rj[:, 16:272]))
+            op("v", ["rj"], ["r2"], lambda: V.transpose(T.r1[:, 256:544], T.rj[:, 0:288]))
 
         def best_pair():
             tt([n_("ub"), "eye", n_("fc")], n_("oh"), B("oh")[:], eye.indirect(tu(t, 3)), B("fc")[:], A.mult)
@@ -425,10 +448,10 @@ def rank_program(g, core, T, topo):
         ts([n_("kk"), "r256"], n_("uo"), tu(t, 2), ti(t, 4), cf(2), A.add)
         tt([n_("J"), "jc"], n_("sf"), tf(t, 1), tf(t, 0), jc, A.add)
         yb = B("yk")[:, 0:4096].indirect(tu(t, 2))
-        tt(yk + [n_("uo"), n_("xm")], n_("sm"), B("sm")[:], yb, B("xm")[:], A.add)
+        tt(yk + [n_("uo"), minen[t]], n_("sm"), B("sm")[:], yb, mine[t], A.add)
         cp([n_("sf")], n_("us"), tu(t, 4), tf(t, 1))
         tt(yk + [n_("uo"), n_("xn")], n_("Wd"), B("W")[:, 0:256], yb, B("xn")[:], A.subtract)
-        act([n_("sm")], n_("Wa"), B("W")[:, 256:512], B("sm")[:], F.Identity, C1, 0.5)
+        act([n_("sm")], n_("Wa"), B("W")[:, 256:512], B("sm")[:], F.Identity, C1, 0.4995)
         xout = T.yxs[:, 0::2] if t == 2 else xs(t + 1, rank)
         act([n_("Wd"), n_("Wa"), n_("us")], "x%d" % (t + 1), xout, B("W")[:, 0:512].indirect(tu(t, 4)), F.Abs, -C1)
         if t == 2:
@@ -438,26 +461,28 @@ def rank_program(g, core, T, topo):
             kb()
             op("v", [n_("J")], [n_("jr")], lambda: V.tensor_reduce(cf(9 + t), tf(t, 0), AxisListType.X, A.add))
             ub()
-            mms([n_("jr"), "onef"], ["AAP"], [(T.AAP[:, 0:1], T.onef[:], cf(9 + t), True, True)])
+            mms([n_("jr"), "onef"], ["FCP"], [(T.FCP[:, 64:65], T.onef[:], cf(9 + t), True, True)])
         ts([n_("nr")], n_("J2"), tf(t, 8), nrej, 9.0, A.is_ge, 544.0, A.mult)
         if t < 2:
             best_pair()
-            for r0, r1 in ((3, 8), (8, 12), (12, 16)):
+            for r0, r1 in ((EARLY[t], 6), (6, 10), (10, 16)):
                 frames(t + 1, "s", r0, r1)
-            if t == 0:
-                own(2)
-            else:
-                act(["x2"], "yxo", T.yxs[:, 1::2], xs(2, rank), F.Copy)
-            turn_rejected()
+        turn_rejected()
         if t == 1:
             x_offsets(2)
+        tt([n_("J2"), "roff"], n_("jb"), tf(t, 3), tf(t, 8), roff, A.max)
+        ts([n_("J")], n_("J1"), tf(t, 2), tf(t, 0), 1.0 / 256, A.mult)
         fm = B("tf")[:, 160:224]; fh = B("tf")[:, 224:256]
         tt(["FCP", "mk"], n_("fm"), fm, T.FCP[:, 0:64], T.kf[:, 64:128], A.mult)
-        tt([n_("J2"), "roff"], n_("jb"), tf(t, 3), tf(t, 8), roff, A.max)
-        tt([n_("fm")], n_("fh"), fh, B("tf")[:, 160:224:2], B("tf")[:, 161:224:2], A.add)
-        ts([n_("J")], n_("J1"), tf(t, 2), tf(t, 0), 1.0 / 256, A.mult)
-        tt([n_("fh")], n_("fi"), ti(t, 6), B("tf")[:, 224:256:2], B("tf")[:, 225:256:2], A.add)
+        if t < 2:
+            cp(["FCP"], n_("a1"), ci(4 + t), T.FCP[:, 64:65])
         cp([n_("jb")], n_("up"), tu(t, 7), tf(t, 3))
+        tt([n_("fm")], n_("fh"), fh, B("tf")[:, 160:224:2], B("tf")[:, 161:224:2], A.add)
+        if t < 2:
+            ts([n_("a1")], n_("a2"), ci(6 + t), ci(4 + t), 65535, A.bitwise_and)
+        tt([n_("fh")], n_("fi"), ti(t, 6), B("tf")[:, 224:256:2], B("tf")[:, 225:256:2], A.add)
+        if t < 2:
+            ts([n_("a2")], n_("a3"), nb[t + 1], ci(6 + t), -1.0, A.mult)
         fi = ti(t, 6); FI = [n_("fi")]
         at = 12 if t < 2 else 0
 
@@ -466,13 +491,12 @@ def rank_program(g, core, T, topo):
                 lambda: tt([n_("fb"), n_("eb")], n_("e1"), tf(t, 4), ti(t, 7), ti(t, 2), A.subtract),
                 lambda: tt([n_("e1"), n_("J1")], n_("e2"), tf(t, 5), tf(t, 4), tf(t, 2), A.mult),
                 lambda: tt([n_("e2"), n_("eb")], en, eo, tf(t, 5), ti(t, 2), A.add)]
-        if t < 2:
-            fill += [lambda: cp(["AAP"], n_("a1"), ci(4 + t), T.AAP[:, 0:1]),
-                     lambda: ts([n_("a1")], n_("a2"), ci(6 + t), ci(4 + t), 65535, A.bitwise_and),
-                     lambda: cp([n_("a2")], "nb%d" % (t + 1), nb[t + 1], ci(6 + t)),
-                     lambda: act(["nb%d" % (t + 1), "TH0"], "TH%d" % (t + 1), T["TH%d" % (t + 1)][:], T.TH0[:], F.Identity, nb[t + 1])]
-        else:
-            fill += turn_steps(["en2"], "ye2", 3, tf(t, 9), T.yes[:, 0::2])
+        if t == 0:
+            fill += [lambda: cp(["ew2"], "eu2", tu(2, 1), ti(2, 0)),
+                     lambda: ts(["ew2"], "ea2", ti(2, 1), ti(2, 0), 1.0, A.add),
+                     lambda: ts(["ea2"], "eb2", ti(2, 2), ti(2, 1), 2047, A.bitwise_and)]
+        if t == 2:
+            fill += turn_steps([en], "ye2", 3, tf(t, 9), T.yes[:, 0::2])
             fill.append(lambda: dma("s", "oe", ["ye1", "ye2"], [], T.ye[:], T.yes[:]))
 
         def more(n=1):
@@ -483,42 +507,44 @@ def rank_program(g, core, T, topo):
         else:
             ts(FI, n_("h"), ti(t, 8), fi, 1, A.arith_shift_right, 2047, A.bitwise_and)
         ts(FI, n_("s"), ti(t, 9), fi, at, A.arith_shift_right, 1, A.bitwise_and)
+        if t < 2:
+            ts([n_("a3"), "oneb", "ka%d" % t if t else "oneb"], "ar%d" % (t + 1), T.ar[0:1, :], T.oneb[0:1, 0:128], T.cf[0:1, 7 + t:8 + t], A.mult)
+        more()
         ts([n_("h")], n_("uc"), tu(t, 5), ti(t, 8), 1536.0 if t == 1 else 0.0, A.add)
         ts([n_("s")], n_("q1"), tf(t, 6), ti(t, 9), 256.0, A.mult)
+        more()
         cw = T.CT[:, CWIN[t][0]:CWIN[t][1]].indirect(tu(t, 5))
         lh = "LH%d" % (t >> 1)
-        if t < 2:
-            more(4)
         ts(CR + [n_("uc")], lh + "lo", LH[t][:, 0:256], cw, 4095, A.bitwise_and)
         tt([n_("q1"), "jc"], n_("q2"), tf(t, 7), tf(t, 6), jc, A.add)
+        more()
         ts(CR + [n_("uc")], lh + "hi", LH[t][:, 256:512], cw, 12, A.arith_shift_right)
         cp([n_("q2")], n_("uq"), tu(t, 6), tf(t, 7))
-        if t == 2:
-            turn_rejected()
-        else:
-            more()
-        tt([lh + "lo", lh + "hi", ckn[t], n_("uq")], n_("df"), B("df")[:], LH[t][:, 0:512].indirect(tu(t, 6)), ck[t], A.subtract)
         more()
-        tt([n_("r1"), n_("r2"), n_("rz"), n_("up"), n_("df")], n_("dm"), B("dm")[:], B("r1")[:, 0:560].indirect(tu(t, 7)), B("df")[:], A.mult)
-        more()
-        cout = [ck[2], T.ycs[:, 1::2], T.ycs[:, 0::2]][t]
-        tt([n_("dm"), ckn[t]], n_("cn"), cout, B("dm")[:], ck[t], A.add)
+        parts = ((0, 16),) if t < 2 else ((0, 8), (8, 16))
+        for step in range(3):
+            for c0, c1 in parts:
+                p = slice(16 * c0, 16 * c1); n = "%d_%d" % (t, c0)
+                was = [T.LHa[:, 512:1024:2], T.LHa[:, 513:1024:2], T.cn0[:, p]][t]
+                if step == 0:
+                    tt([lh + "lo", lh + "hi", ckn[t], n_("uq")], "df" + n, B("df")[:, p], LH[t][:, 0:512].indirect(B("tu")[:, 96 + c0:96 + c1]), was, A.subtract)
+                elif step == 1:
+                    tt(["r1", "r2", "rz", n_("up"), "df" + n], "dm" + n, B("dm")[:, p], T.r1[:, 0:560].indirect(B("tu")[:, 112 + c0:112 + c1]), B("df")[:, p], A.mult)
+                elif t < 2:
+                    tt(["dm" + n, "FCP", "cas"], n_("cn"), [ck[2], T.ycs[:, 1::2]][t], B("dm")[:], [T.FCP[:, 256:512], ck[1]][t], A.add)
+                else:
+                    tt(["dm" + n, "XP"], "cn" + n, T.ycs[:, 32 * c0:32 * c1:2], B("dm")[:, p], T.XP[:, p], A.add)
+                    dma("y", "oc%d" % (c0 // 8), ["cn1", "cn" + n], [], T.yc[:, 32 * c0:32 * c1], T.ycs[:, 32 * c0:32 * c1])
+            more(2 if t == 2 else 1)
         if t == 0:
-            more(9)
-            cp(["ew2"], "eu2", tu(2, 1), ti(2, 0))
-            pack(1, ["cn0"], T.LHb[:, 512:768:2], T.LHb[:, 513:768:2])
+            pack(1, ["cn0"], T.cn0[:, 0::2], T.cn0[:, 1::2])
             send_c(1)
-            ts(["ew2"], "ea2", ti(2, 1), ti(2, 0), 1.0, A.add)
             ts(["rol", "eu2"], "f42", T.f42[:], rol.indirect(tu(2, 1)), 4096.0, A.mult)
-            ts(["ea2"], "eb2", ti(2, 2), ti(2, 1), 2047, A.bitwise_and)
         elif t == 1:
-            more(9)
             pack(2, ["cn1"], T.ycs[:, 1::4], T.ycs[:, 3::4])
             send_c(2)
             turn(["en1"], "ye1", 2, tf(1, 9), T.yes[:, 1::2])
-        else:
-            dma("y", "oc", ["cn1", "cn2"], [], T.yc[:], T.ycs[:])
-            more(9)
+        more(9)
 
     wait("g", [("loc", loc[0])])
-    wait("y", [("ox", 16), ("oc", 16), ("oe", 16)] + list(cnt.items()))
+    wait("y", [("ox", 16), ("oc0", 16), ("oc1", 16), ("oe", 16)] + list(cnt.items()))

@@ -5,14 +5,15 @@ N = 8
 SIM = 128
 C1 = 12582912.0
 XOFF = (0, 4096, 6144); XW = (512, 256, 256)
-COFF = (0, 2048, 3072); CW = (256, 128, 128)
+COFF = (0, 2048, 4096); CW = (256, 256, 256)
 XWIN = ((0, 4096), (0, 6144), (4096, 8192))
-CWIN = ((0, 2048), (0, 3072), (2048, 4096))
+CWIN = ((0, 2048), (0, 4096), (2048, 6144))
 EARLY = (3, 3)
+BIG = 8192.0
 PIECES = ((0, 2, "B"), (2, 4, "B"), (4, 6, "B"), (6, 7, "B"), (7, 8, "B"), (8, 10, "A"), (10, 12, "A"), (12, 14, "A"), (14, 15, "A"), (15, 16, "A"))
 
 SCRATCH = {
-    "XT": ("sbuf", [128, 8192], "bfloat16"), "CT": ("sbuf", [128, 4096], "int32"),
+    "XT": ("sbuf", [128, 8192], "bfloat16"), "CT": ("sbuf", [128, 6144], "int32"),
     "frs": ("sbuf", [128, 4096], "bfloat16"), "rls": ("sbuf", [128, 2048], "int32"),
     "LHa": ("sbuf", [128, 1024], "int32"), "LHb": ("sbuf", [128, 512], "int32"), "cn0": ("sbuf", [128, 256], "float32"),
     "rj": ("sbuf", [128, 288], "bfloat16"), "r1": ("sbuf", [128, 560], "bfloat16"), "TH": ("sbuf", [128, 256], "float32"),
@@ -82,14 +83,14 @@ def rank_program(g, core, T, topo):
         p = place[a][0]
         return [h for h in range(SIM) if topo.mates(topo.chip(h), chips[a]) and topo.may_write(h, p) and (topo.die(h) == topo.die(p)) == (j == 0)]
 
-    def across(a, j):
-        return [h for h in topo.cores_of(place[a][0]) if topo.die(h) != topo.die(place[a][0])][j]
+    def across(a, j, k=0):
+        return [h for h in topo.cores_of(place[a][0]) if topo.die(h) != topo.die(place[a][0])][2 * k + j]
 
     def high_of(c, a):
         return [e for e in topo.engines(c, aid[a][0]) if e not in topo.engines(c, place[order(a)[2]][0])]
 
     def via_c(b, a, j):
-        return aid[a][j] if topo.same_plane(chips[a], chips[b]) else beside(a, j)[1]
+        return beside(a, j)[1] if b == order(a)[0] else aid[a][j]
 
     def dst(c):
         rid, pid, _ = topo.addr(c)
@@ -107,17 +108,20 @@ def rank_program(g, core, T, topo):
         for e in range(3):
             for a in range(4):
                 for j in range(2):
-                    if across(a, j) == core:
-                        ap = xs(e, T.rank_of(place[a][j])); to = place[order(a)[2]]
-                        g.wait_ge(T.sem["xa%d_%d" % (e, a)], len(high_of(place[a][j], a)))
-                        two = ((to, topo.engines(core, to[0]), "xr%d" % e), ([place[a][1 - j]], high_of(core, a), "xa%d_%d" % (e, a)))
-                        g.remote_dma_fused([RemoteDMATransfer(dst_ids=[dst(c) for c in cs_], dma_engine_mask=bits(eng), remote_sem=T.sem[sem],
-                                                              srcs=[ap], dsts=[ap] * len(cs_)) for cs_, eng, sem in two], local_sem=T.sem.loc)
-                        sent += sum(len(x[1]) for x in two)
+                    for k, blk, got, far_sem, near_sem in ((0, xs, "xa%d_%d" % (e, a), "xr%d" % e, "xa%d_%d" % (e, a)), (1, cs, "ha%d_%d" % (e, a), "ca%d" % e, "ca%d" % e)):
+                        if across(a, j, k) == core:
+                            ap = blk(e, T.rank_of(place[a][j])); to = place[order(a)[2]]
+                            g.wait_ge(T.sem[got], len(high_of(place[a][j], a)))
+                            two = ((to, topo.engines(core, to[0]), far_sem), ([place[a][1 - j]], high_of(core, a), near_sem))
+                            trs = [RemoteDMATransfer(dst_ids=[dst(c) for c in cs_], dma_engine_mask=bits(eng), remote_sem=T.sem[sem],
+                                                     srcs=[ap], dsts=[ap] * len(cs_)) for cs_, eng, sem in two]
+                            for part in ([trs] if e else [trs[:1], trs[1:]]):
+                                g.remote_dma_fused(part, local_sem=T.sem.loc)
+                            sent += sum(len(x[1]) for x in two)
                     b = order(a)[0]
                     jobs = [(beside(a, j)[0], "xa%d_%d" % (e, b), len(topo.engines(place[b][j], beside(a, j)[0])), xs(e, T.rank_of(place[b][j])), "xr", place[a])]
                     jobs += [(via_c(b, a, j), "ha%d_%d" % (e, b), len(topo.engines(place[b][j], via_c(b, a, j))), cs(e, T.rank_of(place[b][j])), "ca", place[a])
-                             for b in order(a)]
+                             for b in order(a)[:2]]
                     for via, got, n, ap, sem, to in jobs:
                         if via == core:
                             eng = topo.engines(core, to[0])
@@ -207,8 +211,9 @@ def rank_program(g, core, T, topo):
     def send_x(e, meanwhile=None):
         deps("g", ["x%d" % e], [])
         ap = xs(e, rank)
-        g.remote_dma_fused([tr([beside(far[0], j)[0], place[far[1]][j]], off, "xa%d_%d" % (e, a), ap),
-                            tr([across(a, j)], high, "xa%d_%d" % (e, a), ap)], local_sem=T.sem.loc)
+        trs = [tr([beside(far[0], j)[0], place[far[1]][j]], off, "xa%d_%d" % (e, a), ap), tr([across(a, j)], high, "xa%d_%d" % (e, a), ap)]
+        for part in ([trs] if e else [trs[:1], trs[1:]]):
+            g.remote_dma_fused(part, local_sem=T.sem.loc)
         if meanwhile:
             meanwhile()
         toks = [("xa%d_%d" % (e, far[1]), len(off))]
@@ -219,9 +224,9 @@ def rank_program(g, core, T, topo):
     def send_c(e):
         deps("g", ["c%d" % e], [])
         ap = cs(e, rank)
-        g.remote_dma_fused([tr([via_c(a, b, j) for b in far], off, "ha%d_%d" % (e, a), ap), tr([mate], high, "ca%d" % e, ap)], local_sem=T.sem.loc)
-        n = sum(len(topo.engines(via_c(b, a, i), core)) for b in far for i in range(2))
-        wr["C%d" % e] = [("ca%d" % e, len(high) + n)] + wr["c%d" % e]
+        g.remote_dma_fused([tr([via_c(a, b, j) for b in far[:2]], off, "ha%d_%d" % (e, a), ap), tr([across(a, j, 1)], high, "ha%d_%d" % (e, a), ap)], local_sem=T.sem.loc)
+        n = sum(len(topo.engines(via_c(b, a, i), core)) for b in far[:2] for i in range(2))
+        wr["C%d" % e] = [("ca%d" % e, len(high) + 2 * len(off) + n)] + wr["c%d" % e]
 
     cas = T.LHa[:, 512:1024]
     dma("y", "lx", [], ["x0"], xs(0, rank), T.x0[:])
@@ -297,26 +302,31 @@ def rank_program(g, core, T, topo):
     ti = lambda t, i: col(T["ti%d" % t], i)
     tf = lambda t, i: col(T["tf%d" % t], i)
     tu = lambda t, i: col(T["tu%d" % t], i)
-    ck = [T.LHa[:, 512:1024:2], T.LHa[:, 513:1024:2], T.cn0[:]]
-    ckn = ["cas", "cas", "cn0"]
+    ck = [T.LHa[:, 512:1024:2], T.LHa[:, 513:1024:2], cs(1, rank)]
+    ckn = ["cas", "cas", "c1"]
     LH = [T.LHa, T.LHa, T.LHb]
     nb = [cf(6), cf(7), cf(8)]
     rol = T.rls[:, 0:2048]
 
     def scene_next(t):
-        cp(["ew%d" % t], "eu%d" % t, tu(t, 1), ti(t, 0))
-        ts(["ew%d" % t], "ea%d" % t, ti(t, 1), ti(t, 0), 1.0, A.add)
-        ts(["ea%d" % t], "eb%d" % t, ti(t, 2), ti(t, 1), 2047, A.bitwise_and)
+        return [lambda: cp(["ew%d" % t], "eu%d" % t, tu(t, 1), ti(t, 0)),
+                lambda: ts(["ew%d" % t], "ea%d" % t, ti(t, 1), ti(t, 0), 1.0, A.add),
+                lambda: ts(["ea%d" % t], "eb%d" % t, ti(t, 2), ti(t, 1), 2047, A.bitwise_and)]
 
-    def x_offsets(t):
+    def x_offsets(t, between):
         ts([ckn[t]], "wa", T.wa[:], ck[t], 4097.0, A.mult, -4096.0 if t == 1 else 0.0, A.add)
-        ts(["wa"], "wb", T.wb[:], T.wa[:], 1, A.arith_shift_right, 4095, A.bitwise_and)
+        between[0]()
         if t == 1:
-            ts(["wb"], "wc", T.wc[:], T.wb[:], 1.0, A.add, 2048.0, A.min)
-            tt(["wb", "wc"], "wa", T.wa[:], T.wb[:], T.wc[:], A.add)
+            ts(["wa"], "wb", T.wb[:], T.wa[:], 8191, A.bitwise_and)
+            between[1]()
+            ts(["wb"], "XP", T.XP[:, 0:256], T.wb[:], 0.5, A.mult, 2048.0, A.add)
+            between[2]()
+            tt(["wb", "XP"], "wa", T.wa[:], T.wb[:], T.XP[:, 0:256], A.min)
+            ts(["wb"], "f41", T.f41[:], T.wb[:], -4096.0, A.add, 4096.0, A.mult)
             cp(["wa", "perm"], "xo1", T.xo1[:], T.wa[:, 0:256].indirect(perm))
-            ts(["wa"], "f41", T.f41[:], T.wa[:], -3072.0, A.add, 4096.0, A.mult)
         else:
+            ts(["wa"], "wb", T.wb[:], T.wa[:], 1, A.arith_shift_right, 4095, A.bitwise_and)
+            between[1]()
             cp(["wb", "perm"], "xo2", T.xo2[:], T.wb[:, 0:256].indirect(perm))
 
     def pack(e, R, lo, hi):
@@ -341,8 +351,8 @@ def rank_program(g, core, T, topo):
     turns = [turn_steps(["sc"], "ew%d" % t, t, T.scs[:, t::2], ti(t, 0)) for t in (0, 1)]
     for f0, f1 in zip(*turns):
         f0(); f1()
-    for t in (0, 1):
-        scene_next(t)
+    for f0, f1 in zip(scene_next(0), scene_next(1)):
+        f0(); f1()
     cp(["cas", "perm20"], "xo0", T.xo0[:], cas.indirect(perm2[0]))
     pack(0, ["cas"], ck[0], ck[1])
     send_c(0)
@@ -354,18 +364,14 @@ def rank_program(g, core, T, topo):
     ts(["K2", "m1"], "K2", T.tin[:, 96:112], T.tin[:, 96:112], cf(5), A.not_equal, 272.0, A.mult)
     ts(["K4", "rh"], "mk", T.kf[:, 64:128], T.tout[:, 64:128], cf(11), A.is_equal)
     tt(["K2", "jc"], "roff", roff, T.tin[:, 96:112], jc, A.add)
-    ts(["cas"], "f40", T.f40[:], ck[0], 4096.0, A.mult)
-    x_offsets(1)
-    for t in (0, 1):
-        cp(["rol", "er%d" % t], "fo%d" % t, T["fo%d" % t][:], rol.indirect(tu(t, 0)))
+    frame_list = lambda t: cp(["rol", "er%d" % t], "fo%d" % t, T["fo%d" % t][:], rol.indirect(tu(t, 0)))
 
     def pair(t):
         if t < 2:
             tt(["rol", "eu%d" % t, "f4%d" % t], "fc%d" % t, T["fc%d" % t][:], rol.indirect(tu(t, 1)), T["f4%d" % t][:], A.add)
         else:
             tt(["f42", "wb"], "fc2", T.fc2[:], T.f42[:], T.wb[:], A.add)
-    pair(0)
-    cp(["cas"], "FCP", T.FCP[:, 256:512], ck[0])
+    x_offsets(1, [lambda: (ts(["cas"], "f40", T.f40[:], ck[0], 4096.0, A.mult), frame_list(0)), lambda: frame_list(1), lambda: pair(0)])
     frames(0, "s", 0, 4); frames(0, "v", 8, 16); frames(0, "s", 4, 8)
 
     for t in range(3):
@@ -413,12 +419,10 @@ def rank_program(g, core, T, topo):
             ts(["f42", "perm"], "fo2", T.fo2[:], T.f42[:, 0:256].indirect(perm), 1.0 / 4096, A.mult)
         else:
             pair(2)
-        if t == 1:
-            own(2)
         if t < 2:
             frames(t + 1, "s", 0, EARLY[t])
         else:
-            act(["cn0"], "XP", T.XP[:, 0:256], ck[2], F.Copy)
+            mms(["Id", "Idn", "x1"], ["YP0", "YP1"], [(T.YP0[:, 0:256], T.Id[:], mine[2], True, False), (T.YP1[:, 0:256], T.Idn[:], mine[2], True, False)])
             act(["x2"], "yxo", T.yxs[:, 1::2], xs(2, rank), F.Copy)
         op("v", [key, "rst"], [n_("sn")], lambda: V.tensor_tensor_scan(B("sn")[:], T.rst[:], KEY[:, 0:256], 0.0, A.add, A.min))
         tt([key, "TH"], "rj", T.rj[:, 16:272], KEY[:, 0:256], T.TH[:], A.is_gt)
@@ -448,15 +452,18 @@ def rank_program(g, core, T, topo):
         ts([n_("kk"), "r256"], n_("uo"), tu(t, 2), ti(t, 4), cf(2), A.add)
         tt([n_("J"), "jc"], n_("sf"), tf(t, 1), tf(t, 0), jc, A.add)
         yb = B("yk")[:, 0:4096].indirect(tu(t, 2))
-        tt(yk + [n_("uo"), minen[t]], n_("sm"), B("sm")[:], yb, mine[t], A.add)
-        cp([n_("sf")], n_("us"), tu(t, 4), tf(t, 1))
-        tt(yk + [n_("uo"), n_("xn")], n_("Wd"), B("W")[:, 0:256], yb, B("xn")[:], A.subtract)
-        act([n_("sm")], n_("Wa"), B("W")[:, 256:512], B("sm")[:], F.Identity, C1, 0.4995)
         xout = T.yxs[:, 0::2] if t == 2 else xs(t + 1, rank)
-        act([n_("Wd"), n_("Wa"), n_("us")], "x%d" % (t + 1), xout, B("W")[:, 0:512].indirect(tu(t, 4)), F.Abs, -C1)
+        choose = lambda: act([n_("Wd"), n_("Wa"), n_("us")], "x%d" % (t + 1), xout, B("W")[:, 0:512].indirect(tu(t, 4)), F.Abs, -C1)
         if t == 2:
-            dma("y", "ox", ["x3", "yxo"], [], T.yx[:], T.yxs[:])
+            act(yk + ["uo2"], "yb", T.rr[:], yb, F.Copy)
+            mms(["Id", "yb"], ["YP0", "YP1"], [(T.YP0[:, 0:256], T.Id[:], T.rr[:], False, True), (T.YP1[:, 0:256], T.Id[:], T.rr[:], False, True)])
+            cp([n_("sf")], n_("us"), tu(t, 4), tf(t, 1))
         else:
+            tt(yk + [n_("uo"), minen[t]], n_("sm"), B("sm")[:], yb, mine[t], A.add)
+            cp([n_("sf")], n_("us"), tu(t, 4), tf(t, 1))
+            tt(yk + [n_("uo"), n_("xn")], n_("Wd"), B("W")[:, 0:256], yb, B("xn")[:], A.subtract)
+            act([n_("sm")], n_("Wa"), B("W")[:, 256:512], B("sm")[:], F.Identity, C1, 0.4995)
+            choose()
             send_x(t + 1)
             kb()
             op("v", [n_("J")], [n_("jr")], lambda: V.tensor_reduce(cf(9 + t), tf(t, 0), AxisListType.X, A.add))
@@ -468,15 +475,22 @@ def rank_program(g, core, T, topo):
             for r0, r1 in ((EARLY[t], 6), (6, 10), (10, 16)):
                 frames(t + 1, "s", r0, r1)
         turn_rejected()
-        if t == 1:
-            x_offsets(2)
-        tt([n_("J2"), "roff"], n_("jb"), tf(t, 3), tf(t, 8), roff, A.max)
-        ts([n_("J")], n_("J1"), tf(t, 2), tf(t, 0), 1.0 / 256, A.mult)
+        small = [lambda: tt([n_("J2"), "roff"], n_("jb"), tf(t, 3), tf(t, 8), roff, A.max),
+                 lambda: ts([n_("J")], n_("J1"), tf(t, 2), tf(t, 0), 1.0 / 256, A.mult)]
+        small[0](); small[1]()
+        if t < 2:
+            cp(["cas"], "XP", T.XP[:, 256:512], ck[t])
         fm = B("tf")[:, 160:224]; fh = B("tf")[:, 224:256]
         tt(["FCP", "mk"], n_("fm"), fm, T.FCP[:, 0:64], T.kf[:, 64:128], A.mult)
         if t < 2:
             cp(["FCP"], n_("a1"), ci(4 + t), T.FCP[:, 64:65])
         cp([n_("jb")], n_("up"), tu(t, 7), tf(t, 3))
+        if t == 2:
+            act(["r1", "r2", "rz", "up2"], "pen", T.dm2[:], T.r1[:, 0:560].indirect(tu(t, 7)), F.Identity, -BIG, BIG)
+            act(["YP0"], "Wa2", T.W2[:, 256:512], T.YP0[:, 0:256], F.Identity, C1, 0.4995)
+            act(["YP1"], "Wd2", T.W2[:, 0:256], T.YP1[:, 0:256], F.Identity, C1)
+            choose()
+            dma("y", "ox", ["x3", "yxo"], [], T.yx[:], T.yxs[:])
         tt([n_("fm")], n_("fh"), fh, B("tf")[:, 160:224:2], B("tf")[:, 161:224:2], A.add)
         if t < 2:
             ts([n_("a1")], n_("a2"), ci(6 + t), ci(4 + t), 65535, A.bitwise_and)
@@ -496,7 +510,9 @@ def rank_program(g, core, T, topo):
                      lambda: ts(["ew2"], "ea2", ti(2, 1), ti(2, 0), 1.0, A.add),
                      lambda: ts(["ea2"], "eb2", ti(2, 2), ti(2, 1), 2047, A.bitwise_and)]
         if t == 2:
-            fill += turn_steps([en], "ye2", 3, tf(t, 9), T.yes[:, 0::2])
+            fill += [lambda: act([en, "m0"], "ta3", T.tin[:, 96:112], tf(t, 9), F.Copy, 0.0, cf(4)),
+                     lambda: act([en, "m1"], "tb3", T.tin[:, 112:128], tf(t, 9), F.Copy, 0.0, cf(5))]
+            fill += turn_steps([en], "ye2", 3, tf(t, 9), T.yes[:, 0::2])[2:]
             fill.append(lambda: dma("s", "oe", ["ye1", "ye2"], [], T.ye[:], T.yes[:]))
 
         def more(n=1):
@@ -505,45 +521,49 @@ def rank_program(g, core, T, topo):
         if t < 2:
             ts(FI, n_("h"), ti(t, 8), fi, 13, A.arith_shift_right)
         else:
-            ts(FI, n_("h"), ti(t, 8), fi, 1, A.arith_shift_right, 2047, A.bitwise_and)
-        ts(FI, n_("s"), ti(t, 9), fi, at, A.arith_shift_right, 1, A.bitwise_and)
+            ts(FI, n_("h"), ti(t, 8), fi, 4095, A.bitwise_and)
         if t < 2:
+            ts(FI, n_("s"), ti(t, 9), fi, at, A.arith_shift_right, 1, A.bitwise_and)
             ts([n_("a3"), "oneb", "ka%d" % t if t else "oneb"], "ar%d" % (t + 1), T.ar[0:1, :], T.oneb[0:1, 0:128], T.cf[0:1, 7 + t:8 + t], A.mult)
         more()
-        ts([n_("h")], n_("uc"), tu(t, 5), ti(t, 8), 1536.0 if t == 1 else 0.0, A.add)
-        ts([n_("s")], n_("q1"), tf(t, 6), ti(t, 9), 256.0, A.mult)
-        more()
-        cw = T.CT[:, CWIN[t][0]:CWIN[t][1]].indirect(tu(t, 5))
-        lh = "LH%d" % (t >> 1)
-        ts(CR + [n_("uc")], lh + "lo", LH[t][:, 0:256], cw, 4095, A.bitwise_and)
-        tt([n_("q1"), "jc"], n_("q2"), tf(t, 7), tf(t, 6), jc, A.add)
-        more()
-        ts(CR + [n_("uc")], lh + "hi", LH[t][:, 256:512], cw, 12, A.arith_shift_right)
-        cp([n_("q2")], n_("uq"), tu(t, 6), tf(t, 7))
-        more()
-        parts = ((0, 16),) if t < 2 else ((0, 8), (8, 16))
-        for step in range(3):
-            for c0, c1 in parts:
-                p = slice(16 * c0, 16 * c1); n = "%d_%d" % (t, c0)
-                was = [T.LHa[:, 512:1024:2], T.LHa[:, 513:1024:2], T.cn0[:, p]][t]
-                if step == 0:
-                    tt([lh + "lo", lh + "hi", ckn[t], n_("uq")], "df" + n, B("df")[:, p], LH[t][:, 0:512].indirect(B("tu")[:, 96 + c0:96 + c1]), was, A.subtract)
-                elif step == 1:
-                    tt(["r1", "r2", "rz", n_("up"), "df" + n], "dm" + n, B("dm")[:, p], T.r1[:, 0:560].indirect(B("tu")[:, 112 + c0:112 + c1]), B("df")[:, p], A.mult)
-                elif t < 2:
-                    tt(["dm" + n, "FCP", "cas"], n_("cn"), [ck[2], T.ycs[:, 1::2]][t], B("dm")[:], [T.FCP[:, 256:512], ck[1]][t], A.add)
-                else:
-                    tt(["dm" + n, "XP"], "cn" + n, T.ycs[:, 32 * c0:32 * c1:2], B("dm")[:, p], T.XP[:, p], A.add)
-                    dma("y", "oc%d" % (c0 // 8), ["cn1", "cn" + n], [], T.yc[:, 32 * c0:32 * c1], T.ycs[:, 32 * c0:32 * c1])
-            more(2 if t == 2 else 1)
+        ts([n_("h")], n_("uc"), tu(t, 5), ti(t, 8), 2048.0 if t == 1 else 0.0, A.add)
+        cwin = T.CT[:, CWIN[t][0]:CWIN[t][1]]
+        if t < 2:
+            ts([n_("s")], n_("q1"), tf(t, 6), ti(t, 9), 256.0, A.mult)
+            more()
+            ts(CR + [n_("uc")], "lo", T.LHa[:, 0:256], cwin.indirect(tu(t, 5)), 4095, A.bitwise_and)
+            tt([n_("q1"), "jc"], n_("q2"), tf(t, 7), tf(t, 6), jc, A.add)
+            more()
+            ts(CR + [n_("uc")], "hi", T.LHa[:, 256:512], cwin.indirect(tu(t, 5)), 12, A.arith_shift_right)
+            cp([n_("q2")], n_("uq"), tu(t, 6), tf(t, 7))
+            more()
+            tt(["lo", "hi", ckn[t], n_("uq")], n_("df"), B("df")[:], T.LHa[:, 0:512].indirect(tu(t, 6)), ck[t], A.subtract)
+            more()
+            tt(["r1", "r2", "rz", n_("up"), n_("df")], n_("dm"), B("dm")[:], T.r1[:, 0:560].indirect(tu(t, 7)), B("df")[:], A.mult)
+            more()
+            tt([n_("dm"), "XP"], "c%d" % (t + 1), cs(t + 1, rank), B("dm")[:], T.XP[:, 256:512], A.add)
+            send_c(t + 1)
+            more()
+        else:
+            more()
+            tt(["XP", "pen"], "XP", T.XP[:, 256:512], T.XP[:, 0:256], T.dm2[:], A.subtract)
+            more()
+            for h in range(2):
+                tt(CR + ["pen", "uc2"], "df2_%d" % h, T.df2[:, 128 * h:128 * h + 128], cwin.indirect(T.tu2[:, 80 + 8 * h:88 + 8 * h]),
+                   T.dm2[:, 128 * h:128 * h + 128], A.add)
+                if h == 0:
+                    more(3)
+            for h in range(2):
+                tt(["df2_%d" % h, "XP"], "cn2_%d" % h, T.ycs[:, 256 * h:256 * h + 256:2], T.df2[:, 128 * h:128 * h + 128], T.XP[:, 256 + 128 * h:384 + 128 * h], A.max)
+                dma("y", "oc%d" % h, ["cn1", "cn2_%d" % h], [], T.yc[:, 256 * h:256 * h + 256], T.ycs[:, 256 * h:256 * h + 256])
         if t == 0:
-            pack(1, ["cn0"], T.cn0[:, 0::2], T.cn0[:, 1::2])
-            send_c(1)
             ts(["rol", "eu2"], "f42", T.f42[:], rol.indirect(tu(2, 1)), 4096.0, A.mult)
+            ts(["c1"], "XP", T.XP[:, 0:256], ck[2], -BIG, A.add)
         elif t == 1:
-            pack(2, ["cn1"], T.ycs[:, 1::4], T.ycs[:, 3::4])
-            send_c(2)
-            turn(["en1"], "ye1", 2, tf(1, 9), T.yes[:, 1::2])
+            ye1 = turn_steps(["en1"], "ye1", 2, tf(1, 9), T.yes[:, 1::2])
+            ye1[0](); ye1[1]()
+            x_offsets(2, ye1[2:])
+            cp(["c2"], "cn1", T.ycs[:, 1::2], cs(2, rank))
         more(9)
 
     wait("g", [("loc", loc[0])])

from concourse.bass import DstId, RemoteDMATransfer
from concourse.mybir import AluOpType as A, AxisListType, ActivationFunctionType as F

N = 8
SIM = 128
C1 = 12582912.0
XOFF = (0, 4096, 6144); XW = (512, 256, 256)
COFF = (0, 2048, 4096); CW = (256, 256, 256)
XWIN = ((0, 4096), (0, 6144), (4096, 8192))
CWIN = ((0, 2048), (0, 4096), (2048, 6144))
EARLY = (3, 3)
BIG = 8192.0
PIECES = ((0, 2, "B"), (2, 4, "B"), (4, 6, "B"), (6, 7, "B"), (7, 8, "B"), (8, 10, "A"), (10, 12, "A"), (12, 14, "A"), (14, 15, "A"), (15, 16, "A"))

SCRATCH = {
    "XT": ("sbuf", [128, 8192], "bfloat16"), "CT": ("sbuf", [128, 6144], "int32"),
    "frs": ("sbuf", [128, 4096], "bfloat16"), "rls": ("sbuf", [128, 2048], "int32"),
    "LHa": ("sbuf", [128, 1024], "int32"), "LHb": ("sbuf", [128, 512], "int32"), "cn0": ("sbuf", [128, 256], "float32"),
    "rj": ("sbuf", [128, 288], "bfloat16"), "r1": ("sbuf", [128, 560], "bfloat16"), "TH": ("sbuf", [128, 256], "float32"),
    "ar": ("sbuf", [128, 128], "bfloat16"),
    "scs": ("sbuf", [128, 32], "int32"), "ths": ("sbuf", [128, 8], "int32"),
    "M": ("sbuf", [128, 256], "float32"), "Mb": ("sbuf", [128, 256], "bfloat16"),
    "Bb": ("sbuf", [128, 144], "bfloat16"), "Bf": ("sbuf", [128, 144], "float32"),
    "oneb": ("sbuf", [128, 256], "bfloat16"), "onef": ("sbuf", [128, 128], "float32"),
    "rst": ("sbuf", [128, 256], "float32"),
    "ci": ("sbuf", [128, 16], "int32"), "cf": ("sbuf", [128, 16], "float32"),
    "kf": ("sbuf", [128, 128], "float32"), "ku": ("sbuf", [128, 64], "uint16"),
    "tin": ("sbuf", [128, 128], "float32"), "tout": ("sbuf", [128, 128], "float32"),
    "yxs": ("sbuf", [128, 512], "bfloat16"), "ycs": ("sbuf", [128, 512], "float32"), "yes": ("sbuf", [128, 32], "float32"),
    "wa": ("sbuf", [128, 256], "int32"), "wb": ("sbuf", [128, 256], "int32"), "wc": ("sbuf", [128, 256], "int32"),
    "pk": ("sbuf", [128, 256], "int32"),
    "keep": ("sbuf", [128, 256], "bfloat16"), "Bo": ("sbuf", [128, 128], "float32"), "E": ("sbuf", [128, 256], "float32"),
    "Bn": ("sbuf", [128, 144], "bfloat16"), "B2": ("sbuf", [128, 144], "bfloat16"), "Id": ("sbuf", [128, 128], "bfloat16"),
    "Idn": ("sbuf", [128, 128], "bfloat16"),
    "KEY": ("psum", [128, 512], "float32"), "FCP": ("psum", [128, 512], "float32"), "XP": ("psum", [128, 512], "float32"),
    "rr": ("sbuf", [128, 256], "bfloat16"),
}
for _i in range(4):
    SCRATCH["YP%d" % _i] = ("psum", [128, 512], "float32")
for _t in range(3):
    for _n, _w, _d in (("yk", 4096, "bfloat16"), ("dd", 4096, "bfloat16"), ("ab", 4096, "bfloat16"),
                       ("xo", 256, "uint16"), ("fo", 256, "uint16"), ("f4", 256, "float32"), ("fc", 256, "float32"),
                       ("xn", 256, "float32"), ("sm", 256, "float32"), ("W", 512, "float32"),
                       ("sn", 256, "float32"), ("oh", 256, "float32"), ("nr", 256, "bfloat16"),
                       ("df", 256, "float32"), ("dm", 256, "float32"),
                       ("ti", 256, "int32"), ("tf", 256, "float32"), ("tu", 128, "uint16")):
        SCRATCH["%s%d" % (_n, _t)] = ("sbuf", [128, _w], _d)

SEMAPHORES = ["cv", "cs", "ct", "cg", "loc", "lx", "lsc", "lth", "lca", "lro", "lfr", "ox", "oc0", "oc1", "oe"]
for _e in range(3):
    SEMAPHORES += ["xa%d_%d" % (_e, _a) for _a in range(4)] + ["ha%d_%d" % (_e, _a) for _a in range(4)] + ["xp%d" % _e, "xr%d" % _e, "ca%d" % _e]


def bits(engines):
    m = 0
    for e in engines:
        m |= 1 << e
    return m


def distance_order():
    n = len(PIECES) // 2; out = []
    for i in range(n + 1):
        for step, p, sums in (("diff", n + i, None), ("pick", i, "less"), ("max", i - 1, "twice"), ("abs", n + i - 1, "sum")):
            if (i < n if step in ("diff", "pick") else i > 0):
                out += [(step, p, None)] + [(sums, p, r) for r in range(*PIECES[p][:2]) if sums]
    return out


def rank_program(g, core, T, topo):
    cores = list(T.cores)
    chips = []
    for c in cores:
        if topo.chip(c) not in chips:
            chips.append(topo.chip(c))
    place = [[c for c in cores if topo.chip(c) == ch] for ch in chips]
    aid = [[h for h in topo.cores_of(p[0]) if h not in cores and topo.die(h) == topo.die(p[0])][:2] for p in place]

    def order(a):
        return [a ^ s for s in sorted((1, 2, 3), key=lambda s: topo.same_plane(chips[a], chips[a ^ s]))]

    def beside(a, j):
        p = place[a][0]
        return [h for h in range(SIM) if topo.mates(topo.chip(h), chips[a]) and topo.may_write(h, p) and (topo.die(h) == topo.die(p)) == (j == 0)]

    def across(a, j, k=0):
        return [h for h in topo.cores_of(place[a][0]) if topo.die(h) != topo.die(place[a][0])][2 * k + j]

    def high_of(c, a):
        return [e for e in topo.engines(c, aid[a][0]) if e not in topo.engines(c, place[order(a)[2]][0])]

    def via_c(b, a, j):
        return beside(a, j)[1] if b == order(a)[0] else aid[a][j]

    def dst(c):
        rid, pid, _ = topo.addr(c)
        return DstId(rid=rid, pnc=pid)

    def xs(e, q):
        return T.XT[:, XOFF[e] + q * XW[e]:XOFF[e] + (q + 1) * XW[e]]

    def cs(e, q):
        return T.CT[:, COFF[e] + q * CW[e]:COFF[e] + (q + 1) * CW[e]]

    rank = T.rank_of(core)
    if rank is None:
        sent = 0
        for e in range(3):
            for a in range(4):
                for j in range(2):
                    for k, blk, got, far_sem, near_sem in ((0, xs, "xa%d_%d" % (e, a), "xr%d" % e, "xa%d_%d" % (e, a)), (1, cs, "ha%d_%d" % (e, a), "ca%d" % e, "ca%d" % e)):
                        if across(a, j, k) == core:
                            ap = blk(e, T.rank_of(place[a][j])); to = place[order(a)[2]]
                            g.wait_ge(T.sem[got], len(high_of(place[a][j], a)))
                            two = ((to, topo.engines(core, to[0]), far_sem), ([place[a][1 - j]], high_of(core, a), near_sem))
                            trs = [RemoteDMATransfer(dst_ids=[dst(c) for c in cs_], dma_engine_mask=bits(eng), remote_sem=T.sem[sem],
                                                     srcs=[ap], dsts=[ap] * len(cs_)) for cs_, eng, sem in two]
                            for part in ([trs] if e else [trs[:1], trs[1:]]):
                                g.remote_dma_fused(part, local_sem=T.sem.loc)
                            sent += sum(len(x[1]) for x in two)
                    b = order(a)[0]
                    jobs = [(beside(a, j)[0], "xa%d_%d" % (e, b), len(topo.engines(place[b][j], beside(a, j)[0])), xs(e, T.rank_of(place[b][j])), "xr", place[a])]
                    jobs += [(via_c(b, a, j), "ha%d_%d" % (e, b), len(topo.engines(place[b][j], via_c(b, a, j))), cs(e, T.rank_of(place[b][j])), "ca", place[a])
                             for b in order(a)[:2]]
                    for via, got, n, ap, sem, to in jobs:
                        if via == core:
                            eng = topo.engines(core, to[0])
                            g.wait_ge(T.sem[got], n)
                            g.remote_dma_fused([RemoteDMATransfer(dst_ids=[dst(c) for c in to], dma_engine_mask=bits(eng),
                                                                  remote_sem=T.sem["%s%d" % (sem, e)], srcs=[ap], dsts=[ap] * len(to))], local_sem=T.sem.loc)
                            sent += len(eng)
        if sent:
            g.wait_ge(T.sem.loc, sent)
        return

    a = chips.index(topo.chip(core)); j = place[a].index(core); mate = place[a][1 - j]
    far = order(a)
    off = topo.engines(core, place[far[0]][j]); on = topo.engines(core, mate); high = [e for e in on if e not in off]

    Q = {"v": g.vector, "s": g.scalar, "t": g.tensor, "y": g.sync, "g": g}
    CS = {"v": "cv", "s": "cs", "t": "ct", "g": "cg"}
    cnt = {"cv": 0, "cs": 0, "ct": 0, "cg": 0}
    seen = {q: {} for q in Q}
    wr = {}; rd = {}; loc = [0]

    def wait(q, toks):
        need = {}
        for s, v in toks:
            need[s] = max(need.get(s, 0), v)
        for s, v in need.items():
            if seen[q].get(s, 0) < v:
                Q[q].wait_ge(T.sem[s], v); seen[q][s] = v

    def deps(q, R, W):
        toks = []
        for n in R:
            toks += wr[n]
        for n in W:
            toks += wr.get(n, []) + rd.get(n, [])
        wait(q, toks)

    def done(tok, R, W):
        for n in R:
            rd.setdefault(n, []).append(tok)
        for n in W:
            wr[n] = [tok]; rd[n] = []

    def op(q, R, W, fn):
        deps(q, R, W)
        s = CS[q]; cnt[s] += 1
        fn().then_inc(T.sem[s], 1)
        done((s, cnt[s]), R, W)

    def dma(q, sem, R, W, out, in_):
        deps(q, R, W)
        Q[q].dma_start(out, in_).then_inc(T.sem[sem], 16)
        done((sem, 16), R, W)

    V = g.vector

    def ts(R, W, out, in0, s1, op0, s2=None, op1=None):
        if op1 is None:
            op("v", R, [W], lambda: V.tensor_scalar(out, in0, s1, None, op0))
        else:
            op("v", R, [W], lambda: V.tensor_scalar(out, in0, s1, s2, op0, op1))

    def tt(R, W, out, in0, in1, o):
        op("v", R, [W], lambda: V.tensor_tensor(out, in0, in1, o))

    def cp(R, W, out, in_):
        op("v", R, [W], lambda: V.tensor_copy(out, in_))

    def act(R, W, out, in_, f, bias=0.0, scale=1.0):
        op("s", R, [W], lambda: g.scalar.activation(out, in_, f, bias=bias, scale=scale))

    def mms(R, W, ms):
        deps("t", R, W)
        for m in ms[:-1]:
            g.tensor.matmul(*m)
        cnt["ct"] += 1
        g.tensor.matmul(*ms[-1]).then_inc(T.sem.ct, 1)
        done(("ct", cnt["ct"]), R, W)

    def col(b, i, n=16):
        return b[:, i * 16:i * 16 + n]

    def tr(cores_, eng, sem, ap):
        loc[0] += len(eng)
        return RemoteDMATransfer(dst_ids=[dst(c) for c in cores_], dma_engine_mask=bits(eng), remote_sem=T.sem[sem], srcs=[ap], dsts=[ap] * len(cores_))

    def send_x(e, meanwhile=None):
        deps("g", ["x%d" % e], [])
        ap = xs(e, rank)
        trs = [tr([beside(far[0], j)[0], place[far[1]][j]], off, "xa%d_%d" % (e, a), ap), tr([across(a, j)], high, "xa%d_%d" % (e, a), ap)]
        for part in ([trs] if e else [trs[:1], trs[1:]]):
            g.remote_dma_fused(part, local_sem=T.sem.loc)
        if meanwhile:
            meanwhile()
        toks = [("xa%d_%d" % (e, far[1]), len(off))]
        wait("g", toks)
        g.remote_dma_fused([tr([mate], on, "xp%d" % e, xs(e, T.rank_of(place[far[1]][j])))], local_sem=T.sem.loc)
        wr["X%d" % e] = toks + [("xa%d_%d" % (e, a), len(high)), ("xp%d" % e, len(on)), ("xr%d" % e, 4 * len(off))] + wr["x%d" % e]

    def send_c(e):
        deps("g", ["c%d" % e], [])
        ap = cs(e, rank)
        g.remote_dma_fused([tr([via_c(a, b, j) for b in far[:2]], off, "ha%d_%d" % (e, a), ap), tr([across(a, j, 1)], high, "ha%d_%d" % (e, a), ap)], local_sem=T.sem.loc)
        n = sum(len(topo.engines(via_c(b, a, i), core)) for b in far[:2] for i in range(2))
        wr["C%d" % e] = [("ca%d" % e, len(high) + 2 * len(off) + n)] + wr["c%d" % e]

    cas = T.LHa[:, 512:1024]
    dma("y", "lx", [], ["x0"], xs(0, rank), T.x0[:])
    dma("s", "lsc", [], ["sc"], T.scs[:], T.sc0[:])
    dma("s", "lth", [], ["th"], T.ths[:, 0:1], T.th[:])
    dma("y", "lca", [], ["cas"], cas, T.cas[:])
    dma("y", "lro", [], ["rol"], T.rls[:], T.rol[:])
    dma("y", "lfr", ["rol"], ["frm"], T.frs[:], T.frm[:])

    op("g", [], ["P"], lambda: g.iota(T.ci[:, 0:1], [[0, 1]], 0, 1))
    op("g", [], ["M"], lambda: g.iota(T.M[:], [[1, 256]], 0, 0, allow_small_or_imprecise_dtypes=True))

    def patterns():
        for n, out, pat, base in (("K16", T.E[:], [[0, 16], [1, 16]], 0), ("K2", T.tin[:, 96:112], [[0, 8], [1, 2]], 0),
                                  ("K4", T.tout[:, 64:128], [[0, 16], [1, 4]], 0), ("KL", T.sn0[:, 0:128], [[16, 8], [0, 16]], 15)):
            op("g", [], [n], lambda: g.iota(out, pat, base, 0, allow_small_or_imprecise_dtypes=True))
    send_x(0, patterns)
    act(["M"], "oneb", T.oneb[:], T.M[:], F.Identity, 1.0, 0.0)
    act(["M"], "onef", T.onef[:], T.M[:, 0:128], F.Identity, 1.0, 0.0)
    act(["M"], "Mb", T.Mb[:], T.M[:], F.Copy)
    op("v", [], ["rst"], lambda: V.memset(T.rst[:], 0.0))
    op("v", [], ["rz"], lambda: V.memset(T.r1[:, 544:560], 0.0))
    op("v", [], ["rj"], lambda: V.memset(T.rj[:], 0.0))
    op("v", [], ["rst"], lambda: V.memset(T.rst[:, 0::16], 33554432.0))
    ci = lambda i: T.ci[:, i:i + 1]
    cf = lambda i: T.cf[:, i:i + 1]
    ts(["P"], "ci1", ci(1), ci(0), 15, A.bitwise_and)
    ts(["P"], "ci2", ci(2), ci(0), 112, A.bitwise_and)
    ts(["P"], "ci3", ci(3), ci(0), 4, A.arith_shift_right, 1, A.bitwise_and)
    cp(["ci1"], "rf", cf(0), ci(1))
    ts(["ci1"], "r16", cf(1), ci(1), 16.0, A.mult)
    ts(["ci1"], "r256", cf(2), ci(1), 256.0, A.mult)
    ts(["ci2"], "tgt", cf(3), ci(2), 15.0, A.add)
    cp(["ci3"], "m1", cf(5), ci(3))
    ts(["ci3"], "m0", cf(4), ci(3), -1.0, A.mult, 1.0, A.add)
    M16 = T.M[:, 0:16]
    permf, jc, eye = col(T.kf, 0), col(T.kf, 1), col(T.kf, 2)
    perm = col(T.ku, 0); perm2 = [col(T.ku, 1), col(T.ku, 2)]
    ts(["M", "r16"], "permf", permf, M16, cf(1), A.add)
    ts(["M", "rf"], "jc", jc, M16, 16.0, A.mult, cf(0), A.add)
    ts(["M", "rf"], "eye", eye, M16, cf(0), A.is_equal)
    ts(["permf"], "perm20", perm2[0], permf, 2.0, A.mult)
    cp(["permf"], "perm", perm, permf)
    ts(["M", "tgt"], "Bb", T.Bb[:], T.M[:, 0:144], cf(3), A.is_equal, 256.0, A.mult)
    ts(["M", "tgt"], "wa", T.wa[:, 0:144], T.M[:, 0:144], cf(3), A.subtract, 12.0, A.add)
    ts(["ci1"], "ci8", ci(8), ci(1), 2, A.arith_shift_right)
    cp(["P"], "pf", cf(12), ci(0))
    ts(["wa"], "wb", T.wb[:, 0:144], T.wa[:, 0:144], 4083, A.bitwise_and)
    cp(["ci8"], "rh", cf(11), ci(8))
    ts(["M", "pf"], "Id", T.Id[:], T.M[:, 0:128], cf(12), A.is_equal)
    ts(["wb"], "Bf", T.Bf[:], T.wb[:, 0:144], 0.0, A.is_equal)
    act(["rst"], "keep", T.keep[:], T.rst[:], F.Identity, 1.0, -1.0 / 33554432.0)
    act(["Bb"], "Bn", T.Bn[:], T.Bb[:], F.Identity, 0.0, -1.0)
    act(["Bb"], "B2", T.B2[:], T.Bb[:], F.Identity, 0.0, 2.0)
    act(["Id"], "Idn", T.Idn[:], T.Id[:], F.Identity, 0.0, -1.0)
    roff = col(T.kf, 3)
    selb = lambda x: T.Bb[:, 15 - x:143 - x]
    seln = lambda x: T.Bn[:, 15 - x:143 - x]
    sel2 = lambda x: T.B2[:, 15 - x:143 - x]
    self_ = lambda x: T.Bf[:, 3 - x:131 - x]

    def turn_steps(R, W, blk, src, out):
        i0 = T.tin[:, 32 * blk:32 * blk + 32]; o0 = T.tout[:, 32 * blk:32 * blk + 32]
        return [lambda: ts(R + ["m0"], "ta%d" % blk, T.tin[:, 32 * blk:32 * blk + 16], src, cf(4), A.mult),
                lambda: ts(R + ["m1"], "tb%d" % blk, T.tin[:, 32 * blk + 16:32 * blk + 32], src, cf(5), A.mult),
                lambda: op("v", ["ta%d" % blk, "tb%d" % blk], ["to%d" % blk], lambda: V.transpose(o0, i0)),
                lambda: tt(["to%d" % blk], W, out, T.tout[:, 32 * blk:32 * blk + 16], T.tout[:, 32 * blk + 16:32 * blk + 32], A.add)]

    def turn(R, W, blk, src, out):
        for f in turn_steps(R, W, blk, src, out):
            f()

    ti = lambda t, i: col(T["ti%d" % t], i)
    tf = lambda t, i: col(T["tf%d" % t], i)
    tu = lambda t, i: col(T["tu%d" % t], i)
    ck = [T.LHa[:, 512:1024:2], T.LHa[:, 513:1024:2], cs(1, rank)]
    ckn = ["cas", "cas", "c1"]
    LH = [T.LHa, T.LHa, T.LHb]
    nb = [cf(6), cf(7), cf(8)]
    rol = T.rls[:, 0:2048]

    def scene_next(t):
        return [lambda: cp(["ew%d" % t], "eu%d" % t, tu(t, 1), ti(t, 0)),
                lambda: ts(["ew%d" % t], "ea%d" % t, ti(t, 1), ti(t, 0), 1.0, A.add),
                lambda: ts(["ea%d" % t], "eb%d" % t, ti(t, 2), ti(t, 1), 2047, A.bitwise_and)]

    def x_offsets(t, between):
        ts([ckn[t]], "wa", T.wa[:], ck[t], 4097.0, A.mult, -4096.0 if t == 1 else 0.0, A.add)
        between[0]()
        if t == 1:
            ts(["wa"], "wb", T.wb[:], T.wa[:], 8191, A.bitwise_and)
            between[1]()
            ts(["wb"], "XP", T.XP[:, 0:256], T.wb[:], 0.5, A.mult, 2048.0, A.add)
            between[2]()
            tt(["wb", "XP"], "wa", T.wa[:], T.wb[:], T.XP[:, 0:256], A.min)
            ts(["wb"], "f41", T.f41[:], T.wb[:], -4096.0, A.add, 4096.0, A.mult)
            cp(["wa", "perm"], "xo1", T.xo1[:], T.wa[:, 0:256].indirect(perm))
        else:
            ts(["wa"], "wb", T.wb[:], T.wa[:], 1, A.arith_shift_right, 4095, A.bitwise_and)
            between[1]()
            cp(["wb", "perm"], "xo2", T.xo2[:], T.wb[:, 0:256].indirect(perm))

    def pack(e, R, lo, hi):
        w = CW[e]
        ts(R, "FCP", T.FCP[:, 256:256 + w], hi, 4096.0, A.mult)
        tt(R + ["FCP"], "c%d" % e, cs(e, rank), T.FCP[:, 256:256 + w], lo, A.add)

    mine = [T.XT[:, rank * 512:rank * 512 + 512:2], T.XT[:, rank * 512 + 1:rank * 512 + 512:2], xs(1, rank)]
    minen = ["x0", "x0", "x1"]

    def own(t):
        act([minen[t]], "xn%d" % t, T["xn%d" % t][:], mine[t], F.Identity, -C1)

    def frames(t, q, r0, r1):
        o = T["yk%d" % t][:, r0 * 256:r1 * 256]; i = T.frs[:, 0:4096].indirect(T["fo%d" % t][:, r0 * 16:r1 * 16])
        W = ["yk%d_%d" % (t, r) for r in range(r0, r1)]
        op(q, ["frm", "fo%d" % t], W, (lambda: V.tensor_copy(o, i)) if q == "v" else (lambda: g.scalar.activation(o, i, F.Copy)))

    for t in (0, 1):
        cp(["sc"], "er%d" % t, tu(t, 0), T.scs[:, t::2])
    own(0); own(1)
    turns = [turn_steps(["sc"], "ew%d" % t, t, T.scs[:, t::2], ti(t, 0)) for t in (0, 1)]
    for f0, f1 in zip(*turns):
        f0(); f1()
    for f0, f1 in zip(scene_next(0), scene_next(1)):
        f0(); f1()
    cp(["cas", "perm20"], "xo0", T.xo0[:], cas.indirect(perm2[0]))
    pack(0, ["cas"], ck[0], ck[1])
    send_c(0)
    ts(["th"], "nb0", nb[0], T.ths[:, 0:1], 256.0, A.mult, 255.0, A.add)
    ts(["KL", "tgt"], "Bo", T.Bo[:], T.sn0[:, 0:128], cf(3), A.is_equal)
    ts(["K16", "rf", "nb0"], "K16", T.E[:], T.E[:], cf(0), A.is_equal, nb[0], A.mult)
    mms(["K16", "Bo"], ["KEY"], [(T.KEY[:, 0:256], T.Bo[:], T.E[:], True, True)])
    act(["KEY"], "TH", T.TH[:], T.KEY[:, 0:256], F.Copy)
    ts(["K2", "m1"], "K2", T.tin[:, 96:112], T.tin[:, 96:112], cf(5), A.not_equal, 272.0, A.mult)
    ts(["K4", "rh"], "mk", T.kf[:, 64:128], T.tout[:, 64:128], cf(11), A.is_equal)
    tt(["K2", "jc"], "roff", roff, T.tin[:, 96:112], jc, A.add)
    frame_list = lambda t: cp(["rol", "er%d" % t], "fo%d" % t, T["fo%d" % t][:], rol.indirect(tu(t, 0)))

    def pair(t):
        if t < 2:
            tt(["rol", "eu%d" % t, "f4%d" % t], "fc%d" % t, T["fc%d" % t][:], rol.indirect(tu(t, 1)), T["f4%d" % t][:], A.add)
        else:
            tt(["f42", "wb"], "fc2", T.fc2[:], T.f42[:], T.wb[:], A.add)
    x_offsets(1, [lambda: (ts(["cas"], "f40", T.f40[:], ck[0], 4096.0, A.mult), frame_list(0)), lambda: frame_list(1), lambda: pair(0)])
    frames(0, "s", 0, 4); frames(0, "v", 8, 16); frames(0, "s", 4, 8)

    for t in range(3):
        B = lambda n: T["%s%d" % (n, t)]
        n_ = lambda n: "%s%d" % (n, t)
        KEY = T.KEY; key = "KEY"
        win = T.XT[:, XWIN[t][0]:XWIN[t][1]]
        XR = [["X0"], ["X0", "X1"], ["X1", "X2"]][t]; CR = [["C0"], ["C0", "C1"], ["C1", "C2"]][t]
        yk = ["yk%d_%d" % (t, r) for r in range(16)]
        mms(["oneb", "Mb"], [key], [(KEY[:, 0:256], T.oneb[0:1, 0:128], T.Mb[0:1, :], True, False)])
        if t > 0:
            mms(["oneb", n_("ar")], [n_("ka")], [(KEY[:, 0:256], T.ar[0:1, :], T.oneb[0:1, :], False, False)])
        blk = lambda n, r0, r1: B(n)[:, r0 * 256:r1 * 256]
        yp = lambda r0, r1: T["YP%d" % (r0 // 2)][:, 256 * (r0 % 2):256 * (r0 % 2 + r1 - r0)]
        for r0, r1, w in PIECES:
            if w in "CD":
                mms(["Idn"] + yk[r0:r1], ["YP%d" % (r0 // 2)], [(yp(r0, r1), T.Idn[:], blk("yk", r0, r1), True, False)])
            elif w == "B":
                mms(["Id", "Bn"] + yk[r0:r1], ["YP%d" % (r0 // 2)], [(yp(r0, r1), T.Id[:], blk("yk", r0, r1), True, True)] +
                    [(KEY[:, 0:256], seln(r), blk("yk", r, r + 1), False, False) for r in range(r0, r1)])
        calls = distance_order()
        for step, i, r in calls:
            r0, r1, w = PIECES[i]
            dd, ab, y = "dd%d_%d" % (t, r0), "ab%d_%d" % (t, r0), "YP%d" % (r0 // 2)
            xk = win.indirect(B("xo")[:, r0 * 16:r1 * 16])
            if step == "diff":
                tt(XR + [n_("xo")] + yk[r0:r1], dd, blk("dd", r0, r1), xk, blk("yk", r0, r1), A.subtract)
            elif step == "take":
                cp(XR + [n_("xo")], dd, blk("dd", r0, r1), xk)
            elif step == "pick":
                act(XR + [n_("xo")], dd, blk("dd", r0, r1), xk, F.Copy)
            elif step == "max":
                tt([dd, y], ab, blk("ab", r0, r1), blk("dd", r0, r1), yp(r0, r1), A.max)
            elif step == "add":
                mms(["Id", dd], [y], [(yp(r0, r1), T.Id[:], blk("dd", r0, r1), False, True)])
            elif step == "abs":
                act([dd if w == "A" else y], ab, blk("ab", r0, r1), blk("dd", r0, r1) if w == "A" else yp(r0, r1), F.Abs)
            else:
                sel, wt, n, src = {"less": (seln, "Bn", "dd", dd), "twice": (sel2, "B2", "ab", ab), "sum": (selb, "Bb", "ab", ab)}[step]
                last = (step, i, r) == calls[-1]
                mms([wt, src], [key] if last else [], [(KEY[:, 0:256], sel(r), blk(n, r, r + 1), False, last)])
        if t == 0:
            pair(1)
        elif t == 1:
            ts(["f42", "perm"], "fo2", T.fo2[:], T.f42[:, 0:256].indirect(perm), 1.0 / 4096, A.mult)
        else:
            pair(2)
        if t < 2:
            frames(t + 1, "s", 0, EARLY[t])
        else:
            mms(["Id", "Idn", "x1"], ["YP0", "YP1"], [(T.YP0[:, 0:256], T.Id[:], mine[2], True, False), (T.YP1[:, 0:256], T.Idn[:], mine[2], True, False)])
            act(["x2"], "yxo", T.yxs[:, 1::2], xs(2, rank), F.Copy)
        op("v", [key, "rst"], [n_("sn")], lambda: V.tensor_tensor_scan(B("sn")[:], T.rst[:], KEY[:, 0:256], 0.0, A.add, A.min))
        tt([key, "TH"], "rj", T.rj[:, 16:272], KEY[:, 0:256], T.TH[:], A.is_gt)
        cp([n_("sn")], n_("ki"), ti(t, 3), B("sn")[:, 15::16])
        count = lambda: op("v", ["rj", "keep"], [n_("nr")], lambda: V.tensor_tensor_scan(B("nr")[:], T.keep[:], T.rj[:, 16:272], 0.0, A.mult, A.add))

        def turn_rejected():
            op("v", ["rj"], ["r1"], lambda: V.transpose(T.r1[:, 0:256], T.rj[:, 16:272]))
            op("v", ["rj"], ["r2"], lambda: V.transpose(T.r1[:, 256:544], T.rj[:, 0:288]))

        def best_pair():
            tt([n_("ub"), "eye", n_("fc")], n_("oh"), B("oh")[:], eye.indirect(tu(t, 3)), B("fc")[:], A.mult)
            mms([n_("oh"), "Bf"], ["FCP"], [(T.FCP[:, 0:64], self_(x), B("oh")[:, x::4], x == 0, x == 3) for x in range(4)])

        kb = lambda: ts([n_("ki")], n_("kb"), ti(t, 5), ti(t, 3), 15, A.bitwise_and)
        ub = lambda: cp([n_("kb")], n_("ub"), tu(t, 3), ti(t, 5))
        nrej = B("nr")[:, 15::16]
        count()
        if t == 2:
            kb()
        ts([n_("ki")], n_("kk"), ti(t, 4), ti(t, 3), 255, A.bitwise_and)
        if t == 2:
            ub()
        ts([n_("nr")], n_("J"), tf(t, 0), nrej, 9.0, A.is_ge, 256.0, A.mult)
        if t == 2:
            best_pair()
        ts([n_("kk"), "r256"], n_("uo"), tu(t, 2), ti(t, 4), cf(2), A.add)
        tt([n_("J"), "jc"], n_("sf"), tf(t, 1), tf(t, 0), jc, A.add)
        yb = B("yk")[:, 0:4096].indirect(tu(t, 2))
        xout = T.yxs[:, 0::2] if t == 2 else xs(t + 1, rank)
        choose = lambda: act([n_("Wd"), n_("Wa"), n_("us")], "x%d" % (t + 1), xout, B("W")[:, 0:512].indirect(tu(t, 4)), F.Abs, -C1)
        if t == 2:
            act(yk + ["uo2"], "yb", T.rr[:], yb, F.Copy)
            mms(["Id", "yb"], ["YP0", "YP1"], [(T.YP0[:, 0:256], T.Id[:], T.rr[:], False, True), (T.YP1[:, 0:256], T.Id[:], T.rr[:], False, True)])
            cp([n_("sf")], n_("us"), tu(t, 4), tf(t, 1))
        else:
            tt(yk + [n_("uo"), minen[t]], n_("sm"), B("sm")[:], yb, mine[t], A.add)
            cp([n_("sf")], n_("us"), tu(t, 4), tf(t, 1))
            tt(yk + [n_("uo"), n_("xn")], n_("Wd"), B("W")[:, 0:256], yb, B("xn")[:], A.subtract)
            act([n_("sm")], n_("Wa"), B("W")[:, 256:512], B("sm")[:], F.Identity, C1, 0.4995)
            choose()
            send_x(t + 1)
            kb()
            op("v", [n_("J")], [n_("jr")], lambda: V.tensor_reduce(cf(9 + t), tf(t, 0), AxisListType.X, A.add))
            ub()
            mms([n_("jr"), "onef"], ["FCP"], [(T.FCP[:, 64:65], T.onef[:], cf(9 + t), True, True)])
        ts([n_("nr")], n_("J2"), tf(t, 8), nrej, 9.0, A.is_ge, 544.0, A.mult)
        if t < 2:
            best_pair()
            for r0, r1 in ((EARLY[t], 6), (6, 10), (10, 16)):
                frames(t + 1, "s", r0, r1)
        turn_rejected()
        small = [lambda: tt([n_("J2"), "roff"], n_("jb"), tf(t, 3), tf(t, 8), roff, A.max),
                 lambda: ts([n_("J")], n_("J1"), tf(t, 2), tf(t, 0), 1.0 / 256, A.mult)]
        small[0](); small[1]()
        if t < 2:
            cp(["cas"], "XP", T.XP[:, 256:512], ck[t])
        fm = B("tf")[:, 160:224]; fh = B("tf")[:, 224:256]
        tt(["FCP", "mk"], n_("fm"), fm, T.FCP[:, 0:64], T.kf[:, 64:128], A.mult)
        if t < 2:
            cp(["FCP"], n_("a1"), ci(4 + t), T.FCP[:, 64:65])
        cp([n_("jb")], n_("up"), tu(t, 7), tf(t, 3))
        if t == 2:
            act(["r1", "r2", "rz", "up2"], "pen", T.dm2[:], T.r1[:, 0:560].indirect(tu(t, 7)), F.Identity, -BIG, BIG)
            act(["YP0"], "Wa2", T.W2[:, 256:512], T.YP0[:, 0:256], F.Identity, C1, 0.4995)
            act(["YP1"], "Wd2", T.W2[:, 0:256], T.YP1[:, 0:256], F.Identity, C1)
            choose()
            dma("y", "ox", ["x3", "yxo"], [], T.yx[:], T.yxs[:])
        tt([n_("fm")], n_("fh"), fh, B("tf")[:, 160:224:2], B("tf")[:, 161:224:2], A.add)
        if t < 2:
            ts([n_("a1")], n_("a2"), ci(6 + t), ci(4 + t), 65535, A.bitwise_and)
        tt([n_("fh")], n_("fi"), ti(t, 6), B("tf")[:, 224:256:2], B("tf")[:, 225:256:2], A.add)
        if t < 2:
            ts([n_("a2")], n_("a3"), nb[t + 1], ci(6 + t), -1.0, A.mult)
        fi = ti(t, 6); FI = [n_("fi")]
        at = 12 if t < 2 else 0

        eo, en = (ti(2, 0), "ew2") if t == 0 else (tf(t, 9), n_("en"))
        fill = [lambda: ts(FI, n_("fb"), ti(t, 7), fi, 12 - at, A.arith_shift_right, 2047, A.bitwise_and),
                lambda: tt([n_("fb"), n_("eb")], n_("e1"), tf(t, 4), ti(t, 7), ti(t, 2), A.subtract),
                lambda: tt([n_("e1"), n_("J1")], n_("e2"), tf(t, 5), tf(t, 4), tf(t, 2), A.mult),
                lambda: tt([n_("e2"), n_("eb")], en, eo, tf(t, 5), ti(t, 2), A.add)]
        if t == 0:
            fill += [lambda: cp(["ew2"], "eu2", tu(2, 1), ti(2, 0)),
                     lambda: ts(["ew2"], "ea2", ti(2, 1), ti(2, 0), 1.0, A.add),
                     lambda: ts(["ea2"], "eb2", ti(2, 2), ti(2, 1), 2047, A.bitwise_and)]
        if t == 2:
            fill += [lambda: act([en, "m0"], "ta3", T.tin[:, 96:112], tf(t, 9), F.Copy, 0.0, cf(4)),
                     lambda: act([en, "m1"], "tb3", T.tin[:, 112:128], tf(t, 9), F.Copy, 0.0, cf(5))]
            fill += turn_steps([en], "ye2", 3, tf(t, 9), T.yes[:, 0::2])[2:]
            fill.append(lambda: dma("s", "oe", ["ye1", "ye2"], [], T.ye[:], T.yes[:]))

        def more(n=1):
            for _ in range(min(n, len(fill))):
                fill.pop(0)()
        if t < 2:
            ts(FI, n_("h"), ti(t, 8), fi, 13, A.arith_shift_right)
        else:
            ts(FI, n_("h"), ti(t, 8), fi, 4095, A.bitwise_and)
        if t < 2:
            ts(FI, n_("s"), ti(t, 9), fi, at, A.arith_shift_right, 1, A.bitwise_and)
            ts([n_("a3"), "oneb", "ka%d" % t if t else "oneb"], "ar%d" % (t + 1), T.ar[0:1, :], T.oneb[0:1, 0:128], T.cf[0:1, 7 + t:8 + t], A.mult)
        more()
        ts([n_("h")], n_("uc"), tu(t, 5), ti(t, 8), 2048.0 if t == 1 else 0.0, A.add)
        cwin = T.CT[:, CWIN[t][0]:CWIN[t][1]]
        if t < 2:
            ts([n_("s")], n_("q1"), tf(t, 6), ti(t, 9), 256.0, A.mult)
            more()
            ts(CR + [n_("uc")], "lo", T.LHa[:, 0:256], cwin.indirect(tu(t, 5)), 4095, A.bitwise_and)
            tt([n_("q1"), "jc"], n_("q2"), tf(t, 7), tf(t, 6), jc, A.add)
            more()
            ts(CR + [n_("uc")], "hi", T.LHa[:, 256:512], cwin.indirect(tu(t, 5)), 12, A.arith_shift_right)
            cp([n_("q2")], n_("uq"), tu(t, 6), tf(t, 7))
            more()
            tt(["lo", "hi", ckn[t], n_("uq")], n_("df"), B("df")[:], T.LHa[:, 0:512].indirect(tu(t, 6)), ck[t], A.subtract)
            more()
            tt(["r1", "r2", "rz", n_("up"), n_("df")], n_("dm"), B("dm")[:], T.r1[:, 0:560].indirect(tu(t, 7)), B("df")[:], A.mult)
            more()
            tt([n_("dm"), "XP"], "c%d" % (t + 1), cs(t + 1, rank), B("dm")[:], T.XP[:, 256:512], A.add)
            send_c(t + 1)
            more()
        else:
            more()
            tt(["XP", "pen"], "XP", T.XP[:, 256:512], T.XP[:, 0:256], T.dm2[:], A.subtract)
            more()
            for h in range(2):
                tt(CR + ["pen", "uc2"], "df2_%d" % h, T.df2[:, 128 * h:128 * h + 128], cwin.indirect(T.tu2[:, 80 + 8 * h:88 + 8 * h]),
                   T.dm2[:, 128 * h:128 * h + 128], A.add)
                if h == 0:
                    more(3)
            for h in range(2):
                tt(["df2_%d" % h, "XP"], "cn2_%d" % h, T.ycs[:, 256 * h:256 * h + 256:2], T.df2[:, 128 * h:128 * h + 128], T.XP[:, 256 + 128 * h:384 + 128 * h], A.max)
                dma("y", "oc%d" % h, ["cn1", "cn2_%d" % h], [], T.yc[:, 256 * h:256 * h + 256], T.ycs[:, 256 * h:256 * h + 256])
        if t == 0:
            ts(["rol", "eu2"], "f42", T.f42[:], rol.indirect(tu(2, 1)), 4096.0, A.mult)
            ts(["c1"], "XP", T.XP[:, 0:256], ck[2], -BIG, A.add)
        elif t == 1:
            ye1 = turn_steps(["en1"], "ye1", 2, tf(1, 9), T.yes[:, 1::2])
            ye1[0](); ye1[1]()
            x_offsets(2, ye1[2:])
            cp(["c2"], "cn1", T.ycs[:, 1::2], cs(2, rank))
        more(9)

    wait("g", [("loc", loc[0])])
    wait("y", [("ox", 16), ("oc0", 16), ("oc1", 16), ("oe", 16)] + list(cnt.items()))
